import numpy as np, ml_dtypes
CORES = [48,51,52,55]
N = 4
import mx_ref
BF = ml_dtypes.bfloat16
def gcols(t, e):
    v = np.concatenate([t.reshape(8, 16, -1, 4), np.zeros((8, 16, 1, 4), BF)], axis=2)
    return np.ascontiguousarray(np.stack([v[g][:, e[g]] for g in range(8)])).reshape(128, -1)
def tile(rs):
    return np.stack(rs, axis=2).reshape(128, -1).astype(BF)
def cut(t, i, w=512):
    return t[:, w * i:w * i + w]
def pick(q, e):
    c = np.concatenate([q[0].reshape(128, -1, 4), np.zeros((128, 1, 4), np.uint8)], axis=1); s = np.concatenate([q[1], np.ones((16, 1), np.uint8)], axis=1)
    return (np.ascontiguousarray(c[:, e].reshape(128, -1)), np.ascontiguousarray(s[:, e]))
def join(*qs):
    return (np.concatenate([q[0] for q in qs], axis=1), np.concatenate([q[1] for q in qs], axis=1))
def put(q, e, v):
    c, s = q[0].reshape(128, -1, 4).copy(), q[1].copy(); c[:, e] = v[0].reshape(128, -1, 4); s[:, e] = v[1]
    return (c.reshape(128, -1), s)
def pk(c, s):
    return (np.ascontiguousarray(c), mx_ref.live(s))
def emit(q):
    return q[0], q[1]
def packed(v, rng):
    q = [mx_ref.quantize(np.ascontiguousarray(v[r])) for r in range(N)]
    return np.stack([a for a, b in q]), np.stack([mx_ref.plane(b, rng) for a, b in q])
def values_of_codes():
    e, c = np.zeros((128, 128, 4), np.float32), np.zeros((128, 2, 4), np.uint8)
    e[np.arange(128), np.arange(128), 0] = 1
    c[:127, :, 0] = np.arange(256).reshape(2, 128).T[:127]
    return mx_ref.matmul(mx_ref.quantize(e.reshape(128, 512).astype(BF)), (c.reshape(128, 8), np.full((16, 2), 127, np.uint8))).T.reshape(-1).astype(np.float64)
CODE_VALUE, SCALE_VALUE = values_of_codes(), 2.0 ** (np.arange(256) - 127.0)
def decode(q):
    return (CODE_VALUE[q[0]].reshape(16, 8, -1, 4) * SCALE_VALUE[q[1]][:, None, :, None] + 0.0).reshape(128, -1).astype(np.float32)
def f(rng, *shape):
    return mx_ref.flush((rng.standard_normal(shape, dtype=np.float32) * np.exp2(rng.integers(-2, 3, shape[:-1] + (1,)))).astype(BF))
def wide(rng, *shape, cols=0):
    v = rng.standard_normal(shape, dtype=np.float32) * np.exp2(rng.integers(-12, 13, shape)).astype(np.float32)
    if cols: v *= np.repeat(np.exp2(rng.integers(-cols, cols + 1, shape[:-2] + (1, shape[-1] // 4))) * (rng.random(shape[:-2] + (1, shape[-1] // 4)) > 0.0625), 4, axis=-1).astype(np.float32)
    return mx_ref.flush(v.astype(BF))
C, K, R = 384, 96, 3
def turned(s, t):
    s = s + np.float32(0.0)
    k, g = np.arange(C), np.arange(8)
    above = (s[:, None, :] > s[:, :, None]) | (s[:, None, :] == s[:, :, None]) & (k[None, :] < k[:, None])
    low = np.max(np.where(above & (k[None, :] < k[:, None]), k, -1), axis=2) + 1
    high = np.min(np.where(above & (k[None, :] > k[:, None]), k, C), axis=2) - 1
    at = np.tile(k, (8, 1))
    for c in np.argsort(high - low, axis=1, kind="stable").T:
        a, b = low[g, c][:, None], high[g, c][:, None]
        at = np.where((t[g, c][:, None] > 0) & (at >= a) & (at <= b), a + b - at, at)
    return np.argsort(at, axis=1)
def numbers_of(rng):
    return {"x": np.array(f(rng, N, 128, 4 * C)), "u": np.array(f(rng, N, 128, 512)), "v": np.array(f(rng, N, 128, 512))}
def weights(rng, w):
    c, p = packed(w, rng)
    return {"wc": c, "ws": p}
def still(rng):
    return weights(rng, np.zeros((N, 128, 2048), np.float32).astype(BF))
def apart(rng):
    w = np.array(f(rng, N, 128, 2048)).reshape(N, 8, 16, 4, 8, 16, 4)
    w[:, :, :8] = 0
    w[:, :, :, :, :, :8] = 0
    return weights(rng, w.reshape(N, 128, 2048))
def signs(rng):
    return np.stack([rng.permutation(8) % 2 * 2.0 - 1.0 for r in range(N)])
def small(rng):
    return np.where(rng.permutation(N) < N // 2, 2.0 ** -30, 1.0).astype(np.float32)
def planted(rng, s, t):
    d, k = numbers_of(rng), small(rng)
    neg = rng.permutation(N) % 2
    b = ((np.where(neg[:, None, None] == 1, 511 - s, s)[..., None] >> np.arange(9)) & 1) * k[:, None, None, None]
    x = d["x"].astype(np.float32).reshape(N, 8, 16, C, 4)
    x[:, :, :8] = 0
    x[:, :, 0] = b[..., :4]
    x[:, :, 1] = 16 * b[..., 4:8]
    x[:, :, 2, :, 0] = 16 * b[..., 8]
    x[:, :, 4, :, 0] = t * k[:, None, None]
    u = d["u"].astype(np.float32).reshape(N, 128, 128, 4)
    u[:, :, ::16] = 0
    u[:, :, 1::16] = 0
    m = (1 - 2 * neg) * k
    for h in range(0, 128, 16):
        u[:, h:h + 2, h] = m[:, None, None] * np.array([1.0, 2.0, 4.0, 8.0])
        u[:, h + 2, h, 0] = 16 * m
        u[:, h + 4, h + 1, 0] = k
    return {"x": x.reshape(N, 128, 4 * C).astype(BF), "u": u.reshape(N, 128, 512).astype(BF), "v": d["v"], **apart(rng)}
def setup_inputs(rng):
    return {**numbers_of(rng), **weights(rng, f(rng, N, 128, 2048))}
def setup_inputs_ties(rng):
    s, t = rng.integers(0, 3, (N, 8, C)), rng.integers(-1, 2, (N, 8, C))
    e = rng.permutation(N)
    s[e[0]] = 1
    t[e[1]] = 0
    return planted(rng, s, t)
def setup_inputs_chains(rng):
    c = np.arange(C)
    one = np.ones(C, np.int64)
    zig = np.where(c < C // 2, C - 1 - 2 * c, 2 * c - C)
    halves = np.sum((c[:, None] + 1) % 2 ** np.arange(1, 9) == 0, axis=1)
    s, t = np.zeros((N, 8, C), np.int64), np.zeros((N, 8, C), np.int64)
    for r in range(N):
        g, m, n = rng.permutation(8), rng.permutation(C), rng.permutation(C)
        s[r, g] = np.stack([c, C - 1 - c, zig, c, 7 * one, halves, m, n])
        t[r, g] = np.stack([one, one, one, rng.integers(-1, 2, C), one, one, (m == C - 1) * 2 - 1, -(n % 2)])
    return planted(rng, s, t)
def setup_inputs_near(rng):
    d = numbers_of(rng)
    x = d["x"].astype(np.float32).reshape(N, 8, 16, C, 4)
    i = np.array([[np.arange(C) // 2 if a > 0 else rng.permutation(C) // 2 for a in e] for e in signs(rng)])
    b = ((i[..., None] >> np.arange(8)) & 1) * np.exp2(np.arange(8) - 23.0)
    x[:, :, 0] = 0
    x[:, :, 0, :, 0] = signs(rng)[:, :, None]
    x[:, :, 8] = b[..., :4]
    x[:, :, 9] = b[..., 4:]
    x[:, :, 10] = 0
    x[:, :, 10, :, 0] = rng.integers(-1, 2, (N, 8, C)) * 2.0 ** -20
    x[:, :, 11:] = rng.integers(4, 8, (N, 8, 5, C, 4)) * rng.choice([-1.0, 1.0], (N, 8, 5, C, 4)) * 2.0 ** -20
    u = d["u"].astype(np.float32).reshape(N, 128, 128, 4)
    k = small(rng)
    u[:, :, ::16] = 0
    u[:, :, 1::16] = 0
    for h in range(0, 128, 16):
        u[:, h, h, 0] = k
        u[:, h + 8:h + 10, h] = k[:, None, None]
        u[:, h + 10, h + 1, 0] = k
    return {"x": x.reshape(N, 128, 4 * C).astype(BF), "u": u.reshape(N, 128, 512).astype(BF), "v": d["v"], **still(rng)}
def setup_inputs_huge(rng):
    d = numbers_of(rng)
    x = 2.0 ** 30 * (0.6 + 0.4 * rng.random((N, 8, 16, C, 4)))
    c = np.stack([rng.permutation(C) % 2 * 2.0 - 1.0 for r in range(N)])
    e = rng.permutation(N)
    c[e < N // 2] = 1
    x[..., :2] *= c[:, None, None, :, None]
    x[..., 2:] *= rng.choice([-1.0, 1.0], (N, 8, 1, C, 1))
    g = signs(rng)
    u = d["u"].astype(np.float32).reshape(N, 128, 128, 4)
    u[:, :, ::16] = 0
    u[:, :, 1::16] = 0
    u[:, :, ::16, :2] = 2.0 ** 30 * (1 - 0.25 * rng.random((N, 128, 8, 2))) * g[:, None, :, None]
    for h in range(0, 128, 16):
        u[:, h:h + 16, h + 1, 2:] = 2.0 ** 30
    r = int(np.argmin(e))
    x[r] = np.abs(x[r])
    x[r, :, :, C // 2:] = 2.0 ** 30
    u[r, :, ::16] = 2.0 ** 30 * g[r][None, :, None]
    return {"x": x.astype(np.float32).reshape(N, 128, 4 * C).astype(BF), "u": u.reshape(N, 128, 512).astype(BF), "v": d["v"], **still(rng)}
def setup_inputs_spread(rng):
    d = setup_inputs(rng)
    d["x"] = wide(rng, N, 128, 4 * C, cols=6)
    return d
def check_inputs(d):
    b = []
    for k in ("x", "u", "v"):
        a = np.abs(d[k].astype(np.float32))
        if not (np.isfinite(a).all() and ((a == 0) | (a >= 2.0 ** -30) & (a <= 2.0 ** 30)).all()): b.append("a value of " + k)
    return b
def reference(x, u, v, wc, ws):
    qu = [mx_ref.quantize(u[r]) for r in range(N)]
    lay = [pk(wc[r], ws[r]) for r in range(N)]
    now = [x[r] for r in range(N)]
    for t in range(R):
        o, border = [], []
        for r in range(N):
            p = mx_ref.matmul(qu[r], mx_ref.quantize(now[r]))
            o.append(turned(p[::16], p[1::16]))
            border.append(mx_ref.quantize(gcols(now[r], o[r][:, C - K:])))
        came = decode(join(*border)).astype(BF)
        for r in range(N):
            z = np.ascontiguousarray(np.concatenate([cut(came, (r - 1) % N, 4 * K), gcols(now[r], o[r][:, :C - K])], axis=1))
            q = mx_ref.quantize(z)
            now[r] = tile([z[:, b::4].astype(np.float32) + mx_ref.matmul(pick(lay[r], np.arange(128 * b, 128 * b + 128)), q) * np.float32(0.015625) for b in range(4)])
    y, ol = np.zeros((N, 128, C), np.float32), np.zeros((N, 8, C), np.float32)
    oc, osc = np.zeros((N, 128, 4 * C), np.uint8), np.zeros((N, 16, C), np.uint8)
    for r in range(N):
        q = mx_ref.quantize(now[r])
        y[r] = mx_ref.matmul(mx_ref.quantize(v[r]), q)
        ol[r] = o[r]
        oc[r], osc[r] = emit(q)
    return {"y": y, "ol": ol, "oc": oc, "osc": osc}

@@ -1,0 +1,397 @@
+from concourse.mybir import dt, AluOpType as OP, ActivationFunctionType as AF
+
+C, K, R, N = 384, 96, 3, 4
+NB, H = C // 16, C - K
+F32, BF, I32, U16, Q4, U8 = "float32", "bfloat16", "int32", "uint16", "float8_e4m3fn_x4", "uint8"
+BIG = 1e28
+
+SCRATCH = {"ps": ("psum", [128, 4096], F32)}
+for _d, _l in (
+        (BF, "X:1536 X64:1536 Z:1536 Z64:1536 Dd:1536 ut:512 vt:512 tA:2048 tB:2048 tE:2048 A:1536 B:1536 one:608 BD:128 ID:128 "
+             "seg:384 CNT:1024 cov:608 run:608 junk:768"),
+        (Q4, "qu:128 qv:128 qp:256 wq:512 qz:384 qzb:128 kqA:512 kqB:512 kqE:512 qa:384 qb:384 qx0:384 qx1:384 qx2:384 qx3:384 lq0:384 lq1:384 lq2:384"),
+        (U8, "su:128 sv:128 sp:256 wsp:512 sz:384 szb:128 ksA:512 ksB:512 ksE:512 sa:384 sb:384 sx0:384 sx1:384 sx2:384 sx3:384 ls0:384 ls1:384 ls2:384"),
+        (I32, "cI:64 WI:16"),
+        (U16, "rep:24 upk:24 lBM:38 lTH:20 lE:8 tt:66 lD:24 lp:66 oc16:48 at:24 oo:72 ob:72 ll:72"),
+        (F32, "cF:16 dm:32 tm:32 PP:96 c1:384 c2:384 c3:384 c4:384 c5:384 c5y:384 c6:384 arow:384 a2row:384 aW:48 aX:128 J:160 ER:128 ERd:128 "
+              "DT:96 OH:32 base:64 cc:64 S:384 V:384 U:384 TB:96 BMx:608 m:64 E:128 TD:192 acc:2 rp:128 rt:128 dL:512 dR:512 GL:400 GR:400 "
+              "GgL:384 GgR:384 mL:384 mR:384 xx:1024 uu:128 sm:256 zt:384 z:384 EW:768 PH:768 Y:768 Yg:384 dg:384 O:384 o4:384 ys:384")):
+    for _e in _l.split():
+        _n, _w = _e.split(":")
+        SCRATCH[_n] = ("sbuf", [128, int(_w)], _d)
+
+SEMAPHORES = ["v", "s", "t", "g", "dx", "du", "dv", "dwc", "dws", "dkA", "dkB", "dkE", "dy", "dol", "doc", "dos", "loc"] + \
+             ["aq%d" % t for t in range(R)] + ["al%d" % t for t in range(R)]
+
+GA, SC, LAG = 1.56, 3.8, 120.0
+
+
+def rank_program(g, core, T, topo):
+    rank = T.rank_of(core)
+    if rank is None:
+        return
+    nxt, prv = T.cores[(rank + 1) % N], T.cores[(rank - 1) % N]
+    rid, pid = topo.addr(nxt)[0:2]
+    mask = topo.mask(core, nxt)
+    n_out, n_in = len(topo.engines(core, nxt)), len(topo.engines(prv, core))
+    QS = {"v": g.vector, "s": g.scalar, "t": g.tensor, "g": g, "y": g.sync}
+    ops, wrote, read = [], {}, {}
+
+    def add(q, emit, r, w, busy, lag, sem, inc, acc=False):
+        r, w = r.split(), w.split()
+        deps = {}
+        for k in r + w:
+            if k in wrote:
+                deps[wrote[k]] = deps.get(wrote[k], False) or not (acc and k in w)
+        for k in w + [k for k in r if k[0] == "#"]:
+            for i in read.get(k, []):
+                if k in w or ops[i]["q"] != q:
+                    deps[i] = True
+        ops.append({"q": q, "emit": emit, "deps": deps, "busy": busy, "lag": lag, "sem": sem, "inc": inc})
+        for k in r:
+            read.setdefault(k, []).append(len(ops) - 1)
+        for k in w:
+            wrote[k] = len(ops) - 1
+            read[k] = []
+
+    def op(q, name, args, r, w, c, acc=False, **kw):
+        e = QS[q]
+        call = {"copy": lambda: e.tensor_copy(*args), "tt": lambda: e.tensor_tensor(*args), "ts": lambda: e.tensor_scalar(*args),
+                "scan": lambda: e.tensor_tensor_scan(*args), "set": lambda: e.memset(*args), "q": lambda: e.quantize_mx(*args),
+                "tr": lambda: e.transpose(*args), "act": lambda: e.activation(*args, **kw), "mm": lambda: e.matmul_mx(*args),
+                "iota": lambda: e.iota(*args, **kw), "sel": lambda: e.affine_select(*args)}[name]
+        add(q, lambda: call().then_inc(T.sem[q], 1), r, w, max(c, 64) * 1.04, LAG, q, 1, acc)
+
+    def dma(q, sem, out, in_, r, w):
+        add(q, lambda: QS[q].dma_start(out, in_).then_inc(T.sem[sem], 16), r, w, 100.0, 2200.0, sem, 16)
+
+    def send(out, in_, sem, r, w):
+        add("g", lambda: g.remote_dma(out, in_, T.sem[sem], T.sem.loc, pid, rid, mask), r, w, 300.0, 0.0, "loc", n_out)
+
+    def landed(sem, n, r, w, lag):
+        add("x", None, r, w, 0.0, lag, sem, n)
+
+    def v(name, args, r, w, c=64):
+        op("v", name, args, r, w, c)
+
+    def act(out, in_, r, w, c, f=AF.Copy, **kw):
+        op("s", "act", (out, in_, f), r, w, c, **kw)
+
+    def iota(out, pat, base, w, c=32, whole=False):
+        if whole:
+            op("g", "iota", (out, pat, base, 0), "", w, 130 + 2 * c)
+        else:
+            op("g", "iota", (out, pat, base, 0), "", w, 130 + 2 * c, allow_small_or_imprecise_dtypes=True)
+
+    def bank(b, n=C, a=0):
+        return T.ps[:, 512 * b + a:512 * b + n]
+
+    def rbank(b, n=C):
+        return T.ps[:, 512 * b + n - 1:512 * b - 1:-1] if b else T.ps[:, n - 1::-1]
+
+    def rev(t, a=0, b=C):
+        return t[:, b - 1:a - 1:-1] if a else t[:, b - 1::-1]
+
+    def mm(b, n, lq, ls, rq, rs, start, stop, r):
+        op("t", "mm", (bank(b, n), lq, ls, rq, rs, start, stop), r, "#%d" % b, 0.7 * (n + 16), acc=not start)
+
+    def cm(b, i, rq, rs, key, start, stop):
+        n, a = "ABE"[i // 4], 128 * (i % 4)
+        mm(b, C, T["kq" + n][:, a:a + 128], T["ks" + n][:, a:a + 128], rq[:], rs[:], start, stop, "k%s %s" % (n, key))
+
+    lane, l4c, lq4, e16, l3 = [T.cF[:, i:i + 1] for i in range(5)]
+    l0, l15 = T.OH[:, 0:1], T.OH[:, 15:16]
+    sm = lambda i: T.sm[:, 24 * i:24 * i + 24]
+    keys = lambda s, n: " ".join(s + str(i) for i in range(n))
+    XA = keys("Xa", 4)
+    GC = 50 + GA * C
+
+    dma("y", "dx", T.X[:], T.x[:], "", XA + " Xb")
+    dma("s", "du", T.ut[:], T.u[:], "", "ut")
+    dma("y", "dwc", T.wq[:].bitcast(dt.uint8), T.wc[:], "", "wq")
+    dma("y", "dws", T.wsp[:], T.ws[:], "", "wsp")
+    dma("y", "dv", T.vt[:], T.v[:], "", "vt")
+
+    op("g", "iota", (T.cI[:, 0:1], [[0, 1]], 0, 1), "", "cI0", 130)
+    iota(T.cI[:, 16:32], [[1, 2], [16, 8]], 0, "cIu", whole=True)
+    iota(T.cI[:, 32:40], [[1, 4], [0, 2]], 0, "cIr", whole=True)
+    iota(T.tm[:, 0:16], [[1, 16]], 0, "tm0")
+    iota(T.tm[:, 16:32], [[0, 4], [1, 4]], 0, "tm1")
+    iota(T.aW[:, 0:24], [[16, NB]], 0, "aW0")
+    iota(T.J[:, 0:20], [[16, 20]], 0, "J0")
+    for name, w, parts in (("base", 64, ((1, 24, 1, 0), (33, 24, -1, 23))),
+                           ("ER", 128, ((1, 12, 25, 328), (13, 12, -24, 591), (33, 12, 24, 23), (45, 12, -25, 299),
+                                        (64, 9, -1, 40), (73, 15, -1, 15), (96, 15, 1, 65), (111, 9, 1, 96)))):
+        iota(T[name][:], [[0, w]], 0, keys(name, 8), w)
+        for i, (a, n, st, b0) in enumerate(parts):
+            iota(T[name][:, a:a + n], [[st, n]], b0, name + str(i))
+    iota(T.DT[:, 48:96], [[1, 48]], 0, "DT1", 48)
+    iota(T.a2row[:], [[2, C]], -1024 - 16 * (NB - 1), "a2row", C)
+    iota(T.arow[:], [[1, C]], 0, "arow", C)
+    iota(T.one[:, 0:C], [[0, C]], 1, "one", C)
+    iota(T.one[:, C:], [[0, 608 - C]], 1, "one1", 224)
+    op("g", "sel", (T.junk[:, 0:128], T.one[:, 0:128], [[-16, 8], [0, 16]], OP.is_ge, 0.0, 0, 1), "one", "junk0", 420)
+    op("g", "sel", (T.BD[:], T.junk[:, 0:128], [[16, 8], [0, 16]], OP.is_ge, 0.0, 15, -1), "junk0", "BD", 420)
+    op("g", "sel", (T.ID[:], T.one[:, 0:128], [[-1, 128]], OP.is_equal, 0.0, 0, 1), "one", "ID", 420)
+    op("g", "sel", (T.seg[:], T.one[:, 0:C], [[0, NB], [1, 16]], OP.not_equal, 0.0, 0, 0), "one", "seg", 170 + 2 * C)
+    op("g", "sel", (T.dR[:, 0:C], T.one[:, 0:C], [[0, NB], [1, 16]], OP.is_equal, 0.0, 0, 0), "one", "dR", 170 + 2 * C)
+    iota(T.dL[:, 0:C], [[0, C]], 0, "dL", C)
+    iota(T.cc[:], [[-1, 2], [0, 32]], 1, "cc", 64)
+    iota(T.aX[:, 0:64], [[0, 64]], 0, "aX0 aX1", 64)
+    for n in ("GL", "GR"):
+        iota(T[n][:, 0:1], [[0, 1]], 0, n + "0")
+        iota(T[n][:, C + 1:], [[0, 15]], 900, n + "1")
+    v("set", (T.tA[:, 0:512], 0.0), "", "tA0", 256)
+    for n, first in (("A", 1), ("B", 0), ("E", 0)):
+        for i in range(first, 4):
+            if n != "B" or i in (0, 3):
+                dma("y", "dk" + n, T["t" + n][:, 512 * i:512 * i + 512], T.tA[:, 0:512], "tA0", "z%s%d" % (n, i))
+    for col, key, n in ((lane, "lane", 15), (e16, "e16", 16)):
+        v("ts", (T.cI[:, n - 14:n - 13], T.cI[:, 0:1], n, None, OP.bitwise_and), "cI0", "i" + key)
+        v("copy", (col, T.cI[:, n - 14:n - 13]), "i" + key, key)
+    v("ts", (T.cI[:, 3:4], T.cI[:, 1:2], 2, None, OP.arith_shift_right), "ilane", "cI3")
+    v("ts", (T.cI[:, 4:5], T.cI[:, 1:2], 3, None, OP.bitwise_and), "ilane", "cI4")
+    v("copy", (lq4, T.cI[:, 3:4]), "cI3", "lq4")
+    v("ts", (l4c, T.cI[:, 4:5], 16000.0, None, OP.add), "cI4", "l4c")
+    v("copy", (T.upk[:], T.cI[:, 16:40]), "cIu cIr", "upk")
+    v("ts", (T.rep[:], T.aW[:, 0:24], 0.0, lane, OP.mult, OP.add), "aW0 lane", "rep")
+    v("ts", (T.dm[:, 0:16], T.tm[:, 0:16], lane, None, OP.subtract), "tm0 lane", "dm0")
+    v("ts", (T.dm[:, 16:32], T.tm[:, 16:32], lq4, None, OP.subtract), "tm1 lq4", "dm1")
+    for i, col, a, b in ((0, 15, -10 * BIG, BIG), (1, 0, -10 * BIG, BIG), (2, 0, -1000.0, 3000.0), (3, 15, -1000.0, 3000.0)):
+        v("ts", (T.PP[:, 16 * i:16 * i + 16], T.dm[:, 0:16], 0.0, a, OP.is_equal, OP.mult), "dm0", "PP%d" % i)
+        one = T.PP[:, 16 * i + col:16 * i + col + 1]
+        v("ts", (one, one, b, None, OP.add), "PP%d" % i, "PP%d" % i)
+    v("ts", (T.PP[:, 64:96], T.dm[:], 0.0, 2000.0, OP.is_equal, OP.mult), "dm0 dm1", "PP4 PP5")
+    v("ts", (T.tm[:], T.dm[:], -1.0, -4000.0, OP.is_equal, OP.mult), "dm0 dm1", "tm0 tm1")
+    v("tt", (T.PP[:, 64:96], T.PP[:, 64:96], T.tm[:], OP.add), "PP4 PP5 tm0 tm1", "PP4 PP5")
+    v("ts", (T.PP[:, 79:96:4], T.PP[:, 79:96:4], -6000.0, None, OP.add), "PP4 PP5", "PP4 PP5")
+    for name, i in (("c1", 0), ("c2", 1), ("c3", 2), ("c4", 3), ("c5", 4), ("c5y", 4), ("c6", 5)):
+        act(T[name][:], T.PP[:, 16 * i:16 * i + 16].indirect(T.rep[:, 0:24]), "PP%d rep" % i, name, GC)
+    v("ts", (T.aW[:, 24:48], T.aW[:, 0:24], lane, 0.5, OP.add, OP.add), "aW0 lane", "aW1")
+    v("tt", (T.c5y[:, 15::16], T.c5y[:, 15::16], T.aW[:, 24:48], OP.add), "c5y aW1", "c5y")
+    v("ts", (T.aX[:, 1:25], T.aW[:, 24:48], -4392.5, None, OP.add), "aW1", "aX0")
+    v("ts", (T.aX[:, 33:57], T.aW[:, 24:48], -1.0, C - 4391.5, OP.mult, OP.add), "aW1", "aX1")
+    v("scan", (T.ERd[:], T.ER[:], T.c5[:, 0:128], -5000.0, OP.max, OP.add), keys("ER", 8) + " c5", "ERd", 128)
+    v("ts", (T.lE[:, 0:4], T.ERd[:, 15:64:16], 4000.0, None, OP.add), "ERd", "lE")
+    v("ts", (T.lE[:, 4:8], T.ERd[:, 79::16], 4000.0, e16, OP.add, OP.add), "ERd e16", "lT")
+    v("ts", (T.OH[:, 0:16], T.dm[:, 0:16], 0.0, None, OP.is_equal), "dm0", "OH0")
+    v("ts", (T.OH[:, 16:32], T.dm[:, 0:16], 0.0, 512.0, OP.is_equal, OP.mult), "dm0", "OH1")
+    v("set", (T.TB[:], BIG), "", "TBs TBp TBm", 96)
+    v("set", (T.A[:, 3::4], 0.0), "", "A3", 192)
+    v("set", (T.B[:, 3::4], 0.0), "", "B3", 192)
+    v("set", (T.CNT[:, 15::16], 5.0), "", "CL CR")
+    v("set", (T.xx[:, 15::16], 0.0), "", "xL xR")
+    Jc = lambda i: T.J[:, 20 * i:20 * i + 20]
+    Ji = T.cI[:, 40:60]
+    v("ts", (Jc(1), Jc(0), lane, None, OP.add), "J0 lane", "J1")
+    v("ts", (Jc(2), Jc(1), -12.0, 0.04, OP.add, OP.mult), "J1", "J2")
+    v("copy", (Ji, Jc(2)), "J2", "Ji")
+    v("ts", (Jc(2), Ji, -25.0, None, OP.mult), "Ji", "J2")
+    v("ts", (Jc(3), Ji, -1.0, 24.0, OP.mult, OP.add), "Ji", "J3")
+    v("ts", (Jc(4), Ji, 1.0, None, OP.add), "Ji", "J4")
+    v("tt", (Jc(5), Jc(1), Jc(2), OP.add), "J1 J2", "J5")
+    v("tt", (Jc(6), Jc(5), Jc(3), OP.is_ge), "J5 J3", "J6")
+    v("tt", (Jc(7), Jc(6), Jc(3), OP.mult), "J6 J3", "J7")
+    v("tt", (Jc(5), Jc(5), Jc(7), OP.subtract), "J5 J7", "J5")
+    v("tt", (Jc(4), Jc(4), Jc(7), OP.max), "J4 J7", "J4")
+    v("copy", (T.lTH[:], Jc(4)), "J4", "lTH")
+    v("ts", (T.lBM[:, 0:19], T.J[:, 100:119], -1.0, 25.0, OP.mult, OP.add), "J5", "lBM0")
+    v("copy", (T.lBM[:, 19:38], T.J[:, 100:119]), "J5", "lBM1")
+    v("ts", (l3, lane, -3.0, None, OP.mult), "lane", "l3")
+    v("ts", (T.DT[:, 48:96], T.DT[:, 48:96], l3, 0.0, OP.add, OP.max), "DT1 l3", "DT1")
+    v("ts", (T.DT[:, 0:48], T.DT[:, 48:96], 3.0, None, OP.min), "DT1", "DT")
+    zA, zB, zE = "zA1 zA2 zA3", "zB0 zB3", keys("zE", 4)
+    for n, zs, items in (("A", " ".join((zA, zB, zE)), [(0, 0, 1.0, "BD"), (1, 1, 1.0, "BD"), (2, 0, 1.0, "BD"), (2, 1, -1.0, "BD"),
+                                                        (2, 2, 64.0, "BD"), (3, 0, l15, "BD OH0")]),
+                         ("B", zB, [(0, 1, l0, "BD OH0"), (3, 0, 1.0, "BD"), (3, 1, -1.0, "BD"), (3, 2, 16.0, "BD")]),
+                         ("E", zE, [(b, b, 1.0, "ID") for b in range(4)])):
+        for j, (i, s, sc, r) in enumerate(items):
+            act(T["t" + n][:, 512 * i + s:512 * i + 512:4], T[r[0:2]][:], r + " " + zs, "t%s%d" % (n, j), 128, f=AF.Identity, scale=sc)
+        for a, b in ((0, 1), (3, 4)) if n == "B" else ((0, 4),):
+            v("q", (T["kq" + n][:, 128 * a:128 * b], T["ks" + n][:, 128 * a:128 * b], T["t" + n][:, 512 * a:512 * b]),
+              keys("t" + n, len(items)), "k" + n, 140 * (b - a))
+
+    v("q", (T.qu[:], T.su[:], T.ut[:]), "ut", "qu", 150)
+    v("q", (T.qv[:], T.sv[:], T.vt[:]), "vt", "qv", 150)
+    for i in range(2):
+        off = T.upk[:, 8 * i:8 * i + 8]
+        v("copy", (T.qp[:, 128 * i:128 * i + 128].bitcast(dt.uint32), T.qu[:].bitcast(dt.uint32).indirect(off)), "qu upk", "qp%d" % i, 250)
+        act(T.sp[:, 128 * i:128 * i + 128], T.su[:].indirect(off), "qu upk", "sp%d" % i, 250)
+    v("q", (T.qx0[:, 128:], T.sx0[:, 128:], T.X[:, 512:]), XA, "qx0a", 290)
+    v("q", (T.qx0[:, 0:128], T.sx0[:, 0:128], T.X[:, 0:512]), XA + " Xb", "qx0b", 150)
+
+    for t in range(R):
+        qx, sx, lq, ls = [T[n + str(t)] for n in ("qx", "sx", "lq", "ls")]
+        kx = "qx%da qx%db" % (t, t)
+        send(lq[:].bitcast(dt.uint8), qx[:].bitcast(dt.uint8), "aq%d" % t, kx, "sent0")
+        send(ls[:], sx[:], "aq%d" % t, kx, "sent1")
+        landed("aq%d" % t, 2 * n_in, "sent0 sent1", "qL%d" % t, 4000.0)
+        for p, a, b, bs, bd in (("a", 128, C, 1, 3), ("b", 0, 128, 4, 5)):
+            n = b - a
+            for bk, i in ((bs, 0), (bd, 1)):
+                mm(bk, n, T.qp[:, 128 * i:128 * i + 128], T.sp[:, 128 * i:128 * i + 128], qx[:, a:b], sx[:, a:b], True, True,
+                   "qp%d sp%d qx%d%s" % (i, i, t, p))
+            ks = "#%d" % bs
+            act(T.A[:, 4 * a + 2:4 * b:4], bank(bd, n), "#%d" % bd, "A2" + p, n, f=AF.Sign)
+            v("scan", (rev(T.V, a, b), rev(T.c1, a, b), rbank(bs, n), 0.0, OP.add, OP.max), "c1 " + ks, "V" + p, n)
+            v("scan", (T.U[:, a:b], T.c2[:, a:b], bank(bs, n), 0.0, OP.add, OP.max), "c2 " + ks, "U" + p, n)
+            v("tt", (T.A[:, 4 * a:4 * b:4], bank(bs, n), T.V[:, a:b], OP.is_ge), ks + " V" + p, "A0" + p, n)
+            v("tt", (T.A[:, 4 * a + 5:4 * b:4], bank(bs, n, 1), T.U[:, a:b - 1], OP.is_gt), ks + " U" + p, "A1" + p, n)
+            act(T.S[:, a:b], bank(bs, n), ks, "S" + p, n)
+        v("tt", (T.TB[:, 65:89], T.V[:, 0::16], T.U[:, 15::16], OP.max), "Va Vb Ua Ub", "TBm")
+        act(T.BMx[:], T.TB[:, 64:96].indirect(T.lBM[:, 0:38]), "TBm lBM0 lBM1", "BMx", 60 + GA * 608)
+        v("copy", (T.TB[:, 1:25], T.U[:, 15::16]), "Ua Ub", "TBs")
+        v("copy", (T.TB[:, 33:57], T.V[:, C - 16::-16]), "Va Vb", "TBp")
+        v("set", (T.A[:, 1::64], 0.0), "", "A1a A1b")
+        v("scan", (T.CNT[:, 16:16 + C], T.seg[:], T.A[:, 0::4], 0.0, OP.mult, OP.add), "seg A0a A0b", "CL", 192)
+        v("scan", (T.CNT[:, 528:528 + C], T.seg[:], T.A[:, 1::4], 0.0, OP.mult, OP.add), "seg A1a A1b", "CR", 192)
+        v("tt", (T.m[:], T.CNT[:, 15::16], T.cc[:], OP.is_equal), "CL CR cc", "m", 128)
+        v("q", (T.qa[:], T.sa[:], T.A[:]), "A0a A0b A1a A1b A2a A2b A3", "qa", 420)
+        for b, i, stop in ((0, 1, False), (2, 0, False), (3, 2, False), (6, 3, True), (7, 4, True)):
+            cm(b, i, T.qa, T.sa, "qa", True, stop)
+        v("tt", (T.cov[:, 0:304], T.TB[:, 0:32].indirect(T.lTH[:, 0:19]), T.BMx[:, 0:304], OP.is_ge), "TBs lTH BMx", "cov0", 520)
+        v("tt", (T.cov[:, 304:608], T.TB[:, 32:64].indirect(T.lTH[:, 0:19]), T.BMx[:, 304:608], OP.is_gt), "TBp lTH BMx", "cov1", 520)
+        v("scan", (T.run[:], T.one[:], T.cov[:], 0.0, OP.add, OP.mult), "one one1 cov0 cov1", "run", 304)
+        v("copy", (T.E[:, 0:64], T.run[:].indirect(T.lE[:, 0:4])), "run lE", "E", 150)
+        v("tt", (T.E[:, 64:128], T.base[:], T.E[:, 0:64], OP.subtract), "base0 base1 E", "t1", 128)
+        v("tt", (T.TD[:, 64:128], T.E[:, 0:64], T.m[:], OP.mult), "E m", "TD1", 128)
+        v("tt", (T.TD[:, 0:64], T.E[:, 64:128], T.m[:], OP.mult), "t1 m", "TD0", 128)
+        v("copy", (T.tt[:, 1:65], T.TD[:, 0:64]), "TD0", "tt")
+        v("tt", (sm(9), T.TD[:, 97:121], T.TD[:, 65:89], OP.subtract), "TD1", "sm9")
+        v("ts", (T.lD[:], sm(9), NB - 1.0, None, OP.add), "sm9", "lD")
+        v("ts", (T.TD[:, 128:192], T.TD[:, 64:128], -16.0, None, OP.mult), "TD1", "TD2")
+        v("tt", (T.aX[:, 64:128], T.aX[:, 0:64], T.TD[:, 128:192], OP.add), "aX0 aX1 TD2", "aX2", 128)
+        act(T.B[:, 2::4], T.DT[:, 0:48].indirect(T.lD[:, 0:24]), "DT lD", "B2", GC)
+        v("tt", (T.B[:, 1::4], T.TB[:, 0:32].indirect(T.tt[:, 2:26]), T.S[:], OP.is_lt), "TBs tt Sa Sb", "B1", GC)
+        v("tt", (T.B[:, 0::4], T.TB[:, 32:64].indirect(T.tt[:, 34:58]), T.S[:], OP.is_le), "TBp tt Sa Sb", "B0", GC)
+        v("q", (T.qb[:], T.sb[:], T.B[:]), "B0 B1 B2 B3", "qb", 420)
+        for b, i in ((0, 1), (2, 0), (3, 7)):
+            cm(b, i, T.qb, T.sb, "qb", False, True)
+        for i, a in ((0, 34), (1, 2)):
+            act(T.junk[:, C * i:C * i + C], T.OH[:].indirect(T.tt[:, a:a + 24]), "OH0 OH1 tt", "junk%d acc%d" % (i, i), GC,
+                accum_out=T.acc[:, i:i + 1])
+        v("copy", (T.WI[:, 8:10], T.acc[:]), "acc0 acc1", "WI2")
+        v("ts", (T.WI[:, 0:4:2], T.WI[:, 8:10], 511, None, OP.bitwise_and), "WI2", "WI0")
+        v("ts", (T.WI[:, 1:4:2], T.WI[:, 8:10], 9, None, OP.arith_shift_right), "WI2", "WI1")
+        v("copy", (T.rp[:], T.WI[:, 0:4].indirect(T.upk[:, 16:24])), "WI0 WI1 upk", "rp", 250)
+        v("tr", (T.rt[:], T.rp[:]), "rp", "rt", 128)
+        v("ts", (T.dL[:, 0::16], T.rt[:].indirect(T.lE[:, 4:6]), -1.0, None, OP.mult), "rt lT", "dL", 100)
+        v("ts", (T.dR[:, 15::16], T.rt[:].indirect(T.lE[:, 6:8]), -1.0, None, OP.mult), "rt lT", "dR", 100)
+        v("scan", (T.GL[:, 1:C + 1], T.dL[:, 0:C], bank(6), 0.0, OP.add, OP.add), "dL #6", "GL", C)
+        v("scan", (T.GR[:, 1:C + 1], rev(T.dR), rbank(7), 0.0, OP.add, OP.add), "dR #7", "GR", C)
+        v("scan", (T.xx[:, 16:16 + C], bank(0), T.c5[:], -5000.0, OP.max, OP.add), "#0 c5", "xL", C)
+        v("scan", (T.xx[:, 528:528 + C], bank(2), T.c5[:], -5000.0, OP.max, OP.add), "#2 c5", "xR", C)
+        v("tt", (T.uu[:, 0:64], T.aX[:, 64:128], T.xx[:, 15::16], OP.subtract), "aX2 xL xR", "u", 128)
+        v("tt", (T.uu[:, 64:128], T.uu[:, 0:64], T.m[:], OP.mult), "u m", "um", 128)
+        v("ts", (T.lp[:, 1:65], T.uu[:, 64:128], 392.0, None, OP.add), "um", "lp")
+        v("tt", (T.zt[:], bank(3), T.a2row[:], OP.add), "#3 a2row", "zt", C)
+        act(T.z[:], T.zt[:], "zt", "z", C, f=AF.Relu)
+        act(T.GgL[:], T.GL[:].indirect(T.lp[:, 2:26]), "GL GL0 GL1 lp", "GgL", GC)
+        v("copy", (T.GgR[:], T.GR[:].indirect(T.lp[:, 34:58])), "GR GR0 GR1 lp zt", "GgR", GC)
+        v("scan", (T.mL[:], T.GgL[:], T.c4[:], 5000.0, OP.min, OP.add), "GgL c4", "mL", C)
+        v("scan", (rev(T.mR), rev(T.GgR), rev(T.c3), 5000.0, OP.min, OP.add), "GgR c3", "mR", C)
+        v("tt", (sm(0), T.CNT[:, 543:543 + C:16], T.CNT[:, 31:31 + C:16], OP.subtract), "CL CR", "sm0")
+        v("ts", (sm(1), T.uu[:, 1:25], 2.0, 785.0, OP.mult, OP.add), "u", "sm1")
+        v("ts", (sm(2), T.uu[:, 33:57], -2.0, -16.0, OP.mult, OP.add), "u", "sm2")
+        for i in (1, 2):
+            v("tt", (sm(i), sm(i), sm(0), OP.add), "sm%d sm0" % i, "sm%d" % i)
+            v("tt", (sm(i + 2), sm(i), T.mR[:, 0::16], OP.add), "sm%d mR" % i, "sm%d" % (i + 2))
+            v("tt", (sm(i + 4), sm(i + 2), T.mL[:, 15::16], OP.subtract), "sm%d mL" % (i + 2), "sm%d" % (i + 4))
+        v("copy", (T.oc16[:], T.sm[:, 120:168]), "sm5 sm6", "oc16")
+        DB, OB = (0, 2, 6, 7), (1, 3, 4, 5)
+        for b in range(4):
+            cm(DB[b], 8 + b, lq, ls, "qL%d lp" % t, True, True)
+            act(T.Dd[:, b::4], bank(DB[b]), "#%d oc16" % DB[b], "Dd%d" % b, C)
+        v("copy", (T.EW[:].indirect(T.oc16[:, 0:24]), T.z[:]), "oc16 z", "EW", 50 + SC * C)
+        v("copy", (T.EW[:].indirect(T.oc16[:, 24:48]), T.z[:]), "oc16 z", "EW", 50 + SC * C)
+        for h in range(2):
+            act(T.PH[:, C * h:C * h + C], T.EW[:, C * h:C * h + C], "EW", "PH%d" % h, C, f=AF.Sign, scale=-1.0, bias=0.5)
+        v("scan", (T.Y[:, 0:C], T.PH[:, 0:C], T.EW[:, 0:C], 0.0, OP.mult, OP.subtract), "PH0 EW", "Y0", C)
+        v("scan", (T.Y[:, C:], T.PH[:, C:], T.EW[:, C:], T.Y[:, C - 1:C], OP.mult, OP.subtract), "PH1 EW Y0", "Y1", C)
+        act(T.Yg[:, 192:], T.Y[:].indirect(T.oc16[:, 12:24]), "Y0 Y1 oc16", "Yg1", 350)
+        v("copy", (T.Yg[:, 0:192], T.Y[:].indirect(T.oc16[:, 0:12])), "Y0 Y1 oc16", "Yg0", 350)
+        v("scan", (T.dg[:], T.Yg[:], T.c5y[:], -5000.0, OP.max, OP.add), "Yg0 Yg1 c5y", "dg", C)
+        act(sm(7), T.dg[:, 15::16], "dg", "sm7", 64, f=AF.Abs, bias=4000.0)
+        v("ts", (T.at[:], sm(7), -0.5, None, OP.add), "sm7", "at")
+        v("copy", (T.O[:].indirect(T.at[:, 0:24]), T.arow[:]), "at arow", "O", 50 + SC * C)
+        ob, ll = T.ob[:, 24 * t:24 * t + 24], T.ll[:, 24 * t:24 * t + 24]
+        v("scan", (T.o4[:, H:], T.O[:, H:], T.c6[:, H:], -5000.0, OP.max, OP.add), "O c6", "o4b", K)
+        v("ts", (ob, T.o4[:, H + 3::4], 4.0, l4c, OP.mult, OP.add), "o4b l4c", "ob%d" % t)
+        send(ll, ob, "al%d" % t, "ob%d" % t, "sent2")
+        landed("al%d" % t, n_in, "sent2", "ll%d" % t, 2200.0)
+        if t == R - 1:
+            dma("y", "dol", T.ol[:], T.O[0:128:16, :], "O", "")
+        v("scan", (T.o4[:, 0:H], T.O[:, 0:H], T.c6[:, 0:H], -5000.0, OP.max, OP.add), "O c6", "o4a", H)
+        v("ts", (T.oo[:], T.o4[:, 3:H:4], 4.0, l4c, OP.mult, OP.add), "o4a l4c", "oo", 72)
+        act(T.Z[:, 960:], T.X[:].indirect(T.oo[:, 36:72]), XA + " Xb oo", "Z2", 950)
+        v("copy", (T.Z[:, 384:960], T.X[:].indirect(T.oo[:, 0:36])), XA + " Xb oo", "Z1", 950)
+        act(T.Z[:, 0:384], T.Dd[:].indirect(ll), keys("Dd", 4) + " ll%d" % t, "Z0", GC)
+        v("q", (T.qz[:, K:], T.sz[:, K:], T.Z[:, 4 * K:]), "Z1 Z2", "qz", 320)
+        wv = lambda b: (T.wq[:, 128 * b:128 * b + 128], T.wsp[:, 128 * b:128 * b + 128])
+        v("ts", (T.Z64[:, 4 * K:], T.Z[:, 4 * K:], 64.0, None, OP.mult), "Z1 Z2", "Z64a", 2 * H)
+        for b in range(4):
+            mm(OB[b], H, *wv(b), T.qz[:, K:], T.sz[:, K:], True, True, "wq wsp qz")
+            v("tt", (T.X64[:, 4 * K + b::4], bank(OB[b], H), T.Z64[:, 4 * K + b::4], OP.add), "#%d Z64a" % OB[b], "X64a%d" % b, H)
+            act(T.X[:, 4 * K + b::4], T.X64[:, 4 * K + b::4], "X64a%d" % b, "Xa%d" % b, H, scale=0.015625)
+        v("q", (T.qzb[:], T.szb[:], T.Z[:, 0:512]), "Z0 Z1", "qzb", 150)
+        v("ts", (T.Z64[:, 0:4 * K], T.Z[:, 0:4 * K], 64.0, None, OP.mult), "Z0", "Z64b", 2 * K)
+        for b in range(4):
+            mm(DB[b], 128, *wv(b), T.qzb[:], T.szb[:], True, True, "wq wsp qzb")
+            v("tt", (T.X64[:, b:4 * K:4], bank(DB[b], K), T.Z64[:, b:4 * K:4], OP.add), "#%d Z64b" % DB[b], "X64b%d" % b, K)
+        qn, sn = T["qx%d" % (t + 1)], T["sx%d" % (t + 1)]
+        v("q", (qn[:, 128:], sn[:, 128:], T.X[:, 512:]), XA, "qx%da" % (t + 1), 290)
+        v("ts", (T.X[:, 0:4 * K], T.X64[:, 0:4 * K], 0.015625, None, OP.mult), keys("X64b", 4), "Xb", 2 * K)
+        v("q", (qn[:, 0:128], sn[:, 0:128], T.X[:, 0:512]), XA + " Xb", "qx%db" % (t + 1), 150)
+
+    for p, a, b, bk in (("a", 128, C, 1), ("b", 0, 128, 4)):
+        kx = "qx%d%s" % (R, p)
+        mm(bk, b - a, T.qv[:], T.sv[:], T.qx3[:, a:b], T.sx3[:, a:b], True, True, "qv " + kx)
+        dma("y", "doc", T.oc[:, 4 * a:4 * b], T.qx3[:, a:b].bitcast(dt.uint8), kx, "")
+        v("copy", (T.ys[:, a:b], bank(bk, b - a)), "#%d" % bk, "ys" + p, b - a)
+        dma("s", "dy", T.y[:, a:b], T.ys[:, a:b], "ys" + p, "")
+    for k in range(4):
+        dma("y", "dos", T.osc[4 * k:4 * k + 4, :], T.sx3[32 * k:32 * k + 4, :], "qx%da qx%db" % (R, R), "")
+
+    n = len(ops)
+    ahead, users, left = [0.0] * n, [[] for _ in ops], [len(o["deps"]) for o in ops]
+    for i, o in enumerate(ops):
+        for d in o["deps"]:
+            users[d].append(i)
+    for i in range(n - 1, -1, -1):
+        ahead[i] = ops[i]["busy"] + ops[i]["lag"] + max([ahead[j] for j in users[i]] + [0.0])
+    ready, free, order = {i: 0.0 for i in range(n) if not left[i]}, {q: 0.0 for q in "vstgyx"}, []
+    while ready:
+        at = {i: max(tm, free[ops[i]["q"]]) for i, tm in ready.items()}
+        i0 = min(at, key=lambda i: (at[i], -ahead[i]))
+        mine = [i for i in at if ops[i]["q"] == ops[i0]["q"]]
+        best = max([i for i in mine if at[i] <= at[i0] + 300.0], key=lambda i: ahead[i])
+        fill = [i for i in mine if at[i] < at[best] and at[i] + ops[i]["busy"] <= at[best] + 30.0]
+        i = max(fill, key=lambda i: ahead[i]) if fill else best
+        o = ops[i]
+        del ready[i]
+        order.append(i)
+        free[o["q"]] = o["end"] = at[i] + o["busy"]
+        for j in users[i]:
+            left[j] -= 1
+            if not left[j]:
+                ready[j] = max(ops[d]["end"] + (ops[d]["lag"] if s else 0.0) for d, s in ops[j]["deps"].items())
+    total, known = {}, {q: {} for q in QS}
+
+    def wait(q, sem, val):
+        if known[q].get(sem, 0) < val:
+            QS[q].wait_ge(T.sem[sem], val)
+            known[q][sem] = val
+
+    for i in order:
+        o = ops[i]
+        if o["emit"]:
+            need = {}
+            for d, s in o["deps"].items():
+                if s and ops[d]["sem"] != "loc":
+                    need[ops[d]["sem"]] = max(need.get(ops[d]["sem"], 0), ops[d]["count"])
+            for sem, val in need.items():
+                wait(o["q"], sem, val)
+            o["emit"]()
+        total[o["sem"]] = o["count"] = total.get(o["sem"], 0) + o["inc"]
+    for sem, val in total.items():
+        wait("g", sem, val)

@@ -7,15 +7,15 @@ BIG = 1e28
 
 SCRATCH = {"ps": ("psum", [128, 4096], F32)}
 for _d, _l in (
-        (BF, "X:1536 X64:1536 Z:1536 Z64:1536 Dd:1536 ut:512 vt:512 tA:2048 tB:2048 tE:2048 A:1536 B:1536 one:608 BD:128 ID:128 "
+        (BF, "X:1536 X64:1536 Z:1536 Z64:1536 Dd:1536 ut:512 vt:512 tA:2048 tB:1024 tE:2048 A:1536 B:1536 one:608 BD:128 ID:128 "
              "seg:384 CNT:1024 cov:608 run:608 junk:768"),
-        (Q4, "qu:128 qv:128 qp:256 wq:512 qz:384 qzb:128 kqA:512 kqB:512 kqE:512 qa:384 qb:384 qx0:384 qx1:384 qx2:384 qx3:384 lq0:384 lq1:384 lq2:384"),
-        (U8, "su:128 sv:128 sp:256 wsp:512 sz:384 szb:128 ksA:512 ksB:512 ksE:512 sa:384 sb:384 sx0:384 sx1:384 sx2:384 sx3:384 ls0:384 ls1:384 ls2:384"),
+        (Q4, "qu:128 qv:128 qp:256 wq:512 qz:384 qzb:128 kqA:512 kqB:256 kqE:512 qa:384 qb:384 qx0:384 qx1:384 qx2:384 qx3:384 lq0:384 lq1:384 lq2:384"),
+        (U8, "su:128 sv:128 sp:256 wsp:512 sz:384 szb:128 ksA:512 ksB:256 ksE:512 sa:384 sb:384 sx0:384 sx1:384 sx2:384 sx3:384 ls0:384 ls1:384 ls2:384"),
         (I32, "cI:64 WI:16"),
-        (U16, "rep:24 upk:24 lBM:38 lTH:20 lE:8 tt:66 lD:24 lp:66 oc16:48 at:24 oo:72 ob:72 ll:72"),
-        (F32, "cF:16 dm:32 tm:32 PP:96 c1:384 c2:384 c3:384 c4:384 c5:384 c5y:384 c6:384 arow:384 a2row:384 aW:48 aX:128 J:160 ER:128 ERd:128 "
+        (U16, "rep:24 upk:24 lBM:38 lTH:20 lE:8 tt:66 lD:24 lp:48 oc16:48 at:24 oo:72 ob:72 ll:72"),
+        (F32, "cF:16 dm:32 tm:32 PP:96 c1:384 c2:384 c3:384 c4:384 c5:384 c5y:384 c5r:384 c6:384 arow:384 a2row:384 aW:48 aX:128 J:160 ER:128 ERd:128 "
               "DT:96 OH:32 base:64 cc:64 S:384 V:384 U:384 TB:96 BMx:608 m:64 E:128 TD:192 acc:2 rp:128 rt:128 dL:512 dR:512 GL:400 GR:400 "
-              "GgL:384 GgR:384 mL:384 mR:384 xx:1024 uu:128 sm:256 zt:384 z:384 EW:768 PH:768 Y:768 Yg:384 dg:384 O:384 o4:384 ys:384")):
+              "GgL:384 GgR:384 mL:384 mR:384 xx:768 uu:128 sm:288 zt:384 z:384 EW:768 PH:768 Y:768 Yg:384 dg:384 O:384 o4:384 ys:384")):
     for _e in _l.split():
         _n, _w = _e.split(":")
         SCRATCH[_n] = ("sbuf", [128, int(_w)], _d)
@@ -23,7 +23,8 @@ for _d, _l in (
 SEMAPHORES = ["v", "s", "t", "g", "dx", "du", "dv", "dwc", "dws", "dkA", "dkB", "dkE", "dy", "dol", "doc", "dos", "loc"] + \
              ["aq%d" % t for t in range(R)] + ["al%d" % t for t in range(R)]
 
-GA, SC, LAG = 1.56, 3.8, 120.0
+GA, SC, LAG = 1.45, 3.2, 200.0
+ORDER, TRIES = {}, 4000
 
 
 def rank_program(g, core, T, topo):
@@ -60,7 +61,7 @@ def rank_program(g, core, T, topo):
                 "scan": lambda: e.tensor_tensor_scan(*args), "set": lambda: e.memset(*args), "q": lambda: e.quantize_mx(*args),
                 "tr": lambda: e.transpose(*args), "act": lambda: e.activation(*args, **kw), "mm": lambda: e.matmul_mx(*args),
                 "iota": lambda: e.iota(*args, **kw), "sel": lambda: e.affine_select(*args)}[name]
-        add(q, lambda: call().then_inc(T.sem[q], 1), r, w, max(c, 64) * 1.04, LAG, q, 1, acc)
+        add(q, lambda: call().then_inc(T.sem[q], 1), r, w, max(c, 64) * 0.95, LAG, q, 1, acc)
 
     def dma(q, sem, out, in_, r, w):
         add(q, lambda: QS[q].dma_start(out, in_).then_inc(T.sem[sem], 16), r, w, 100.0, 2200.0, sem, 16)
@@ -95,11 +96,10 @@ def rank_program(g, core, T, topo):
     def mm(b, n, lq, ls, rq, rs, start, stop, r):
         op("t", "mm", (bank(b, n), lq, ls, rq, rs, start, stop), r, "#%d" % b, 0.7 * (n + 16), acc=not start)
 
-    def cm(b, i, rq, rs, key, start, stop):
-        n, a = "ABE"[i // 4], 128 * (i % 4)
-        mm(b, C, T["kq" + n][:, a:a + 128], T["ks" + n][:, a:a + 128], rq[:], rs[:], start, stop, "k%s %s" % (n, key))
+    def cm(b, n, i, rq, rs, key, start, stop):
+        mm(b, C, T["kq" + n][:, 128 * i:128 * i + 128], T["ks" + n][:, 128 * i:128 * i + 128], rq[:], rs[:], start, stop, "k%s %s" % (n, key))
 
-    lane, l4c, lq4, e16, l3 = [T.cF[:, i:i + 1] for i in range(5)]
+    lane, l4c, lq4, e16, l3, c15 = [T.cF[:, i:i + 1] for i in range(6)]
     l0, l15 = T.OH[:, 0:1], T.OH[:, 15:16]
     sm = lambda i: T.sm[:, 24 * i:24 * i + 24]
     keys = lambda s, n: " ".join(s + str(i) for i in range(n))
@@ -119,7 +119,7 @@ def rank_program(g, core, T, topo):
     iota(T.tm[:, 16:32], [[0, 4], [1, 4]], 0, "tm1")
     iota(T.aW[:, 0:24], [[16, NB]], 0, "aW0")
     iota(T.J[:, 0:20], [[16, 20]], 0, "J0")
-    for name, w, parts in (("base", 64, ((1, 24, 1, 0), (33, 24, -1, 23))),
+    for name, w, parts in (("base", 64, ((1, 24, 1, 100), (33, 24, -1, 123))),
                            ("ER", 128, ((1, 12, 25, 328), (13, 12, -24, 591), (33, 12, 24, 23), (45, 12, -25, 299),
                                         (64, 9, -1, 40), (73, 15, -1, 15), (96, 15, 1, 65), (111, 9, 1, 96)))):
         iota(T[name][:], [[0, w]], 0, keys(name, 8), w)
@@ -137,15 +137,14 @@ def rank_program(g, core, T, topo):
     op("g", "sel", (T.dR[:, 0:C], T.one[:, 0:C], [[0, NB], [1, 16]], OP.is_equal, 0.0, 0, 0), "one", "dR", 170 + 2 * C)
     iota(T.dL[:, 0:C], [[0, C]], 0, "dL", C)
     iota(T.cc[:], [[-1, 2], [0, 32]], 1, "cc", 64)
+    iota(T.CNT[:, 15::16], [[0, 64]], 5, "CL CR", 64)
     iota(T.aX[:, 0:64], [[0, 64]], 0, "aX0 aX1", 64)
     for n in ("GL", "GR"):
-        iota(T[n][:, 0:1], [[0, 1]], 0, n + "0")
-        iota(T[n][:, C + 1:], [[0, 15]], 900, n + "1")
+        iota(T[n][:, 0:2], [[-900, 2]], 900, n + "0")
     v("set", (T.tA[:, 0:512], 0.0), "", "tA0", 256)
-    for n, first in (("A", 1), ("B", 0), ("E", 0)):
-        for i in range(first, 4):
-            if n != "B" or i in (0, 3):
-                dma("y", "dk" + n, T["t" + n][:, 512 * i:512 * i + 512], T.tA[:, 0:512], "tA0", "z%s%d" % (n, i))
+    for n, a, b in (("A", 1, 4), ("B", 0, 2), ("E", 0, 4)):
+        for i in range(a, b):
+            dma("y", "dk" + n, T["t" + n][:, 512 * i:512 * i + 512], T.tA[:, 0:512], "tA0", "z%s%d" % (n, i))
     for col, key, n in ((lane, "lane", 15), (e16, "e16", 16)):
         v("ts", (T.cI[:, n - 14:n - 13], T.cI[:, 0:1], n, None, OP.bitwise_and), "cI0", "i" + key)
         v("copy", (col, T.cI[:, n - 14:n - 13]), "i" + key, key)
@@ -157,20 +156,22 @@ def rank_program(g, core, T, topo):
     v("ts", (T.rep[:], T.aW[:, 0:24], 0.0, lane, OP.mult, OP.add), "aW0 lane", "rep")
     v("ts", (T.dm[:, 0:16], T.tm[:, 0:16], lane, None, OP.subtract), "tm0 lane", "dm0")
     v("ts", (T.dm[:, 16:32], T.tm[:, 16:32], lq4, None, OP.subtract), "tm1 lq4", "dm1")
-    for i, col, a, b in ((0, 15, -10 * BIG, BIG), (1, 0, -10 * BIG, BIG), (2, 0, -1000.0, 3000.0), (3, 15, -1000.0, 3000.0)):
+    for i, col, a, b in ((0, 15, -10 * BIG, BIG), (1, 0, -10 * BIG, BIG), (2, 0, -1000.0, 3000.0), (3, 15, -1000.0, 0.0)):
         v("ts", (T.PP[:, 16 * i:16 * i + 16], T.dm[:, 0:16], 0.0, a, OP.is_equal, OP.mult), "dm0", "PP%d" % i)
         one = T.PP[:, 16 * i + col:16 * i + col + 1]
-        v("ts", (one, one, b, None, OP.add), "PP%d" % i, "PP%d" % i)
+        if b:
+            v("ts", (one, one, b, None, OP.add), "PP%d" % i, "PP%d" % i)
+    v("ts", (c15, T.PP[:, 63:64], 14001.0, None, OP.add), "PP3", "c15")
     v("ts", (T.PP[:, 64:96], T.dm[:], 0.0, 2000.0, OP.is_equal, OP.mult), "dm0 dm1", "PP4 PP5")
     v("ts", (T.tm[:], T.dm[:], -1.0, -4000.0, OP.is_equal, OP.mult), "dm0 dm1", "tm0 tm1")
     v("tt", (T.PP[:, 64:96], T.PP[:, 64:96], T.tm[:], OP.add), "PP4 PP5 tm0 tm1", "PP4 PP5")
     v("ts", (T.PP[:, 79:96:4], T.PP[:, 79:96:4], -6000.0, None, OP.add), "PP4 PP5", "PP4 PP5")
-    for name, i in (("c1", 0), ("c2", 1), ("c3", 2), ("c4", 3), ("c5", 4), ("c5y", 4), ("c6", 5)):
+    for name, i in (("c1", 0), ("c2", 1), ("c3", 2), ("c4", 3), ("c5", 4), ("c5y", 4), ("c5r", 4), ("c6", 5)):
         act(T[name][:], T.PP[:, 16 * i:16 * i + 16].indirect(T.rep[:, 0:24]), "PP%d rep" % i, name, GC)
     v("ts", (T.aW[:, 24:48], T.aW[:, 0:24], lane, 0.5, OP.add, OP.add), "aW0 lane", "aW1")
     v("tt", (T.c5y[:, 15::16], T.c5y[:, 15::16], T.aW[:, 24:48], OP.add), "c5y aW1", "c5y")
-    v("ts", (T.aX[:, 1:25], T.aW[:, 24:48], -4392.5, None, OP.add), "aW1", "aX0")
-    v("ts", (T.aX[:, 33:57], T.aW[:, 24:48], -1.0, C - 4391.5, OP.mult, OP.add), "aW1", "aX1")
+    v("ts", (T.aX[:, 1:25], T.aW[:, 24:48], -999.5, None, OP.add), "aW1", "aX0")
+    v("ts", (T.aX[:, 33:57], T.aW[:, 24:48], -1.0, C - 998.5, OP.mult, OP.add), "aW1", "aX1")
     v("scan", (T.ERd[:], T.ER[:], T.c5[:, 0:128], -5000.0, OP.max, OP.add), keys("ER", 8) + " c5", "ERd", 128)
     v("ts", (T.lE[:, 0:4], T.ERd[:, 15:64:16], 4000.0, None, OP.add), "ERd", "lE")
     v("ts", (T.lE[:, 4:8], T.ERd[:, 79::16], 4000.0, e16, OP.add, OP.add), "ERd e16", "lT")
@@ -179,8 +180,6 @@ def rank_program(g, core, T, topo):
     v("set", (T.TB[:], BIG), "", "TBs TBp TBm", 96)
     v("set", (T.A[:, 3::4], 0.0), "", "A3", 192)
     v("set", (T.B[:, 3::4], 0.0), "", "B3", 192)
-    v("set", (T.CNT[:, 15::16], 5.0), "", "CL CR")
-    v("set", (T.xx[:, 15::16], 0.0), "", "xL xR")
     Jc = lambda i: T.J[:, 20 * i:20 * i + 20]
     Ji = T.cI[:, 40:60]
     v("ts", (Jc(1), Jc(0), lane, None, OP.add), "J0 lane", "J1")
@@ -200,16 +199,14 @@ def rank_program(g, core, T, topo):
     v("ts", (l3, lane, -3.0, None, OP.mult), "lane", "l3")
     v("ts", (T.DT[:, 48:96], T.DT[:, 48:96], l3, 0.0, OP.add, OP.max), "DT1 l3", "DT1")
     v("ts", (T.DT[:, 0:48], T.DT[:, 48:96], 3.0, None, OP.min), "DT1", "DT")
-    zA, zB, zE = "zA1 zA2 zA3", "zB0 zB3", keys("zE", 4)
-    for n, zs, items in (("A", " ".join((zA, zB, zE)), [(0, 0, 1.0, "BD"), (1, 1, 1.0, "BD"), (2, 0, 1.0, "BD"), (2, 1, -1.0, "BD"),
-                                                        (2, 2, 64.0, "BD"), (3, 0, l15, "BD OH0")]),
-                         ("B", zB, [(0, 1, l0, "BD OH0"), (3, 0, 1.0, "BD"), (3, 1, -1.0, "BD"), (3, 2, 16.0, "BD")]),
+    zA, zB, zE = "zA1 zA2 zA3", "zB0 zB1", keys("zE", 4)
+    for n, zs, items in (("A", " ".join((zA, zB, zE)), [(0, 0, 1.0, "BD"), (1, 1, 1.0, "BD"), (2, 0, 1.0, "BD"),
+                                                        (2, 1, -1.0, "BD"), (2, 2, 64.0, "BD"), (3, 0, l15, "BD OH0")]),
+                         ("B", zB, [(0, 1, l0, "BD OH0"), (1, 0, 1.0, "BD"), (1, 1, -1.0, "BD"), (1, 2, 16.0, "BD")]),
                          ("E", zE, [(b, b, 1.0, "ID") for b in range(4)])):
         for j, (i, s, sc, r) in enumerate(items):
             act(T["t" + n][:, 512 * i + s:512 * i + 512:4], T[r[0:2]][:], r + " " + zs, "t%s%d" % (n, j), 128, f=AF.Identity, scale=sc)
-        for a, b in ((0, 1), (3, 4)) if n == "B" else ((0, 4),):
-            v("q", (T["kq" + n][:, 128 * a:128 * b], T["ks" + n][:, 128 * a:128 * b], T["t" + n][:, 512 * a:512 * b]),
-              keys("t" + n, len(items)), "k" + n, 140 * (b - a))
+        v("q", (T["kq" + n][:], T["ks" + n][:], T["t" + n][:]), keys("t" + n, len(items)), "k" + n, 280 if n == "B" else 550)
 
     v("q", (T.qu[:], T.su[:], T.ut[:]), "ut", "qu", 150)
     v("q", (T.qv[:], T.sv[:], T.vt[:]), "vt", "qv", 150)
@@ -239,7 +236,10 @@ def rank_program(g, core, T, topo):
             v("tt", (T.A[:, 4 * a + 5:4 * b:4], bank(bs, n, 1), T.U[:, a:b - 1], OP.is_gt), ks + " U" + p, "A1" + p, n)
             act(T.S[:, a:b], bank(bs, n), ks, "S" + p, n)
         v("tt", (T.TB[:, 65:89], T.V[:, 0::16], T.U[:, 15::16], OP.max), "Va Vb Ua Ub", "TBm")
-        act(T.BMx[:], T.TB[:, 64:96].indirect(T.lBM[:, 0:38]), "TBm lBM0 lBM1", "BMx", 60 + GA * 608)
+        for h in range(2):
+            a = 18 * h
+            act(T.BMx[:, 16 * a:608 if h else 304], T.TB[:, 64:96].indirect(T.lBM[:, a:38 if h else 19]), "TBm lBM0 lBM1",
+                "BMx1 BMx0" if h else "BMx0 BMx2", 60 + GA * 312)
         v("copy", (T.TB[:, 1:25], T.U[:, 15::16]), "Ua Ub", "TBs")
         v("copy", (T.TB[:, 33:57], T.V[:, C - 16::-16]), "Va Vb", "TBp")
         v("set", (T.A[:, 1::64], 0.0), "", "A1a A1b")
@@ -247,26 +247,30 @@ def rank_program(g, core, T, topo):
         v("scan", (T.CNT[:, 528:528 + C], T.seg[:], T.A[:, 1::4], 0.0, OP.mult, OP.add), "seg A1a A1b", "CR", 192)
         v("tt", (T.m[:], T.CNT[:, 15::16], T.cc[:], OP.is_equal), "CL CR cc", "m", 128)
         v("q", (T.qa[:], T.sa[:], T.A[:]), "A0a A0b A1a A1b A2a A2b A3", "qa", 420)
-        for b, i, stop in ((0, 1, False), (2, 0, False), (3, 2, False), (6, 3, True), (7, 4, True)):
-            cm(b, i, T.qa, T.sa, "qa", True, stop)
-        v("tt", (T.cov[:, 0:304], T.TB[:, 0:32].indirect(T.lTH[:, 0:19]), T.BMx[:, 0:304], OP.is_ge), "TBs lTH BMx", "cov0", 520)
-        v("tt", (T.cov[:, 304:608], T.TB[:, 32:64].indirect(T.lTH[:, 0:19]), T.BMx[:, 304:608], OP.is_gt), "TBp lTH BMx", "cov1", 520)
+        for b, n, i, stop in ((0, "A", 1, False), (2, "A", 0, False), (3, "A", 2, False), (6, "A", 3, True), (7, "B", 0, True)):
+            cm(b, n, i, T.qa, T.sa, "qa", True, stop)
+        v("tt", (T.cov[:, 0:304], T.TB[:, 0:32].indirect(T.lTH[:, 0:19]), T.BMx[:, 0:304], OP.is_ge), "TBs lTH BMx0", "cov0", 500)
+        v("tt", (T.cov[:, 304:608], T.TB[:, 32:64].indirect(T.lTH[:, 0:19]), T.BMx[:, 304:608], OP.is_gt), "TBp lTH BMx1", "cov1", 500)
         v("scan", (T.run[:], T.one[:], T.cov[:], 0.0, OP.add, OP.mult), "one one1 cov0 cov1", "run", 304)
-        v("copy", (T.E[:, 0:64], T.run[:].indirect(T.lE[:, 0:4])), "run lE", "E", 150)
-        v("tt", (T.E[:, 64:128], T.base[:], T.E[:, 0:64], OP.subtract), "base0 base1 E", "t1", 128)
-        v("tt", (T.TD[:, 64:128], T.E[:, 0:64], T.m[:], OP.mult), "E m", "TD1", 128)
-        v("tt", (T.TD[:, 0:64], T.E[:, 64:128], T.m[:], OP.mult), "t1 m", "TD0", 128)
-        v("copy", (T.tt[:, 1:65], T.TD[:, 0:64]), "TD0", "tt")
+        ends = T.run[:].indirect(T.lE[:, 0:4])
+        v("tt", (T.E[:, 64:128], T.base[:], T.m[:], OP.mult), "base0 base1 m", "mb", 128)
+        v("tt", (T.E[:, 0:64], ends, T.E[:, 64:128], OP.subtract), "run lE mb", "E", 150)
+        v("ts", (T.tt[:, 1:65], T.E[:, 0:64], -1.0, -100.0, OP.mult, OP.add), "E", "tt")
+        v("tt", (T.TD[:, 64:128], ends, T.m[:], OP.mult), "run lE m", "TD1", 150)
         v("tt", (sm(9), T.TD[:, 97:121], T.TD[:, 65:89], OP.subtract), "TD1", "sm9")
         v("ts", (T.lD[:], sm(9), NB - 1.0, None, OP.add), "sm9", "lD")
-        v("ts", (T.TD[:, 128:192], T.TD[:, 64:128], -16.0, None, OP.mult), "TD1", "TD2")
-        v("tt", (T.aX[:, 64:128], T.aX[:, 0:64], T.TD[:, 128:192], OP.add), "aX0 aX1 TD2", "aX2", 128)
+        v("ts", (T.uu[:, 0:64], T.m[:], 1000.0, None, OP.mult), "m", "mk")
+        v("tt", (T.uu[:, 64:128], T.uu[:, 0:64], T.aX[:, 0:64], OP.add), "mk aX0 aX1", "aXa", 128)
+        v("ts", (T.TD[:, 128:192], T.TD[:, 64:128], 16.0, None, OP.mult), "TD1", "TD2")
+        v("tt", (T.aX[:, 64:128], T.TD[:, 128:192], T.uu[:, 64:128], OP.subtract), "aXa TD2", "aX2", 128)
+        v("ts", (T.c5[:, 15::16], T.aX[:, 65:89], T.PP[:, 79:80], None, OP.add), "aX2 PP4", "c5")
+        v("ts", (T.c5r[:, 15::16], T.aX[:, 97:121], T.PP[:, 79:80], None, OP.add), "aX2 PP4", "c5r")
         act(T.B[:, 2::4], T.DT[:, 0:48].indirect(T.lD[:, 0:24]), "DT lD", "B2", GC)
         v("tt", (T.B[:, 1::4], T.TB[:, 0:32].indirect(T.tt[:, 2:26]), T.S[:], OP.is_lt), "TBs tt Sa Sb", "B1", GC)
         v("tt", (T.B[:, 0::4], T.TB[:, 32:64].indirect(T.tt[:, 34:58]), T.S[:], OP.is_le), "TBp tt Sa Sb", "B0", GC)
         v("q", (T.qb[:], T.sb[:], T.B[:]), "B0 B1 B2 B3", "qb", 420)
-        for b, i in ((0, 1), (2, 0), (3, 7)):
-            cm(b, i, T.qb, T.sb, "qb", False, True)
+        for b, n, i in ((2, "A", 0), (0, "A", 1), (3, "B", 1)):
+            cm(b, n, i, T.qb, T.sb, "qb", False, True)
         for i, a in ((0, 34), (1, 2)):
             act(T.junk[:, C * i:C * i + C], T.OH[:].indirect(T.tt[:, a:a + 24]), "OH0 OH1 tt", "junk%d acc%d" % (i, i), GC,
                 accum_out=T.acc[:, i:i + 1])
@@ -277,39 +281,44 @@ def rank_program(g, core, T, topo):
         v("tr", (T.rt[:], T.rp[:]), "rp", "rt", 128)
         v("ts", (T.dL[:, 0::16], T.rt[:].indirect(T.lE[:, 4:6]), -1.0, None, OP.mult), "rt lT", "dL", 100)
         v("ts", (T.dR[:, 15::16], T.rt[:].indirect(T.lE[:, 6:8]), -1.0, None, OP.mult), "rt lT", "dR", 100)
-        v("scan", (T.GL[:, 1:C + 1], T.dL[:, 0:C], bank(6), 0.0, OP.add, OP.add), "dL #6", "GL", C)
-        v("scan", (T.GR[:, 1:C + 1], rev(T.dR), rbank(7), 0.0, OP.add, OP.add), "dR #7", "GR", C)
-        v("scan", (T.xx[:, 16:16 + C], bank(0), T.c5[:], -5000.0, OP.max, OP.add), "#0 c5", "xL", C)
-        v("scan", (T.xx[:, 528:528 + C], bank(2), T.c5[:], -5000.0, OP.max, OP.add), "#2 c5", "xR", C)
-        v("tt", (T.uu[:, 0:64], T.aX[:, 64:128], T.xx[:, 15::16], OP.subtract), "aX2 xL xR", "u", 128)
-        v("tt", (T.uu[:, 64:128], T.uu[:, 0:64], T.m[:], OP.mult), "u m", "um", 128)
-        v("ts", (T.lp[:, 1:65], T.uu[:, 64:128], 392.0, None, OP.add), "um", "lp")
+        v("scan", (T.GL[:, 2:C + 2], T.dL[:, 0:C], bank(6), 0.0, OP.add, OP.add), "dL #6", "GL", C)
+        v("scan", (T.GR[:, 2:C + 2], rev(T.dR), rbank(7), 0.0, OP.add, OP.add), "dR #7", "GR", C)
+        rL, rR = T.xx[:, 15:C:16], T.xx[:, C + 15::16]
+        v("scan", (T.xx[:, 0:C], bank(0), T.c5[:], -5000.0, OP.max, OP.add), "#0 c5", "xL", C)
+        v("scan", (T.xx[:, C:], bank(2), T.c5r[:], -5000.0, OP.max, OP.add), "#2 c5r", "xR", C)
+        v("ts", (T.lp[:, 0:24], rL, -1.0, -4000.0, OP.mult, OP.add), "xL", "lp0")
+        v("ts", (T.lp[:, 24:48], rR, -1.0, -4000.0, OP.mult, OP.add), "xR", "lp1")
         v("tt", (T.zt[:], bank(3), T.a2row[:], OP.add), "#3 a2row", "zt", C)
         act(T.z[:], T.zt[:], "zt", "z", C, f=AF.Relu)
-        act(T.GgL[:], T.GL[:].indirect(T.lp[:, 2:26]), "GL GL0 GL1 lp", "GgL", GC)
-        v("copy", (T.GgR[:], T.GR[:].indirect(T.lp[:, 34:58])), "GR GR0 GR1 lp zt", "GgR", GC)
-        v("scan", (T.mL[:], T.GgL[:], T.c4[:], 5000.0, OP.min, OP.add), "GgL c4", "mL", C)
+        act(T.GgL[:], T.GL[:, 0:C + 2].indirect(T.lp[:, 0:24]), "GL GL0 lp0", "GgL", GC)
+        act(T.GgR[:], T.GR[:, 0:C + 2].indirect(T.lp[:, 24:48]), "GR GR0 lp1", "GgR", GC)
         v("scan", (rev(T.mR), rev(T.GgR), rev(T.c3), 5000.0, OP.min, OP.add), "GgR c3", "mR", C)
         v("tt", (sm(0), T.CNT[:, 543:543 + C:16], T.CNT[:, 31:31 + C:16], OP.subtract), "CL CR", "sm0")
-        v("ts", (sm(1), T.uu[:, 1:25], 2.0, 785.0, OP.mult, OP.add), "u", "sm1")
-        v("ts", (sm(2), T.uu[:, 33:57], -2.0, -16.0, OP.mult, OP.add), "u", "sm2")
-        for i in (1, 2):
-            v("tt", (sm(i), sm(i), sm(0), OP.add), "sm%d sm0" % i, "sm%d" % i)
-            v("tt", (sm(i + 2), sm(i), T.mR[:, 0::16], OP.add), "sm%d mR" % i, "sm%d" % (i + 2))
-            v("tt", (sm(i + 4), sm(i + 2), T.mL[:, 15::16], OP.subtract), "sm%d mL" % (i + 2), "sm%d" % (i + 4))
-        v("copy", (T.oc16[:], T.sm[:, 120:168]), "sm5 sm6", "oc16")
+        v("tt", (sm(5), T.uu[:, 1:25], sm(0), OP.subtract), "mk sm0", "sm5")
+        v("tt", (sm(6), T.uu[:, 1:25], sm(5), OP.add), "mk sm5", "sm6")
+        v("tt", (sm(10), T.uu[:, 1:25], T.uu[:, 33:57], OP.add), "mk", "sm10")
+        v("ts", (sm(1), rL, 2.0, c15, OP.mult, OP.add), "xL c15", "sm1")
+        v("tt", (sm(8), sm(1), sm(6), OP.add), "sm1 sm6", "sm8")
+        v("tt", (sm(2), rL, rR, OP.add), "xL xR", "sm2")
+        v("tt", (sm(11), sm(2), sm(10), OP.add), "sm2 sm10", "sm11")
+        v("ts", (sm(3), sm(11), 2.0, 17771.0, OP.mult, OP.add), "sm11", "sm3")
+        v("tt", (T.c4[:, 15::16], sm(8), T.mR[:, 0::16], OP.subtract), "sm8 mR", "c4")
+        v("scan", (T.mL[:], T.GgL[:], T.c4[:], 5000.0, OP.min, OP.add), "GgL c4", "mL", C)
+        v("ts", (T.oc16[:, 0:24], T.mL[:, 15::16], -1.0, 5000.0, OP.mult, OP.add), "mL", "op16")
+        v("tt", (sm(4), sm(3), T.mL[:, 15::16], OP.subtract), "sm3 mL", "sm4")
+        v("copy", (T.oc16[:, 24:48], sm(4)), "sm4", "cl16")
         DB, OB = (0, 2, 6, 7), (1, 3, 4, 5)
         for b in range(4):
-            cm(DB[b], 8 + b, lq, ls, "qL%d lp" % t, True, True)
-            act(T.Dd[:, b::4], bank(DB[b]), "#%d oc16" % DB[b], "Dd%d" % b, C)
-        v("copy", (T.EW[:].indirect(T.oc16[:, 0:24]), T.z[:]), "oc16 z", "EW", 50 + SC * C)
-        v("copy", (T.EW[:].indirect(T.oc16[:, 24:48]), T.z[:]), "oc16 z", "EW", 50 + SC * C)
+            cm(DB[b], "E", b, lq, ls, "qL%d lp0 lp1" % t, True, True)
+            act(T.Dd[:, b::4], bank(DB[b]), "#%d op16" % DB[b], "Dd%d" % b, C)
+        v("copy", (T.EW[:].indirect(T.oc16[:, 0:24]), T.z[:]), "op16 z", "EW", 50 + SC * C)
+        v("copy", (T.EW[:].indirect(T.oc16[:, 24:48]), T.z[:]), "cl16 z", "EW", 50 + SC * C)
         for h in range(2):
             act(T.PH[:, C * h:C * h + C], T.EW[:, C * h:C * h + C], "EW", "PH%d" % h, C, f=AF.Sign, scale=-1.0, bias=0.5)
         v("scan", (T.Y[:, 0:C], T.PH[:, 0:C], T.EW[:, 0:C], 0.0, OP.mult, OP.subtract), "PH0 EW", "Y0", C)
         v("scan", (T.Y[:, C:], T.PH[:, C:], T.EW[:, C:], T.Y[:, C - 1:C], OP.mult, OP.subtract), "PH1 EW Y0", "Y1", C)
-        act(T.Yg[:, 192:], T.Y[:].indirect(T.oc16[:, 12:24]), "Y0 Y1 oc16", "Yg1", 350)
-        v("copy", (T.Yg[:, 0:192], T.Y[:].indirect(T.oc16[:, 0:12])), "Y0 Y1 oc16", "Yg0", 350)
+        act(T.Yg[:, 192:], T.Y[:].indirect(T.oc16[:, 12:24]), "Y0 Y1 op16", "Yg1", 330)
+        v("copy", (T.Yg[:, 0:192], T.Y[:].indirect(T.oc16[:, 0:12])), "Y0 Y1 op16", "Yg0", 330)
         v("scan", (T.dg[:], T.Yg[:], T.c5y[:], -5000.0, OP.max, OP.add), "Yg0 Yg1 c5y", "dg", C)
         act(sm(7), T.dg[:, 15::16], "dg", "sm7", 64, f=AF.Abs, bias=4000.0)
         v("ts", (T.at[:], sm(7), -0.5, None, OP.add), "sm7", "at")
@@ -318,20 +327,21 @@ def rank_program(g, core, T, topo):
         v("scan", (T.o4[:, H:], T.O[:, H:], T.c6[:, H:], -5000.0, OP.max, OP.add), "O c6", "o4b", K)
         v("ts", (ob, T.o4[:, H + 3::4], 4.0, l4c, OP.mult, OP.add), "o4b l4c", "ob%d" % t)
         send(ll, ob, "al%d" % t, "ob%d" % t, "sent2")
-        landed("al%d" % t, n_in, "sent2", "ll%d" % t, 2200.0)
+        landed("al%d" % t, n_in, "sent2", "ll%d" % t, 2800.0)
         if t == R - 1:
             dma("y", "dol", T.ol[:], T.O[0:128:16, :], "O", "")
         v("scan", (T.o4[:, 0:H], T.O[:, 0:H], T.c6[:, 0:H], -5000.0, OP.max, OP.add), "O c6", "o4a", H)
         v("ts", (T.oo[:], T.o4[:, 3:H:4], 4.0, l4c, OP.mult, OP.add), "o4a l4c", "oo", 72)
-        act(T.Z[:, 960:], T.X[:].indirect(T.oo[:, 36:72]), XA + " Xb oo", "Z2", 950)
-        v("copy", (T.Z[:, 384:960], T.X[:].indirect(T.oo[:, 0:36])), XA + " Xb oo", "Z1", 950)
+        act(T.Z[:, 960:], T.X[:].indirect(T.oo[:, 36:72]), XA + " Xb oo", "Z2", 900)
+        v("copy", (T.Z[:, 384:960], T.X[:].indirect(T.oo[:, 0:36])), XA + " Xb oo", "Z1", 900)
         act(T.Z[:, 0:384], T.Dd[:].indirect(ll), keys("Dd", 4) + " ll%d" % t, "Z0", GC)
         v("q", (T.qz[:, K:], T.sz[:, K:], T.Z[:, 4 * K:]), "Z1 Z2", "qz", 320)
         wv = lambda b: (T.wq[:, 128 * b:128 * b + 128], T.wsp[:, 128 * b:128 * b + 128])
-        v("ts", (T.Z64[:, 4 * K:], T.Z[:, 4 * K:], 64.0, None, OP.mult), "Z1 Z2", "Z64a", 2 * H)
+        v("ts", (T.Z64[:, 384:1152], T.Z[:, 384:1152], 64.0, None, OP.mult), "Z1 Z2", "Z64a", 384)
+        act(T.Z64[:, 1152:], T.Z[:, 1152:], "Z2", "Z64c", 384, scale=64.0)
         for b in range(4):
             mm(OB[b], H, *wv(b), T.qz[:, K:], T.sz[:, K:], True, True, "wq wsp qz")
-            v("tt", (T.X64[:, 4 * K + b::4], bank(OB[b], H), T.Z64[:, 4 * K + b::4], OP.add), "#%d Z64a" % OB[b], "X64a%d" % b, H)
+            v("tt", (T.X64[:, 4 * K + b::4], bank(OB[b], H), T.Z64[:, 4 * K + b::4], OP.add), "#%d Z64a Z64c" % OB[b], "X64a%d" % b, H)
             act(T.X[:, 4 * K + b::4], T.X64[:, 4 * K + b::4], "X64a%d" % b, "Xa%d" % b, H, scale=0.015625)
         v("q", (T.qzb[:], T.szb[:], T.Z[:, 0:512]), "Z0 Z1", "qzb", 150)
         v("ts", (T.Z64[:, 0:4 * K], T.Z[:, 0:4 * K], 64.0, None, OP.mult), "Z0", "Z64b", 2 * K)
@@ -350,31 +360,49 @@ def rank_program(g, core, T, topo):
         v("copy", (T.ys[:, a:b], bank(bk, b - a)), "#%d" % bk, "ys" + p, b - a)
         dma("s", "dy", T.y[:, a:b], T.ys[:, a:b], "ys" + p, "")
     for k in range(4):
-        dma("y", "dos", T.osc[4 * k:4 * k + 4, :], T.sx3[32 * k:32 * k + 4, :], "qx%da qx%db" % (R, R), "")
+        dma("ys"[k // 3], "dos", T.osc[4 * k:4 * k + 4, :], T.sx3[32 * k:32 * k + 4, :], "qx%da qx%db" % (R, R), "")
 
     n = len(ops)
-    ahead, users, left = [0.0] * n, [[] for _ in ops], [len(o["deps"]) for o in ops]
+    ahead, users = [0.0] * n, [[] for _ in ops]
     for i, o in enumerate(ops):
         for d in o["deps"]:
             users[d].append(i)
     for i in range(n - 1, -1, -1):
         ahead[i] = ops[i]["busy"] + ops[i]["lag"] + max([ahead[j] for j in users[i]] + [0.0])
-    ready, free, order = {i: 0.0 for i in range(n) if not left[i]}, {q: 0.0 for q in "vstgyx"}, []
-    while ready:
-        at = {i: max(tm, free[ops[i]["q"]]) for i, tm in ready.items()}
-        i0 = min(at, key=lambda i: (at[i], -ahead[i]))
-        mine = [i for i in at if ops[i]["q"] == ops[i0]["q"]]
-        best = max([i for i in mine if at[i] <= at[i0] + 300.0], key=lambda i: ahead[i])
-        fill = [i for i in mine if at[i] < at[best] and at[i] + ops[i]["busy"] <= at[best] + 30.0]
-        i = max(fill, key=lambda i: ahead[i]) if fill else best
-        o = ops[i]
-        del ready[i]
-        order.append(i)
-        free[o["q"]] = o["end"] = at[i] + o["busy"]
-        for j in users[i]:
-            left[j] -= 1
-            if not left[j]:
-                ready[j] = max(ops[d]["end"] + (ops[d]["lag"] if s else 0.0) for d, s in ops[j]["deps"].items())
+
+    def lay_out(bias):
+        left = [len(o["deps"]) for o in ops]
+        ready, free, order, end = {i: 0.0 for i in range(n) if not left[i]}, {q: 0.0 for q in "vstgyx"}, [], [0.0] * n
+        while ready:
+            at = {i: max(tm, free[ops[i]["q"]]) for i, tm in ready.items()}
+            i0 = min(at, key=lambda i: (at[i], -ahead[i]))
+            mine = [i for i in at if ops[i]["q"] == ops[i0]["q"]]
+            best = max([i for i in mine if at[i] <= at[i0] + 200.0], key=lambda i: ahead[i] + bias[i])
+            fill = [i for i in mine if at[i] < at[best] and at[i] + ops[i]["busy"] <= at[best] + 60.0]
+            i = max(fill, key=lambda i: ahead[i] + bias[i]) if fill else best
+            del ready[i]
+            order.append(i)
+            free[ops[i]["q"]] = end[i] = at[i] + ops[i]["busy"]
+            for j in users[i]:
+                left[j] -= 1
+                if not left[j]:
+                    ready[j] = max(end[d] + (ops[d]["lag"] if w else 0.0) for d, w in ops[j]["deps"].items())
+        return max(end[i] + ops[i]["lag"] for i in range(n)), order
+
+    if n not in ORDER:
+        seed, bias = 12345, [0.0] * n
+        span, order = lay_out(bias)
+        for _ in range(TRIES):
+            other = list(bias)
+            for _k in range(8):
+                seed = (seed * 1103515245 + 12345) % 2147483648
+                i = (seed >> 8) % n
+                seed = (seed * 1103515245 + 12345) % 2147483648
+                other[i] = ((seed >> 8) % 3001) - 1500.0
+            a, b = lay_out(other)
+            if a <= span:
+                span, order, bias = a, b, other
+        ORDER[n] = order
     total, known = {}, {q: {} for q in QS}
 
     def wait(q, sem, val):
@@ -382,7 +410,7 @@ def rank_program(g, core, T, topo):
             QS[q].wait_ge(T.sem[sem], val)
             known[q][sem] = val
 
-    for i in order:
+    for i in ORDER[n]:
         o = ops[i]
         if o["emit"]:
             need = {}

@@ -2,29 +2,31 @@ from concourse.mybir import dt, AluOpType as OP, ActivationFunctionType as AF
 
 C, K, R, N = 384, 96, 3, 4
 NB, H = C // 16, C - K
-F32, BF, I32, U16, Q4, U8 = "float32", "bfloat16", "int32", "uint16", "float8_e4m3fn_x4", "uint8"
-BIG = 1e28
+F32, BF, F16, I32, U16, Q4, U8 = "float32", "bfloat16", "float16", "int32", "uint16", "float8_e4m3fn_x4", "uint8"
+BIG, KX, EPS = 1e28, 2125.0, 2.0 ** -12
+UU, TB, VV = 0, 400, 432
 
 SCRATCH = {"ps": ("psum", [128, 4096], F32)}
 for _d, _l in (
-        (BF, "X:1536 X64:1536 Z:1536 Z64:1536 Dd:1536 ut:512 vt:512 tA:2048 tB:1024 tE:2048 A:1536 B:1536 one:608 BD:128 ID:128 "
-             "seg:384 CNT:1024 cov:608 run:608 junk:768"),
-        (Q4, "qu:128 qv:128 qp:256 wq:512 qz:384 qzb:128 kqA:512 kqB:256 kqE:512 qa:384 qb:384 qx0:384 qx1:384 qx2:384 qx3:384 lq0:384 lq1:384 lq2:384"),
-        (U8, "su:128 sv:128 sp:256 wsp:512 sz:384 szb:128 ksA:512 ksB:256 ksE:512 sa:384 sb:384 sx0:384 sx1:384 sx2:384 sx3:384 ls0:384 ls1:384 ls2:384"),
-        (I32, "cI:64 WI:16"),
-        (U16, "rep:24 upk:24 lBM:38 lTH:20 lE:8 tt:66 lD:24 lp:48 oc16:48 at:24 oo:72 ob:72 ll:72"),
-        (F32, "cF:16 dm:32 tm:32 PP:96 c1:384 c2:384 c3:384 c4:384 c5:384 c5y:384 c5r:384 c6:384 arow:384 a2row:384 aW:48 aX:128 J:160 ER:128 ERd:128 "
-              "DT:96 OH:32 base:64 cc:64 S:384 V:384 U:384 TB:96 BMx:608 m:64 E:128 TD:192 acc:2 rp:128 rt:128 dL:512 dR:512 GL:400 GR:400 "
-              "GgL:384 GgR:384 mL:384 mR:384 xx:768 uu:128 sm:288 zt:384 z:384 EW:768 PH:768 Y:768 Yg:384 dg:384 O:384 o4:384 ys:384")):
+        (BF, "X:1536 X64:1536 Z:1536 Z64:1536 Dd:1536 ut:512 vt:512 tW:512 tE:2048 A:1152 B:768 one:512 t32:608 BD:128 seg:384 "
+             "CNT:768 cov:608 run:608 junk:768 FT:16 FR:768 GL:400 GR:400 Gg:768 OH:400 c1:384 c2:384 c3:384 c6:384 O:384 arow:384 PH:768"),
+        (F16, "c4:384 mL:384 mR:384 DD:768 o4:384"),
+        (Q4, "qu:128 qv:128 qp:256 wq:512 qz:384 qzb:128 kqW:128 kqE:512 qa:288 qb:192 qx0:384 qx1:384 qx2:384 qx3:384 lq0:384 lq1:384 lq2:384"),
+        (U8, "su:128 sv:128 sp:256 wsp:512 sz:384 szb:128 ksW:128 ksE:512 sa:288 sb:192 sx0:384 sx1:384 sx2:384 sx3:384 ls0:384 ls1:384 ls2:384"),
+        (I32, "cI:64 WI:32 HI:64"),
+        (U16, "rep:24 upk:16 lBM:40 lTH:20 lE:6 ML:48 ix:48 lp:48 zi:24 oc16:48 at:24 oo:72 ob:72 ll:72"),
+        (F32, "cF:16 dm:32 tm:32 PP:96 c5:384 cx:192 aW:48 J:160 ER:80 ERd:80 base:48 cc:48 S:384 UV:832 BMx:608 "
+              "m:48 mb:48 corr:48 E:48 P2:48 acc:2 rp:64 rt:64 xx:192 fr:96 sm:240 ID:768 z:384 EW:768 Y:768 Yg:384 dg:384 O32:384 ys:384")):
     for _e in _l.split():
         _n, _w = _e.split(":")
         SCRATCH[_n] = ("sbuf", [128, int(_w)], _d)
 
-SEMAPHORES = ["v", "s", "t", "g", "dx", "du", "dv", "dwc", "dws", "dkA", "dkB", "dkE", "dy", "dol", "doc", "dos", "loc"] + \
+SEMAPHORES = ["v", "s", "t", "g", "dxa", "dxb", "du", "dv", "dwc", "dws", "dy", "dol", "doc", "dos", "loc"] + \
              ["aq%d" % t for t in range(R)] + ["al%d" % t for t in range(R)]
 
 GA, SC, LAG = 1.45, 3.2, 200.0
-ORDER, TRIES = {}, 4000
+ORDER, TRIES = {}, 3000
+INORDER = True
 
 
 def rank_program(g, core, T, topo):
@@ -41,13 +43,14 @@ def rank_program(g, core, T, topo):
     def add(q, emit, r, w, busy, lag, sem, inc, acc=False):
         r, w = r.split(), w.split()
         deps = {}
+        own = lambda i: INORDER and ops[i]["q"] == q and ops[i]["sem"] == q == sem
         for k in r + w:
             if k in wrote:
                 deps[wrote[k]] = deps.get(wrote[k], False) or not (acc and k in w)
         for k in w + [k for k in r if k[0] == "#"]:
             for i in read.get(k, []):
                 if k in w or ops[i]["q"] != q:
-                    deps[i] = True
+                    deps[i] = deps.get(i, False) or not own(i)
         ops.append({"q": q, "emit": emit, "deps": deps, "busy": busy, "lag": lag, "sem": sem, "inc": inc})
         for k in r:
             read.setdefault(k, []).append(len(ops) - 1)
@@ -61,10 +64,10 @@ def rank_program(g, core, T, topo):
                 "scan": lambda: e.tensor_tensor_scan(*args), "set": lambda: e.memset(*args), "q": lambda: e.quantize_mx(*args),
                 "tr": lambda: e.transpose(*args), "act": lambda: e.activation(*args, **kw), "mm": lambda: e.matmul_mx(*args),
                 "iota": lambda: e.iota(*args, **kw), "sel": lambda: e.affine_select(*args)}[name]
-        add(q, lambda: call().then_inc(T.sem[q], 1), r, w, max(c, 64) * 0.95, LAG, q, 1, acc)
+        add(q, lambda: call().then_inc(T.sem[q], 1), r, w, max(c, 64) * 0.9, LAG, q, 1, acc)
 
     def dma(q, sem, out, in_, r, w):
-        add(q, lambda: QS[q].dma_start(out, in_).then_inc(T.sem[sem], 16), r, w, 100.0, 2200.0, sem, 16)
+        add(q, lambda: QS[q].dma_start(out, in_).then_inc(T.sem[sem], 16), r, w, 100.0, 2600.0, sem, 16)
 
     def send(out, in_, sem, r, w):
         add("g", lambda: g.remote_dma(out, in_, T.sem[sem], T.sem.loc, pid, rid, mask), r, w, 300.0, 0.0, "loc", n_out)
@@ -80,9 +83,12 @@ def rank_program(g, core, T, topo):
 
     def iota(out, pat, base, w, c=32, whole=False):
         if whole:
-            op("g", "iota", (out, pat, base, 0), "", w, 130 + 2 * c)
+            op("g", "iota", (out, pat, base, 0), "", w, 157 + 2 * c)
         else:
-            op("g", "iota", (out, pat, base, 0), "", w, 130 + 2 * c, allow_small_or_imprecise_dtypes=True)
+            op("g", "iota", (out, pat, base, 0), "", w, 157 + 2 * c, allow_small_or_imprecise_dtypes=True)
+
+    def sel(out, in_, pat, cmp, base, cm, r, w, c):
+        op("g", "sel", (out, in_, pat, cmp, 0.0, base, cm), r, w, 205 + 2 * c)
 
     def bank(b, n=C, a=0):
         return T.ps[:, 512 * b + a:512 * b + n]
@@ -96,95 +102,97 @@ def rank_program(g, core, T, topo):
     def mm(b, n, lq, ls, rq, rs, start, stop, r):
         op("t", "mm", (bank(b, n), lq, ls, rq, rs, start, stop), r, "#%d" % b, 0.7 * (n + 16), acc=not start)
 
-    def cm(b, n, i, rq, rs, key, start, stop):
-        mm(b, C, T["kq" + n][:, 128 * i:128 * i + 128], T["ks" + n][:, 128 * i:128 * i + 128], rq[:], rs[:], start, stop, "k%s %s" % (n, key))
-
-    lane, l4c, lq4, e16, l3, c15 = [T.cF[:, i:i + 1] for i in range(6)]
-    l0, l15 = T.OH[:, 0:1], T.OH[:, 15:16]
+    gv = lambda n: 60 + GA * n
+    gs = lambda n: 78 + GA * n
+    sv = lambda n: 60 + SC * n
+    qc = lambda n: 15 + 1.06 * n
+    lane, l4c, lq4, e16, kL, kR, k0, k1, lane2 = [T.cF[:, i:i + 1] for i in range(9)]
     sm = lambda i: T.sm[:, 24 * i:24 * i + 24]
     keys = lambda s, n: " ".join(s + str(i) for i in range(n))
     XA = keys("Xa", 4)
-    GC = 50 + GA * C
+    wU, wB, wV = T.UV[:, UU:UU + 400], T.UV[:, TB:TB + 32], T.UV[:, VV:VV + 400]
 
-    dma("y", "dx", T.X[:], T.x[:], "", XA + " Xb")
+    dma("y", "dxa", T.X[:, 512:], T.x[:, 512:], "", "Xa0 Xa1")
     dma("s", "du", T.ut[:], T.u[:], "", "ut")
-    dma("y", "dwc", T.wq[:].bitcast(dt.uint8), T.wc[:], "", "wq")
-    dma("y", "dws", T.wsp[:], T.ws[:], "", "wsp")
-    dma("y", "dv", T.vt[:], T.v[:], "", "vt")
+    dma("y", "dxb", T.X[:, 0:512], T.x[:, 0:512], "", "Xa2 Xa3 Xb")
+    dma("y", "dwc", T.wq[:].bitcast(dt.uint8), T.wc[:], "Xb", "wq")
+    dma("y", "dws", T.wsp[:], T.ws[:], "Xb", "wsp")
+    dma("y", "dv", T.vt[:], T.v[:], "Xb", "vt")
 
-    op("g", "iota", (T.cI[:, 0:1], [[0, 1]], 0, 1), "", "cI0", 130)
-    iota(T.cI[:, 16:32], [[1, 2], [16, 8]], 0, "cIu", whole=True)
-    iota(T.cI[:, 32:40], [[1, 4], [0, 2]], 0, "cIr", whole=True)
-    iota(T.tm[:, 0:16], [[1, 16]], 0, "tm0")
-    iota(T.tm[:, 16:32], [[0, 4], [1, 4]], 0, "tm1")
-    iota(T.aW[:, 0:24], [[16, NB]], 0, "aW0")
-    iota(T.J[:, 0:20], [[16, 20]], 0, "J0")
-    for name, w, parts in (("base", 64, ((1, 24, 1, 100), (33, 24, -1, 123))),
-                           ("ER", 128, ((1, 12, 25, 328), (13, 12, -24, 591), (33, 12, 24, 23), (45, 12, -25, 299),
-                                        (64, 9, -1, 40), (73, 15, -1, 15), (96, 15, 1, 65), (111, 9, 1, 96)))):
-        iota(T[name][:], [[0, w]], 0, keys(name, 8), w)
-        for i, (a, n, st, b0) in enumerate(parts):
-            iota(T[name][:, a:a + n], [[st, n]], b0, name + str(i))
-    iota(T.DT[:, 48:96], [[1, 48]], 0, "DT1", 48)
-    iota(T.a2row[:], [[2, C]], -1024 - 16 * (NB - 1), "a2row", C)
-    iota(T.arow[:], [[1, C]], 0, "arow", C)
-    iota(T.one[:, 0:C], [[0, C]], 1, "one", C)
-    iota(T.one[:, C:], [[0, 608 - C]], 1, "one1", 224)
-    op("g", "sel", (T.junk[:, 0:128], T.one[:, 0:128], [[-16, 8], [0, 16]], OP.is_ge, 0.0, 0, 1), "one", "junk0", 420)
-    op("g", "sel", (T.BD[:], T.junk[:, 0:128], [[16, 8], [0, 16]], OP.is_ge, 0.0, 15, -1), "junk0", "BD", 420)
-    op("g", "sel", (T.ID[:], T.one[:, 0:128], [[-1, 128]], OP.is_equal, 0.0, 0, 1), "one", "ID", 420)
-    op("g", "sel", (T.seg[:], T.one[:, 0:C], [[0, NB], [1, 16]], OP.not_equal, 0.0, 0, 0), "one", "seg", 170 + 2 * C)
-    op("g", "sel", (T.dR[:, 0:C], T.one[:, 0:C], [[0, NB], [1, 16]], OP.is_equal, 0.0, 0, 0), "one", "dR", 170 + 2 * C)
-    iota(T.dL[:, 0:C], [[0, C]], 0, "dL", C)
-    iota(T.cc[:], [[-1, 2], [0, 32]], 1, "cc", 64)
-    iota(T.CNT[:, 15::16], [[0, 64]], 5, "CL CR", 64)
-    iota(T.aX[:, 0:64], [[0, 64]], 0, "aX0 aX1", 64)
-    for n in ("GL", "GR"):
-        iota(T[n][:, 0:2], [[-900, 2]], 900, n + "0")
-    v("set", (T.tA[:, 0:512], 0.0), "", "tA0", 256)
-    for n, a, b in (("A", 1, 4), ("B", 0, 2), ("E", 0, 4)):
-        for i in range(a, b):
-            dma("y", "dk" + n, T["t" + n][:, 512 * i:512 * i + 512], T.tA[:, 0:512], "tA0", "z%s%d" % (n, i))
+    op("g", "iota", (T.cI[:, 0:1], [[0, 1]], 0, 1), "", "cI0", 157)
+    iota(T.cI[:, 16:32], [[1, 2], [16, 8]], 0, "cIu", 16, whole=True)
+    iota(T.tm[:, 0:16], [[1, 16]], 0, "tm0", 16)
+    iota(T.tm[:, 16:32], [[0, 4], [1, 4]], 0, "tm1", 16)
+    iota(T.aW[:, 0:24], [[16, NB]], 0, "aW0", 24)
+    iota(T.J[:, 0:20], [[16, 20]], 0, "J0", 20)
+    iota(T.FT[:], [[1, 16]], 0, "FT", 16)
+    iota(T.cc[:], [[-1, 2], [0, NB]], 1, "cc", 48)
+    iota(T.base[:, 0:24], [[32, NB]], 32, "base0", 24)
+    iota(T.base[:, 24:48], [[-32, NB]], 32 * NB, "base1", 24)
+    for i, (a, pat, b0) in enumerate(((0, [[25, 12]], 328), (12, [[-24, 12]], 591), (24, [[24, 12]], 23), (36, [[-25, 12]], 299),
+                                      (48, [[32, 2], [1, 12]], 0), (72, [[0, 8]], 0))):
+        iota(T.ER[:, a:(80 if a == 72 else 72 if a == 48 else a + 12)], pat, b0, "ER%d" % i, 12)
+    iota(T.HI[:, 0:25], [[-1, 25]], NB, "HI0 HI1", 25, whole=True)
+    iota(T.OH[:], [[0, 400]], 0, "OH", 400)
+    iota(T.ID[:], [[-1, 768]], 0, "ID", 768)
+    iota(T.arow[:], [[1, C]], -192, "arow", C)
+    iota(T.GL[:, 0:2], [[448, 2]], -256, "GL0", 2)
+    iota(T.GR[:, 0:2], [[448, 2]], -256, "GR0", 2)
+    v("set", (T.one[:], 1.0), "", "one", 256)
+    v("set", (T.t32[:], 32.0), "", "t32", 304)
+    v("set", (T.tW[:], 0.0), "", "zW", 256)
+    v("set", (T.UV[:, 0:16], BIG), "", "pad0")
+    v("set", (T.UV[:, TB:VV + 16], BIG), "", "TBm pad1")
+    v("set", (T.ID[:, 0:1], EPS), "", "ID")
+    v("ts", (T.DD[:, 0:C], T.one[:, 0:C], 0.0, None, OP.mult), "one", "DD", 192)
+    v("ts", (T.DD[:, C:], T.one[:, 0:C], 0.0, None, OP.mult), "one", "DD1", 192)
+    sel(T.seg[:], T.one[:, 0:C], [[0, NB], [1, 16]], OP.not_equal, 0, 0, "one", "seg", C)
+    sel(T.junk[:, 0:128], T.one[:, 0:128], [[-16, 8], [0, 16]], OP.is_ge, 0, 1, "one", "junk0", 128)
+    sel(T.BD[:], T.junk[:, 0:128], [[16, 8], [0, 16]], OP.is_ge, 15, -1, "junk0", "BD", 128)
     for col, key, n in ((lane, "lane", 15), (e16, "e16", 16)):
         v("ts", (T.cI[:, n - 14:n - 13], T.cI[:, 0:1], n, None, OP.bitwise_and), "cI0", "i" + key)
         v("copy", (col, T.cI[:, n - 14:n - 13]), "i" + key, key)
     v("ts", (T.cI[:, 3:4], T.cI[:, 1:2], 2, None, OP.arith_shift_right), "ilane", "cI3")
     v("ts", (T.cI[:, 4:5], T.cI[:, 1:2], 3, None, OP.bitwise_and), "ilane", "cI4")
     v("copy", (lq4, T.cI[:, 3:4]), "cI3", "lq4")
-    v("ts", (l4c, T.cI[:, 4:5], 16000.0, None, OP.add), "cI4", "l4c")
-    v("copy", (T.upk[:], T.cI[:, 16:40]), "cIu cIr", "upk")
+    v("ts", (l4c, T.cI[:, 4:5], 4.0 * (512 + 192), None, OP.add), "cI4", "l4c")
+    v("copy", (T.upk[:], T.cI[:, 16:32]), "cIu", "upk")
     v("ts", (T.rep[:], T.aW[:, 0:24], 0.0, lane, OP.mult, OP.add), "aW0 lane", "rep")
     v("ts", (T.dm[:, 0:16], T.tm[:, 0:16], lane, None, OP.subtract), "tm0 lane", "dm0")
     v("ts", (T.dm[:, 16:32], T.tm[:, 16:32], lq4, None, OP.subtract), "tm1 lq4", "dm1")
-    for i, col, a, b in ((0, 15, -10 * BIG, BIG), (1, 0, -10 * BIG, BIG), (2, 0, -1000.0, 3000.0), (3, 15, -1000.0, 0.0)):
-        v("ts", (T.PP[:, 16 * i:16 * i + 16], T.dm[:, 0:16], 0.0, a, OP.is_equal, OP.mult), "dm0", "PP%d" % i)
+    for i, col in ((0, 15), (1, 0)):
+        v("ts", (T.PP[:, 16 * i:16 * i + 16], T.dm[:, 0:16], 0.0, -10 * BIG, OP.is_equal, OP.mult), "dm0", "PP%d" % i)
         one = T.PP[:, 16 * i + col:16 * i + col + 1]
-        if b:
-            v("ts", (one, one, b, None, OP.add), "PP%d" % i, "PP%d" % i)
-    v("ts", (c15, T.PP[:, 63:64], 14001.0, None, OP.add), "PP3", "c15")
-    v("ts", (T.PP[:, 64:96], T.dm[:], 0.0, 2000.0, OP.is_equal, OP.mult), "dm0 dm1", "PP4 PP5")
-    v("ts", (T.tm[:], T.dm[:], -1.0, -4000.0, OP.is_equal, OP.mult), "dm0 dm1", "tm0 tm1")
-    v("tt", (T.PP[:, 64:96], T.PP[:, 64:96], T.tm[:], OP.add), "PP4 PP5 tm0 tm1", "PP4 PP5")
-    v("ts", (T.PP[:, 79:96:4], T.PP[:, 79:96:4], -6000.0, None, OP.add), "PP4 PP5", "PP4 PP5")
-    for name, i in (("c1", 0), ("c2", 1), ("c3", 2), ("c4", 3), ("c5", 4), ("c5y", 4), ("c5r", 4), ("c6", 5)):
-        act(T[name][:], T.PP[:, 16 * i:16 * i + 16].indirect(T.rep[:, 0:24]), "PP%d rep" % i, name, GC)
+        v("ts", (one, one, BIG, None, OP.add), "PP%d" % i, "PP%d" % i)
+    v("ts", (T.PP[:, 32:48], T.dm[:, 0:16], 0.0, 512.0, OP.is_equal, OP.mult), "dm0", "PP2")
+    v("ts", (T.PP[:, 32:33], T.PP[:, 32:33], T.PP[:, 47:48], -1024.0, OP.subtract, OP.add), "PP2", "PP2")
+    v("ts", (T.PP[:, 64:96], T.dm[:], 0.0, 512.0, OP.is_equal, OP.mult), "dm0 dm1", "PP4")
+    v("ts", (T.tm[:], T.dm[:], -1.0, -1024.0, OP.is_equal, OP.mult), "dm0 dm1", "tm0 tm1")
+    v("tt", (T.PP[:, 64:96], T.PP[:, 64:96], T.tm[:], OP.add), "PP4 tm0 tm1", "PP4")
+    v("ts", (T.PP[:, 79:96:4], T.PP[:, 79:96:4], -1024.0, None, OP.add), "PP4", "PP4")
+    for name, i, key, n, sc in (("c1", 0, "PP0", C, 1.0), ("c2", 1, "PP1", C, 1.0), ("c3", 2, "PP2", C, 1.0), ("c5", 4, "PP4", C, 4.0),
+                                ("c6", 5, "PP4", C, 1.0), ("cx", 5, "PP4", 192, -1.0)):
+        act(T[name][:], T.PP[:, 16 * i:16 * i + 16].indirect(T.rep[:, 0:n // 16]), key + " rep", name + (" cx1" if name == "cx" else ""), gs(n), scale=sc)
+    v("copy", (T.c4[:], T.c3[:]), "c3", "c4", 192)
+    v("ts", (T.c4[:, 0::16], T.c3[:, 0::16], -512.0, 512.0, OP.is_equal, OP.mult), "c3", "c4")
+    v("ts", (k0, T.PP[:, 95:96], -1.0, KX - 512.0 + 30.0, OP.mult, OP.add), "PP4", "k0")
+    v("ts", (k1, T.PP[:, 95:96], -1.0, KX - 512.0 - 2.0, OP.mult, OP.add), "PP4", "k1")
+    v("ts", (kL, lane, -2.0, k0, OP.mult, OP.add), "lane k0", "kL")
+    v("ts", (kR, lane, 2.0, k1, OP.mult, OP.add), "lane k1", "kR")
+    v("scan", (T.ERd[:], T.ER[:], T.c5[:, 0:80], -5000.0, OP.max, OP.add), keys("ER", 6) + " c5", "ERd", 80)
+    v("ts", (T.lE[:, 0:3], T.ERd[:, 15:48:16], 2048.0, None, OP.add), "ERd", "lE")
+    v("ts", (T.lE[:, 4:6], T.ERd[:, 63::16], 2048.0, e16, OP.add, OP.add), "ERd e16", "lT")
     v("ts", (T.aW[:, 24:48], T.aW[:, 0:24], lane, 0.5, OP.add, OP.add), "aW0 lane", "aW1")
-    v("tt", (T.c5y[:, 15::16], T.c5y[:, 15::16], T.aW[:, 24:48], OP.add), "c5y aW1", "c5y")
-    v("ts", (T.aX[:, 1:25], T.aW[:, 24:48], -999.5, None, OP.add), "aW1", "aX0")
-    v("ts", (T.aX[:, 33:57], T.aW[:, 24:48], -1.0, C - 998.5, OP.mult, OP.add), "aW1", "aX1")
-    v("scan", (T.ERd[:], T.ER[:], T.c5[:, 0:128], -5000.0, OP.max, OP.add), keys("ER", 8) + " c5", "ERd", 128)
-    v("ts", (T.lE[:, 0:4], T.ERd[:, 15:64:16], 4000.0, None, OP.add), "ERd", "lE")
-    v("ts", (T.lE[:, 4:8], T.ERd[:, 79::16], 4000.0, e16, OP.add, OP.add), "ERd e16", "lT")
-    v("ts", (T.OH[:, 0:16], T.dm[:, 0:16], 0.0, None, OP.is_equal), "dm0", "OH0")
-    v("ts", (T.OH[:, 16:32], T.dm[:, 0:16], 0.0, 512.0, OP.is_equal, OP.mult), "dm0", "OH1")
-    v("set", (T.TB[:], BIG), "", "TBs TBp TBm", 96)
-    v("set", (T.A[:, 3::4], 0.0), "", "A3", 192)
-    v("set", (T.B[:, 3::4], 0.0), "", "B3", 192)
+    v("tt", (T.c5[:, 15::16], T.c5[:, 15::16], T.aW[:, 24:48], OP.add), "c5 aW1", "c5")
+    v("ts", (lane2, lane, 2.0, None, OP.mult), "lane", "lane2")
+    v("ts", (T.sm[:, 0:25], T.HI[:, 0:25], lane2, 0.0, OP.subtract, OP.is_equal), "HI0 lane2", "sm0 sm1")
+    v("ts", (T.sm[:, 48:73], T.HI[:, 0:25], lane2, 1.0, OP.subtract, OP.is_equal), "HI0 lane2", "sm2 sm3")
+    v("ts", (T.sm[:, 96:121], T.sm[:, 48:73], 512.0, None, OP.mult), "sm2 sm3", "sm4 sm5")
+    v("tt", (T.OH[:, 15::16], T.sm[:, 0:25], T.sm[:, 96:121], OP.add), "sm0 sm1 sm4 sm5 OH", "OH")
     Jc = lambda i: T.J[:, 20 * i:20 * i + 20]
     Ji = T.cI[:, 40:60]
     v("ts", (Jc(1), Jc(0), lane, None, OP.add), "J0 lane", "J1")
-    v("ts", (Jc(2), Jc(1), -12.0, 0.04, OP.add, OP.mult), "J1", "J2")
-    v("copy", (Ji, Jc(2)), "J2", "Ji")
+    v("ts", (Ji, Jc(1), -12.0, 0.04, OP.add, OP.mult), "J1", "Ji")
     v("ts", (Jc(2), Ji, -25.0, None, OP.mult), "Ji", "J2")
     v("ts", (Jc(3), Ji, -1.0, 24.0, OP.mult, OP.add), "Ji", "J3")
     v("ts", (Jc(4), Ji, 1.0, None, OP.add), "Ji", "J4")
@@ -193,29 +201,23 @@ def rank_program(g, core, T, topo):
     v("tt", (Jc(7), Jc(6), Jc(3), OP.mult), "J6 J3", "J7")
     v("tt", (Jc(5), Jc(5), Jc(7), OP.subtract), "J5 J7", "J5")
     v("tt", (Jc(4), Jc(4), Jc(7), OP.max), "J4 J7", "J4")
-    v("copy", (T.lTH[:], Jc(4)), "J4", "lTH")
-    v("ts", (T.lBM[:, 0:19], T.J[:, 100:119], -1.0, 25.0, OP.mult, OP.add), "J5", "lBM0")
-    v("copy", (T.lBM[:, 19:38], T.J[:, 100:119]), "J5", "lBM1")
-    v("ts", (l3, lane, -3.0, None, OP.mult), "lane", "l3")
-    v("ts", (T.DT[:, 48:96], T.DT[:, 48:96], l3, 0.0, OP.add, OP.max), "DT1 l3", "DT1")
-    v("ts", (T.DT[:, 0:48], T.DT[:, 48:96], 3.0, None, OP.min), "DT1", "DT")
-    zA, zB, zE = "zA1 zA2 zA3", "zB0 zB1", keys("zE", 4)
-    for n, zs, items in (("A", " ".join((zA, zB, zE)), [(0, 0, 1.0, "BD"), (1, 1, 1.0, "BD"), (2, 0, 1.0, "BD"),
-                                                        (2, 1, -1.0, "BD"), (2, 2, 64.0, "BD"), (3, 0, l15, "BD OH0")]),
-                         ("B", zB, [(0, 1, l0, "BD OH0"), (1, 0, 1.0, "BD"), (1, 1, -1.0, "BD"), (1, 2, 16.0, "BD")]),
-                         ("E", zE, [(b, b, 1.0, "ID") for b in range(4)])):
-        for j, (i, s, sc, r) in enumerate(items):
-            act(T["t" + n][:, 512 * i + s:512 * i + 512:4], T[r[0:2]][:], r + " " + zs, "t%s%d" % (n, j), 128, f=AF.Identity, scale=sc)
-        v("q", (T["kq" + n][:], T["ks" + n][:], T["t" + n][:]), keys("t" + n, len(items)), "k" + n, 280 if n == "B" else 550)
+    v("ts", (T.lTH[:], Jc(4), 16.0, 15.0, OP.mult, OP.add), "J4", "lTH")
+    v("ts", (T.lBM[:, 0:20], Jc(5), -1.0, 25.0, OP.mult, OP.add), "J5", "lBM0")
+    v("copy", (T.lBM[:, 20:40], Jc(5)), "J5", "lBM1")
+    for s in range(4):
+        act(T.tW[:, 5 * s::16], T.BD[:, s::4], "BD zW", "tW%d" % s, 64, scale=2.0)
+        sel(T.tE[:, 512 * s:512 * s + 512], T.one[:], [[-1, 512]], OP.is_equal, s, 4, "one", "tE%d" % s, 512)
+    v("q", (T.kqW[:], T.ksW[:], T.tW[:]), keys("tW", 4), "kW", qc(128))
+    v("q", (T.kqE[:], T.ksE[:], T.tE[:]), keys("tE", 4), "kE", qc(512))
 
-    v("q", (T.qu[:], T.su[:], T.ut[:]), "ut", "qu", 150)
-    v("q", (T.qv[:], T.sv[:], T.vt[:]), "vt", "qv", 150)
+    v("q", (T.qu[:], T.su[:], T.ut[:]), "ut", "qu", qc(128))
+    v("q", (T.qv[:], T.sv[:], T.vt[:]), "vt", "qv", qc(128))
     for i in range(2):
         off = T.upk[:, 8 * i:8 * i + 8]
-        v("copy", (T.qp[:, 128 * i:128 * i + 128].bitcast(dt.uint32), T.qu[:].bitcast(dt.uint32).indirect(off)), "qu upk", "qp%d" % i, 250)
-        act(T.sp[:, 128 * i:128 * i + 128], T.su[:].indirect(off), "qu upk", "sp%d" % i, 250)
-    v("q", (T.qx0[:, 128:], T.sx0[:, 128:], T.X[:, 512:]), XA, "qx0a", 290)
-    v("q", (T.qx0[:, 0:128], T.sx0[:, 0:128], T.X[:, 0:512]), XA + " Xb", "qx0b", 150)
+        v("copy", (T.qp[:, 128 * i:128 * i + 128].bitcast(dt.uint32), T.qu[:].bitcast(dt.uint32).indirect(off)), "qu upk", "qp%d" % i, gv(128))
+        act(T.sp[:, 128 * i:128 * i + 128], T.su[:].indirect(off), "qu upk", "sp%d" % i, gs(128))
+    v("q", (T.qx0[:, 128:], T.sx0[:, 128:], T.X[:, 512:]), "Xa0", "qx0a", qc(256))
+    v("q", (T.qx0[:, 0:128], T.sx0[:, 0:128], T.X[:, 0:512]), "Xb", "qx0b", qc(128))
 
     for t in range(R):
         qx, sx, lq, ls = [T[n + str(t)] for n in ("qx", "sx", "lq", "ls")]
@@ -229,113 +231,104 @@ def rank_program(g, core, T, topo):
                 mm(bk, n, T.qp[:, 128 * i:128 * i + 128], T.sp[:, 128 * i:128 * i + 128], qx[:, a:b], sx[:, a:b], True, True,
                    "qp%d sp%d qx%d%s" % (i, i, t, p))
             ks = "#%d" % bs
-            act(T.A[:, 4 * a + 2:4 * b:4], bank(bd, n), "#%d" % bd, "A2" + p, n, f=AF.Sign)
-            v("scan", (rev(T.V, a, b), rev(T.c1, a, b), rbank(bs, n), 0.0, OP.add, OP.max), "c1 " + ks, "V" + p, n)
-            v("scan", (T.U[:, a:b], T.c2[:, a:b], bank(bs, n), 0.0, OP.add, OP.max), "c2 " + ks, "U" + p, n)
-            v("tt", (T.A[:, 4 * a:4 * b:4], bank(bs, n), T.V[:, a:b], OP.is_ge), ks + " V" + p, "A0" + p, n)
-            v("tt", (T.A[:, 4 * a + 5:4 * b:4], bank(bs, n, 1), T.U[:, a:b - 1], OP.is_gt), ks + " U" + p, "A1" + p, n)
+            va, ua = VV + 16 + C - b, UU + 16 + a
+            act(T.A[:, 2 * C + a:2 * C + b], bank(bd, n), "#%d" % bd, "A2" + p, n, f=AF.Sign)
+            v("scan", (T.UV[:, va:va + n], rev(T.c1, a, b), rbank(bs, n), 0.0, OP.add, OP.max), "c1 " + ks, "V" + p, n)
+            v("scan", (T.UV[:, ua:ua + n], T.c2[:, a:b], bank(bs, n), 0.0, OP.add, OP.max), "c2 " + ks, "U" + p, n)
+            v("tt", (T.A[:, C + a:C + b], bank(bs, n), rev(T.UV, va, va + n), OP.is_ge), ks + " V" + p, "A0" + p, n)
+            v("tt", (T.A[:, a + 1:b], bank(bs, n, 1), T.UV[:, ua:ua + n - 1], OP.is_gt), ks + " U" + p, "A1" + p, n)
             act(T.S[:, a:b], bank(bs, n), ks, "S" + p, n)
-        v("tt", (T.TB[:, 65:89], T.V[:, 0::16], T.U[:, 15::16], OP.max), "Va Vb Ua Ub", "TBm")
+        kU, kV = "Ua Ub pad0", "Va Vb pad1"
+        v("tt", (T.UV[:, TB + 1:TB + 25], T.UV[:, VV + 399:VV + 15:-16], T.UV[:, UU + 31:UU + 400:16], OP.max), "Va Vb Ua Ub", "TBm")
         for h in range(2):
-            a = 18 * h
-            act(T.BMx[:, 16 * a:608 if h else 304], T.TB[:, 64:96].indirect(T.lBM[:, a:38 if h else 19]), "TBm lBM0 lBM1",
-                "BMx1 BMx0" if h else "BMx0 BMx2", 60 + GA * 312)
-        v("copy", (T.TB[:, 1:25], T.U[:, 15::16]), "Ua Ub", "TBs")
-        v("copy", (T.TB[:, 33:57], T.V[:, C - 16::-16]), "Va Vb", "TBp")
-        v("set", (T.A[:, 1::64], 0.0), "", "A1a A1b")
-        v("scan", (T.CNT[:, 16:16 + C], T.seg[:], T.A[:, 0::4], 0.0, OP.mult, OP.add), "seg A0a A0b", "CL", 192)
-        v("scan", (T.CNT[:, 528:528 + C], T.seg[:], T.A[:, 1::4], 0.0, OP.mult, OP.add), "seg A1a A1b", "CR", 192)
-        v("tt", (T.m[:], T.CNT[:, 15::16], T.cc[:], OP.is_equal), "CL CR cc", "m", 128)
-        v("q", (T.qa[:], T.sa[:], T.A[:]), "A0a A0b A1a A1b A2a A2b A3", "qa", 420)
-        for b, n, i, stop in ((0, "A", 1, False), (2, "A", 0, False), (3, "A", 2, False), (6, "A", 3, True), (7, "B", 0, True)):
-            cm(b, n, i, T.qa, T.sa, "qa", True, stop)
-        v("tt", (T.cov[:, 0:304], T.TB[:, 0:32].indirect(T.lTH[:, 0:19]), T.BMx[:, 0:304], OP.is_ge), "TBs lTH BMx0", "cov0", 500)
-        v("tt", (T.cov[:, 304:608], T.TB[:, 32:64].indirect(T.lTH[:, 0:19]), T.BMx[:, 304:608], OP.is_gt), "TBp lTH BMx1", "cov1", 500)
-        v("scan", (T.run[:], T.one[:], T.cov[:], 0.0, OP.add, OP.mult), "one one1 cov0 cov1", "run", 304)
-        ends = T.run[:].indirect(T.lE[:, 0:4])
-        v("tt", (T.E[:, 64:128], T.base[:], T.m[:], OP.mult), "base0 base1 m", "mb", 128)
-        v("tt", (T.E[:, 0:64], ends, T.E[:, 64:128], OP.subtract), "run lE mb", "E", 150)
-        v("ts", (T.tt[:, 1:65], T.E[:, 0:64], -1.0, -100.0, OP.mult, OP.add), "E", "tt")
-        v("tt", (T.TD[:, 64:128], ends, T.m[:], OP.mult), "run lE m", "TD1", 150)
-        v("tt", (sm(9), T.TD[:, 97:121], T.TD[:, 65:89], OP.subtract), "TD1", "sm9")
-        v("ts", (T.lD[:], sm(9), NB - 1.0, None, OP.add), "sm9", "lD")
-        v("ts", (T.uu[:, 0:64], T.m[:], 1000.0, None, OP.mult), "m", "mk")
-        v("tt", (T.uu[:, 64:128], T.uu[:, 0:64], T.aX[:, 0:64], OP.add), "mk aX0 aX1", "aXa", 128)
-        v("ts", (T.TD[:, 128:192], T.TD[:, 64:128], 16.0, None, OP.mult), "TD1", "TD2")
-        v("tt", (T.aX[:, 64:128], T.TD[:, 128:192], T.uu[:, 64:128], OP.subtract), "aXa TD2", "aX2", 128)
-        v("ts", (T.c5[:, 15::16], T.aX[:, 65:89], T.PP[:, 79:80], None, OP.add), "aX2 PP4", "c5")
-        v("ts", (T.c5r[:, 15::16], T.aX[:, 97:121], T.PP[:, 79:80], None, OP.add), "aX2 PP4", "c5r")
-        act(T.B[:, 2::4], T.DT[:, 0:48].indirect(T.lD[:, 0:24]), "DT lD", "B2", GC)
-        v("tt", (T.B[:, 1::4], T.TB[:, 0:32].indirect(T.tt[:, 2:26]), T.S[:], OP.is_lt), "TBs tt Sa Sb", "B1", GC)
-        v("tt", (T.B[:, 0::4], T.TB[:, 32:64].indirect(T.tt[:, 34:58]), T.S[:], OP.is_le), "TBp tt Sa Sb", "B0", GC)
-        v("q", (T.qb[:], T.sb[:], T.B[:]), "B0 B1 B2 B3", "qb", 420)
-        for b, n, i in ((2, "A", 0), (0, "A", 1), (3, "B", 1)):
-            cm(b, n, i, T.qb, T.sb, "qb", False, True)
-        for i, a in ((0, 34), (1, 2)):
-            act(T.junk[:, C * i:C * i + C], T.OH[:].indirect(T.tt[:, a:a + 24]), "OH0 OH1 tt", "junk%d acc%d" % (i, i), GC,
+            act(T.BMx[:, 304 * h:304 * h + 304], wB.indirect(T.lBM[:, 20 * h:20 * h + 19]), "TBm lBM%d" % h, "BMx%d" % h, gs(304))
+        v("set", (T.A[:, 0:C:16], 0.0), "", "A1a A1b")
+        v("scan", (T.CNT[:, 0:C], T.seg[:], T.A[:, C:2 * C], 0.0, OP.mult, OP.add), "seg A0a A0b", "CL", 192)
+        v("scan", (T.CNT[:, C:], T.seg[:], T.A[:, 0:C], 0.0, OP.mult, OP.add), "seg A1a A1b", "CR", 192)
+        v("tt", (T.m[:], T.CNT[:, 15::16], T.cc[:], OP.is_equal), "CL CR cc", "m", 96)
+        v("copy", (T.ML[:], T.m[:]), "m", "ML")
+        v("tt", (T.mb[:], T.m[:], T.base[:], OP.mult), "m base0 base1", "mb", 96)
+        v("tt", (T.corr[:], T.base[:], T.mb[:], OP.subtract), "mb base0 base1", "corr", 96)
+        v("tt", (sm(0), T.CNT[:, C + 15::16], T.CNT[:, 15:C:16], OP.subtract), "CL CR", "sm0")
+        for h in (1, 0):
+            act(T.FR[:, C * h:C * h + C], T.FT[:].indirect(T.ML[:, 24 * h:24 * h + 24]), "FT ML", "FR%d" % h, gs(C))
+        v("q", (T.qa[:], T.sa[:], T.A[:]), "A0a A0b A1a A1b A2a A2b", "qa", qc(288))
+        mm(0, 192, T.kqW[:], T.ksW[:], T.qa[:, 0:192], T.sa[:, 0:192], True, False, "kW qa")
+        mm(2, 128, T.kqW[:], T.ksW[:], T.qa[:, 160:288], T.sa[:, 160:288], True, True, "kW qa")
+        v("scan", (T.fr[:], bank(2, 128, 32), T.c6[:, 0:96], -5000.0, OP.max, OP.add), "#2 c6", "fr", 96)
+        v("ts", (sm(1), T.fr[:, 3::4], -500.0, -5000.0, OP.is_le, OP.mult), "fr", "sm1")
+        v("tt", (T.cov[:, 0:304], wU.indirect(T.lTH[:, 0:19]), T.BMx[:, 0:304], OP.is_ge), kU + " lTH BMx0", "cov0", gv(304))
+        v("tt", (T.cov[:, 304:608], wV.indirect(T.lTH[:, 0:19]), T.BMx[:, 304:608], OP.is_gt), kV + " lTH BMx1", "cov1", gv(304))
+        v("scan", (T.run[:], T.t32[:], T.cov[:], 0.0, OP.add, OP.mult), "t32 cov0 cov1", "run", 304)
+        v("tt", (T.E[:], T.run[:].indirect(T.lE[:, 0:3]), T.mb[:], OP.subtract), "run lE mb", "E", gv(48))
+        v("ts", (T.ix[:], T.E[:], -0.5, -1.0, OP.mult, OP.add), "E", "ix")
+        v("ts", (T.cx[:, 3:96:4], T.E[:, 0:24], 0.0, kL, OP.min, OP.add), "E kL", "cx")
+        v("ts", (T.cx[:, 99::4], T.E[:, 24:48], 0.0, kR, OP.min, OP.add), "E kR", "cx1")
+        v("tt", (T.B[:, 0:C], wU.indirect(T.ix[:, 0:24]), T.S[:], OP.is_lt), kU + " ix Sa Sb", "B0", gv(C))
+        v("tt", (T.B[:, C:], wV.indirect(T.ix[:, 24:48]), T.S[:], OP.is_le), kV + " ix Sa Sb", "B1", gv(C))
+        v("q", (T.qb[:], T.sb[:], T.B[:]), "B0 B1", "qb", qc(192))
+        mm(0, 192, T.kqW[:], T.ksW[:], T.qb[:], T.sb[:], False, True, "kW qb")
+        v("scan", (T.xx[:], bank(0, 192), T.cx[:], 5000.0, OP.min, OP.add), "#0 cx cx1", "xx", 192)
+        v("ts", (T.lp[:], T.xx[:, 3::4], -0.5, KX / 2, OP.mult, OP.add), "xx", "lp")
+        v("tt", (T.P2[:], T.xx[:, 3::4], T.corr[:], OP.subtract), "xx corr", "P2", 96)
+        for i, a in ((0, 24), (1, 0)):
+            act(T.junk[:, C * i:C * i + C], T.OH[:].indirect(T.ix[:, a:a + 24]), "OH ix", "junk%d acc%d" % (i, i), gs(C) + 24,
                 accum_out=T.acc[:, i:i + 1])
-        v("copy", (T.WI[:, 8:10], T.acc[:]), "acc0 acc1", "WI2")
-        v("ts", (T.WI[:, 0:4:2], T.WI[:, 8:10], 511, None, OP.bitwise_and), "WI2", "WI0")
-        v("ts", (T.WI[:, 1:4:2], T.WI[:, 8:10], 9, None, OP.arith_shift_right), "WI2", "WI1")
-        v("copy", (T.rp[:], T.WI[:, 0:4].indirect(T.upk[:, 16:24])), "WI0 WI1 upk", "rp", 250)
-        v("tr", (T.rt[:], T.rp[:]), "rp", "rt", 128)
-        v("ts", (T.dL[:, 0::16], T.rt[:].indirect(T.lE[:, 4:6]), -1.0, None, OP.mult), "rt lT", "dL", 100)
-        v("ts", (T.dR[:, 15::16], T.rt[:].indirect(T.lE[:, 6:8]), -1.0, None, OP.mult), "rt lT", "dR", 100)
-        v("scan", (T.GL[:, 2:C + 2], T.dL[:, 0:C], bank(6), 0.0, OP.add, OP.add), "dL #6", "GL", C)
-        v("scan", (T.GR[:, 2:C + 2], rev(T.dR), rbank(7), 0.0, OP.add, OP.add), "dR #7", "GR", C)
-        rL, rR = T.xx[:, 15:C:16], T.xx[:, C + 15::16]
-        v("scan", (T.xx[:, 0:C], bank(0), T.c5[:], -5000.0, OP.max, OP.add), "#0 c5", "xL", C)
-        v("scan", (T.xx[:, C:], bank(2), T.c5r[:], -5000.0, OP.max, OP.add), "#2 c5r", "xR", C)
-        v("ts", (T.lp[:, 0:24], rL, -1.0, -4000.0, OP.mult, OP.add), "xL", "lp0")
-        v("ts", (T.lp[:, 24:48], rR, -1.0, -4000.0, OP.mult, OP.add), "xR", "lp1")
-        v("tt", (T.zt[:], bank(3), T.a2row[:], OP.add), "#3 a2row", "zt", C)
-        act(T.z[:], T.zt[:], "zt", "z", C, f=AF.Relu)
-        act(T.GgL[:], T.GL[:, 0:C + 2].indirect(T.lp[:, 0:24]), "GL GL0 lp0", "GgL", GC)
-        act(T.GgR[:], T.GR[:, 0:C + 2].indirect(T.lp[:, 24:48]), "GR GR0 lp1", "GgR", GC)
-        v("scan", (rev(T.mR), rev(T.GgR), rev(T.c3), 5000.0, OP.min, OP.add), "GgR c3", "mR", C)
-        v("tt", (sm(0), T.CNT[:, 543:543 + C:16], T.CNT[:, 31:31 + C:16], OP.subtract), "CL CR", "sm0")
-        v("tt", (sm(5), T.uu[:, 1:25], sm(0), OP.subtract), "mk sm0", "sm5")
-        v("tt", (sm(6), T.uu[:, 1:25], sm(5), OP.add), "mk sm5", "sm6")
-        v("tt", (sm(10), T.uu[:, 1:25], T.uu[:, 33:57], OP.add), "mk", "sm10")
-        v("ts", (sm(1), rL, 2.0, c15, OP.mult, OP.add), "xL c15", "sm1")
-        v("tt", (sm(8), sm(1), sm(6), OP.add), "sm1 sm6", "sm8")
-        v("tt", (sm(2), rL, rR, OP.add), "xL xR", "sm2")
-        v("tt", (sm(11), sm(2), sm(10), OP.add), "sm2 sm10", "sm11")
-        v("ts", (sm(3), sm(11), 2.0, 17771.0, OP.mult, OP.add), "sm11", "sm3")
-        v("tt", (T.c4[:, 15::16], sm(8), T.mR[:, 0::16], OP.subtract), "sm8 mR", "c4")
-        v("scan", (T.mL[:], T.GgL[:], T.c4[:], 5000.0, OP.min, OP.add), "GgL c4", "mL", C)
-        v("ts", (T.oc16[:, 0:24], T.mL[:, 15::16], -1.0, 5000.0, OP.mult, OP.add), "mL", "op16")
-        v("tt", (sm(4), sm(3), T.mL[:, 15::16], OP.subtract), "sm3 mL", "sm4")
-        v("copy", (T.oc16[:, 24:48], sm(4)), "sm4", "cl16")
+            v("ts", (T.rp[:, 32 * i:32 * i + 32], T.one[:, 0:32], T.acc[:, i:i + 1], None, OP.mult), "one acc%d" % i, "rp%d" % i)
+        v("tr", (T.rt[:], T.rp[:]), "rp0 rp1", "rt")
+        v("copy", (T.WI[:], T.rt[:].indirect(T.lE[:, 4:6])), "rt lT", "WI", gv(32))
+        v("ts", (T.HI[:, 0::2], T.WI[:], 511, None, OP.bitwise_and), "WI", "HI0")
+        v("ts", (T.HI[:, 1::2], T.WI[:], 9, None, OP.arith_shift_right), "WI", "HI1")
+        v("copy", (T.DD[:, 0::16], T.HI[:, 0:48]), "HI0 HI1 DD1", "DD")
+        v("scan", (T.GR[:, 2:C + 2], T.DD[:, C:], rev(T.FR), 192.0, OP.add, OP.subtract), "DD FR0", "GR", 192)
+        v("scan", (T.GL[:, 2:C + 2], T.DD[:, 0:C], T.FR[:, C:], 192.0, OP.add, OP.subtract), "DD FR1", "GL", 192)
+        act(T.Gg[:, C:], T.GR[:, 0:C + 2].indirect(T.lp[:, 24:48]), "GR GR0 lp", "GgR", gs(C))
+        if GGV:
+            v("copy", (T.Gg[:, 0:C], T.GL[:, 0:C + 2].indirect(T.lp[:, 0:24])), "GL GL0 lp", "GgL", gv(C))
+        else:
+            act(T.Gg[:, 0:C], T.GL[:, 0:C + 2].indirect(T.lp[:, 0:24]), "GL GL0 lp", "GgL", gs(C))
+        v("scan", (rev(T.mR), rev(T.Gg, C, 2 * C), rev(T.c3), -2000.0, OP.max, OP.add), "GgR c3", "mR", 192)
+        pL, pR = T.P2[:, 0:24], T.P2[:, 24:48]
+        v("tt", (sm(2), sm(0), pL, OP.subtract), "sm0 P2", "sm2")
+        v("tt", (sm(3), pL, pR, OP.add), "P2", "sm3")
+        v("tt", (sm(4), pR, pL, OP.subtract), "P2", "sm4")
+        v("tt", (sm(5), sm(4), sm(1), OP.add), "sm4 sm1", "sm5")
+        v("ts", (T.zi[:], sm(5), 0.5, 384.0, OP.mult, OP.add), "sm5", "zi")
+        act(T.z[:], T.ID[:].indirect(T.zi[:]), "ID zi", "z", gs(C))
+        v("tt", (T.c4[:, 15::16], sm(2), T.mR[:, 0::16], OP.subtract), "sm2 mR", "c4")
+        v("scan", (T.mL[:], T.Gg[:, 0:C], T.c4[:], -2000.0, OP.max, OP.add), "GgL c4", "mL", 192)
+        v("ts", (T.oc16[:, 0:24], T.mL[:, 15::16], 1100.0, None, OP.add), "mL", "op16")
+        v("tt", (sm(6), sm(3), T.mL[:, 15::16], OP.add), "sm3 mL", "sm6")
+        v("ts", (T.oc16[:, 24:48], sm(6), 1871.0 - 2 * KX, None, OP.add), "sm6", "cl16")
         DB, OB = (0, 2, 6, 7), (1, 3, 4, 5)
         for b in range(4):
-            cm(DB[b], "E", b, lq, ls, "qL%d lp0 lp1" % t, True, True)
+            mm(DB[b], C, T.kqE[:, 128 * b:128 * b + 128], T.ksE[:, 128 * b:128 * b + 128], lq[:], ls[:], True, True, "kE qL%d" % t)
             act(T.Dd[:, b::4], bank(DB[b]), "#%d op16" % DB[b], "Dd%d" % b, C)
-        v("copy", (T.EW[:].indirect(T.oc16[:, 0:24]), T.z[:]), "op16 z", "EW", 50 + SC * C)
-        v("copy", (T.EW[:].indirect(T.oc16[:, 24:48]), T.z[:]), "cl16 z", "EW", 50 + SC * C)
-        for h in range(2):
-            act(T.PH[:, C * h:C * h + C], T.EW[:, C * h:C * h + C], "EW", "PH%d" % h, C, f=AF.Sign, scale=-1.0, bias=0.5)
-        v("scan", (T.Y[:, 0:C], T.PH[:, 0:C], T.EW[:, 0:C], 0.0, OP.mult, OP.subtract), "PH0 EW", "Y0", C)
-        v("scan", (T.Y[:, C:], T.PH[:, C:], T.EW[:, C:], T.Y[:, C - 1:C], OP.mult, OP.subtract), "PH1 EW Y0", "Y1", C)
-        act(T.Yg[:, 192:], T.Y[:].indirect(T.oc16[:, 12:24]), "Y0 Y1 op16", "Yg1", 330)
-        v("copy", (T.Yg[:, 0:192], T.Y[:].indirect(T.oc16[:, 0:12])), "Y0 Y1 op16", "Yg0", 330)
-        v("scan", (T.dg[:], T.Yg[:], T.c5y[:], -5000.0, OP.max, OP.add), "Yg0 Yg1 c5y", "dg", C)
-        act(sm(7), T.dg[:, 15::16], "dg", "sm7", 64, f=AF.Abs, bias=4000.0)
+        v("copy", (T.EW[:].indirect(T.oc16[:, 0:24]), T.z[:]), "op16 z", "EW", sv(C))
+        v("copy", (T.EW[:].indirect(T.oc16[:, 24:48]), T.z[:]), "cl16 z", "EW", sv(C))
+        v("ts", (T.PH[:, 0:C], T.EW[:, 0:C], 1 / EPS, -1.0, OP.mult, OP.max), "EW", "PH0", C)
+        act(T.PH[:, C:], T.EW[:, C:], "EW", "PH1", C, f=AF.Sign)
+        v("scan", (T.Y[:], T.PH[:], T.EW[:], 0.0, OP.mult, OP.add), "PH0 PH1 EW", "Y", 2 * C)
+        act(T.Yg[:, 192:], T.Y[:].indirect(T.oc16[:, 12:24]), "Y op16", "Yg1", gs(192))
+        v("copy", (T.Yg[:, 0:192], T.Y[:].indirect(T.oc16[:, 0:12])), "Y op16", "Yg0", gv(192))
+        v("scan", (T.dg[:], T.Yg[:], T.c5[:], -5000.0, OP.max, OP.add), "Yg0 Yg1 c5", "dg", C)
+        act(sm(7), T.dg[:, 15::16], "dg", "sm7", 64, f=AF.Abs, bias=2048.0)
         v("ts", (T.at[:], sm(7), -0.5, None, OP.add), "sm7", "at")
-        v("copy", (T.O[:].indirect(T.at[:, 0:24]), T.arow[:]), "at arow", "O", 50 + SC * C)
+        v("copy", (T.O[:].indirect(T.at[:, 0:24]), T.arow[:]), "at arow", "O", sv(C))
         ob, ll = T.ob[:, 24 * t:24 * t + 24], T.ll[:, 24 * t:24 * t + 24]
-        v("scan", (T.o4[:, H:], T.O[:, H:], T.c6[:, H:], -5000.0, OP.max, OP.add), "O c6", "o4b", K)
+        v("scan", (T.o4[:, H:], T.O[:, H:], T.c6[:, H:], -2000.0, OP.max, OP.add), "O c6", "o4b")
         v("ts", (ob, T.o4[:, H + 3::4], 4.0, l4c, OP.mult, OP.add), "o4b l4c", "ob%d" % t)
         send(ll, ob, "al%d" % t, "ob%d" % t, "sent2")
         landed("al%d" % t, n_in, "sent2", "ll%d" % t, 2800.0)
+        v("scan", (T.o4[:, 0:H], T.O[:, 0:H], T.c6[:, 0:H], -2000.0, OP.max, OP.add), "O c6", "o4a", H // 2)
+        v("ts", (T.oo[:], T.o4[:, 3:H:4], 4.0, l4c, OP.mult, OP.add), "o4a l4c", "oo")
         if t == R - 1:
-            dma("y", "dol", T.ol[:], T.O[0:128:16, :], "O", "")
-        v("scan", (T.o4[:, 0:H], T.O[:, 0:H], T.c6[:, 0:H], -5000.0, OP.max, OP.add), "O c6", "o4a", H)
-        v("ts", (T.oo[:], T.o4[:, 3:H:4], 4.0, l4c, OP.mult, OP.add), "o4a l4c", "oo", 72)
-        act(T.Z[:, 960:], T.X[:].indirect(T.oo[:, 36:72]), XA + " Xb oo", "Z2", 900)
-        v("copy", (T.Z[:, 384:960], T.X[:].indirect(T.oo[:, 0:36])), XA + " Xb oo", "Z1", 900)
-        act(T.Z[:, 0:384], T.Dd[:].indirect(ll), keys("Dd", 4) + " ll%d" % t, "Z0", GC)
-        v("q", (T.qz[:, K:], T.sz[:, K:], T.Z[:, 4 * K:]), "Z1 Z2", "qz", 320)
+            act(T.O32[:], T.O[:], "O", "O32", C, f=AF.Identity, bias=192.0)
+            dma("y", "dol", T.ol[:], T.O32[0:128:16, :], "O32", "")
+        act(T.Z[:, 960:], T.X[:].indirect(T.oo[:, 36:72]), XA + " Xb oo", "Z2", gs(576))
+        v("copy", (T.Z[:, 384:960], T.X[:].indirect(T.oo[:, 0:36])), XA + " Xb oo", "Z1", gv(576))
+        act(T.Z[:, 0:384], T.Dd[:].indirect(ll), keys("Dd", 4) + " ll%d" % t, "Z0", gs(C))
+        v("q", (T.qz[:, K:], T.sz[:, K:], T.Z[:, 4 * K:]), "Z1 Z2", "qz", qc(H))
         wv = lambda b: (T.wq[:, 128 * b:128 * b + 128], T.wsp[:, 128 * b:128 * b + 128])
         v("ts", (T.Z64[:, 384:1152], T.Z[:, 384:1152], 64.0, None, OP.mult), "Z1 Z2", "Z64a", 384)
         act(T.Z64[:, 1152:], T.Z[:, 1152:], "Z2", "Z64c", 384, scale=64.0)
@@ -343,15 +336,15 @@ def rank_program(g, core, T, topo):
             mm(OB[b], H, *wv(b), T.qz[:, K:], T.sz[:, K:], True, True, "wq wsp qz")
             v("tt", (T.X64[:, 4 * K + b::4], bank(OB[b], H), T.Z64[:, 4 * K + b::4], OP.add), "#%d Z64a Z64c" % OB[b], "X64a%d" % b, H)
             act(T.X[:, 4 * K + b::4], T.X64[:, 4 * K + b::4], "X64a%d" % b, "Xa%d" % b, H, scale=0.015625)
-        v("q", (T.qzb[:], T.szb[:], T.Z[:, 0:512]), "Z0 Z1", "qzb", 150)
+        v("q", (T.qzb[:], T.szb[:], T.Z[:, 0:512]), "Z0 Z1", "qzb", qc(128))
         v("ts", (T.Z64[:, 0:4 * K], T.Z[:, 0:4 * K], 64.0, None, OP.mult), "Z0", "Z64b", 2 * K)
         for b in range(4):
             mm(DB[b], 128, *wv(b), T.qzb[:], T.szb[:], True, True, "wq wsp qzb")
             v("tt", (T.X64[:, b:4 * K:4], bank(DB[b], K), T.Z64[:, b:4 * K:4], OP.add), "#%d Z64b" % DB[b], "X64b%d" % b, K)
         qn, sn = T["qx%d" % (t + 1)], T["sx%d" % (t + 1)]
-        v("q", (qn[:, 128:], sn[:, 128:], T.X[:, 512:]), XA, "qx%da" % (t + 1), 290)
+        v("q", (qn[:, 128:], sn[:, 128:], T.X[:, 512:]), XA, "qx%da" % (t + 1), qc(256))
         v("ts", (T.X[:, 0:4 * K], T.X64[:, 0:4 * K], 0.015625, None, OP.mult), keys("X64b", 4), "Xb", 2 * K)
-        v("q", (qn[:, 0:128], sn[:, 0:128], T.X[:, 0:512]), XA + " Xb", "qx%db" % (t + 1), 150)
+        v("q", (qn[:, 0:128], sn[:, 0:128], T.X[:, 0:512]), XA + " Xb", "qx%db" % (t + 1), qc(128))
 
     for p, a, b, bk in (("a", 128, C, 1), ("b", 0, 128, 4)):
         kx = "qx%d%s" % (R, p)
@@ -423,3 +416,6 @@ def rank_program(g, core, T, topo):
         total[o["sem"]] = o["count"] = total.get(o["sem"], 0) + o["inc"]
     for sem, val in total.items():
         wait("g", sem, val)
+
+
+GGV = False

@@ -3,30 +3,32 @@ from concourse.mybir import dt, AluOpType as OP, ActivationFunctionType as AF
 C, K, R, N = 384, 96, 3, 4
 NB, H = C // 16, C - K
 F32, BF, F16, I32, U16, Q4, U8 = "float32", "bfloat16", "float16", "int32", "uint16", "float8_e4m3fn_x4", "uint8"
-BIG, KX, EPS = 1e28, 2125.0, 2.0 ** -12
+BIG, KX, EPS = 1e28, 1813.0, 2.0 ** -12
 UU, TB, VV = 0, 400, 432
 
 SCRATCH = {"ps": ("psum", [128, 4096], F32)}
 for _d, _l in (
-        (BF, "X:1536 X64:1536 Z:1536 Z64:1536 Dd:1536 ut:512 vt:512 tW:512 tE:2048 A:1152 B:768 one:512 t32:608 BD:128 seg:384 "
-             "CNT:768 cov:608 run:608 junk:768 FT:16 FR:768 GL:400 GR:400 Gg:768 OH:400 c1:384 c2:384 c3:384 c6:384 O:384 arow:384 PH:768"),
-        (F16, "c4:384 mL:384 mR:384 DD:768 o4:384"),
+        (BF, "X:1536 X64:1536 Z:1536 Z64:1536 Dd:1536 ut:512 vt:512 tW:512 tE:2048 A:1152 B:768 one:608 t32:608 BD:128 seg:384 "
+             "CNT:768 cov:608 run:608 junk:768 FT:16 FR:768 GL:400 GR:400 Gg:768 OH:400 c1:384 c2:384 c3:384 c6:384 O:384 arow:384 "
+             "PH:768 base:48 cc:48"),
+        (F16, "c4:384 mL:384 mR:384 DD:768 o4:384 m:48 mb:48 corr:48 P2:48 xx:192"),
         (Q4, "qu:128 qv:128 qp:256 wq:512 qz:384 qzb:128 kqW:128 kqE:512 qa:288 qb:192 qx0:384 qx1:384 qx2:384 qx3:384 lq0:384 lq1:384 lq2:384"),
         (U8, "su:128 sv:128 sp:256 wsp:512 sz:384 szb:128 ksW:128 ksE:512 sa:288 sb:192 sx0:384 sx1:384 sx2:384 sx3:384 ls0:384 ls1:384 ls2:384"),
         (I32, "cI:64 WI:32 HI:64"),
         (U16, "rep:24 upk:16 lBM:40 lTH:20 lE:6 ML:48 ix:48 lp:48 zi:24 oc16:48 at:24 oo:72 ob:72 ll:72"),
-        (F32, "cF:16 dm:32 tm:32 PP:96 c5:384 cx:192 aW:48 J:160 ER:80 ERd:80 base:48 cc:48 S:384 UV:832 BMx:608 "
-              "m:48 mb:48 corr:48 E:48 P2:48 acc:2 rp:64 rt:64 xx:192 fr:96 sm:240 ID:768 z:384 EW:768 Y:768 Yg:384 dg:384 O32:384 ys:384")):
+        (F32, "cF:16 dm:32 tm:32 PP:96 c5:384 cx:192 aW:48 J:160 ER:80 ERd:80 S:384 UV:832 BMx:608 "
+              "E:48 acc:2 rp:64 rt:64 fr:96 sm:240 ID:768 z:384 EW:768 Y:768 Yg:384 dg:384 O32:384 ys:384")):
     for _e in _l.split():
         _n, _w = _e.split(":")
         SCRATCH[_n] = ("sbuf", [128, int(_w)], _d)
 
-SEMAPHORES = ["v", "s", "t", "g", "dxa", "dxb", "du", "dv", "dwc", "dws", "dy", "dol", "doc", "dos", "loc"] + \
+SEMAPHORES = ["v", "s", "t", "g", "dx0", "dx1", "dx2", "du", "dv", "dwc", "dws", "dy", "dol", "doc", "dos", "loc"] + \
              ["aq%d" % t for t in range(R)] + ["al%d" % t for t in range(R)]
 
-GA, SC, LAG = 1.45, 3.2, 200.0
-ORDER, TRIES = {}, 3000
-INORDER = True
+GA, SC, LAG, DLAG, LL = 1.56, 3.8, 200.0, 2400.0, 2800.0
+LAGS = ((0.7, 0.75), (1.15, 1.1))
+ORDER, TRIES, SEED, MUT = {}, 4000, 12345, 4
+CUT, Z64S, XV = (160, 304), "b", "bc"
 
 
 def rank_program(g, core, T, topo):
@@ -38,12 +40,12 @@ def rank_program(g, core, T, topo):
     mask = topo.mask(core, nxt)
     n_out, n_in = len(topo.engines(core, nxt)), len(topo.engines(prv, core))
     QS = {"v": g.vector, "s": g.scalar, "t": g.tensor, "g": g, "y": g.sync}
-    ops, wrote, read = [], {}, {}
+    ops, wrote, read, site = [], {}, {}, [0]
 
     def add(q, emit, r, w, busy, lag, sem, inc, acc=False):
         r, w = r.split(), w.split()
         deps = {}
-        own = lambda i: INORDER and ops[i]["q"] == q and ops[i]["sem"] == q == sem
+        own = lambda i: ops[i]["q"] == q and ops[i]["sem"] == q == sem
         for k in r + w:
             if k in wrote:
                 deps[wrote[k]] = deps.get(wrote[k], False) or not (acc and k in w)
@@ -51,7 +53,8 @@ def rank_program(g, core, T, topo):
             for i in read.get(k, []):
                 if k in w or ops[i]["q"] != q:
                     deps[i] = deps.get(i, False) or not own(i)
-        ops.append({"q": q, "emit": emit, "deps": deps, "busy": busy, "lag": lag, "sem": sem, "inc": inc})
+        ops.append({"q": q, "emit": emit, "deps": deps, "busy": busy, "lag": lag, "sem": sem, "inc": inc, "site": site[0]})
+        site[0] += 1
         for k in r:
             read.setdefault(k, []).append(len(ops) - 1)
         for k in w:
@@ -67,7 +70,7 @@ def rank_program(g, core, T, topo):
         add(q, lambda: call().then_inc(T.sem[q], 1), r, w, max(c, 64) * 0.9, LAG, q, 1, acc)
 
     def dma(q, sem, out, in_, r, w):
-        add(q, lambda: QS[q].dma_start(out, in_).then_inc(T.sem[sem], 16), r, w, 100.0, 2600.0, sem, 16)
+        add(q, lambda: QS[q].dma_start(out, in_).then_inc(T.sem[sem], 16), r, w, 100.0, DLAG, sem, 16)
 
     def send(out, in_, sem, r, w):
         add("g", lambda: g.remote_dma(out, in_, T.sem[sem], T.sem.loc, pid, rid, mask), r, w, 300.0, 0.0, "loc", n_out)
@@ -78,7 +81,7 @@ def rank_program(g, core, T, topo):
     def v(name, args, r, w, c=64):
         op("v", name, args, r, w, c)
 
-    def act(out, in_, r, w, c, f=AF.Copy, **kw):
+    def act(out, in_, r, w, c=64, f=AF.Copy, **kw):
         op("s", "act", (out, in_, f), r, w, c, **kw)
 
     def iota(out, pat, base, w, c=32, whole=False):
@@ -106,18 +109,20 @@ def rank_program(g, core, T, topo):
     gs = lambda n: 78 + GA * n
     sv = lambda n: 60 + SC * n
     qc = lambda n: 15 + 1.06 * n
-    lane, l4c, lq4, e16, kL, kR, k0, k1, lane2 = [T.cF[:, i:i + 1] for i in range(9)]
+    lane, l4c, lq4, e16, kL, kR, k0, kP, kH, kC = [T.cF[:, i:i + 1] for i in range(10)]
     sm = lambda i: T.sm[:, 24 * i:24 * i + 24]
     keys = lambda s, n: " ".join(s + str(i) for i in range(n))
-    XA = keys("Xa", 4)
+    XA = " ".join(keys("X" + c, 4) for c in "abc")
+    PARTS = ((128, 256), (256, C), (0, 128))
     wU, wB, wV = T.UV[:, UU:UU + 400], T.UV[:, TB:TB + 32], T.UV[:, VV:VV + 400]
 
-    dma("y", "dxa", T.X[:, 512:], T.x[:, 512:], "", "Xa0 Xa1")
+    dma("y", "dx0", T.X[:, 512:1024], T.x[:, 512:1024], "", keys("Xa", 4))
     dma("s", "du", T.ut[:], T.u[:], "", "ut")
-    dma("y", "dxb", T.X[:, 0:512], T.x[:, 0:512], "", "Xa2 Xa3 Xb")
-    dma("y", "dwc", T.wq[:].bitcast(dt.uint8), T.wc[:], "Xb", "wq")
-    dma("y", "dws", T.wsp[:], T.ws[:], "Xb", "wsp")
-    dma("y", "dv", T.vt[:], T.v[:], "Xb", "vt")
+    dma("y", "dx1", T.X[:, 1024:], T.x[:, 1024:], "", keys("Xb", 4))
+    dma("s", "dx2", T.X[:, 0:512], T.x[:, 0:512], "", keys("Xc", 4))
+    dma("y", "dwc", T.wq[:].bitcast(dt.uint8), T.wc[:], "Xc0", "wq")
+    dma("y", "dws", T.wsp[:], T.ws[:], "Xc0", "wsp")
+    dma("y", "dv", T.vt[:], T.v[:], "Xc0", "vt")
 
     op("g", "iota", (T.cI[:, 0:1], [[0, 1]], 0, 1), "", "cI0", 157)
     iota(T.cI[:, 16:32], [[1, 2], [16, 8]], 0, "cIu", 16, whole=True)
@@ -129,23 +134,24 @@ def rank_program(g, core, T, topo):
     iota(T.cc[:], [[-1, 2], [0, NB]], 1, "cc", 48)
     iota(T.base[:, 0:24], [[32, NB]], 32, "base0", 24)
     iota(T.base[:, 24:48], [[-32, NB]], 32 * NB, "base1", 24)
-    for i, (a, pat, b0) in enumerate(((0, [[25, 12]], 328), (12, [[-24, 12]], 591), (24, [[24, 12]], 23), (36, [[-25, 12]], 299),
-                                      (48, [[32, 2], [1, 12]], 0), (72, [[0, 8]], 0))):
-        iota(T.ER[:, a:(80 if a == 72 else 72 if a == 48 else a + 12)], pat, b0, "ER%d" % i, 12)
-    iota(T.HI[:, 0:25], [[-1, 25]], NB, "HI0 HI1", 25, whole=True)
+    for i, (a, b, pat, b0) in enumerate(((0, 12, [[25, 12]], 328), (12, 24, [[-24, 12]], 591), (24, 36, [[24, 12]], 23),
+                                         (36, 48, [[-25, 12]], 299), (48, 72, [[32, 2], [1, 12]], 0), (72, 80, [[0, 8]], 0))):
+        iota(T.ER[:, a:b], pat, b0, "ER%d" % i, b - a)
+    iota(T.sm[:, 0:26], [[1, 13], [0, 2]], 0, "sm0 sm1", 26)
+    iota(T.sm[:, 48:74], [[0, 13], [511, 2]], 1, "sm2 sm3", 26)
     iota(T.OH[:], [[0, 400]], 0, "OH", 400)
     iota(T.ID[:], [[-1, 768]], 0, "ID", 768)
     iota(T.arow[:], [[1, C]], -192, "arow", C)
     iota(T.GL[:, 0:2], [[448, 2]], -256, "GL0", 2)
     iota(T.GR[:, 0:2], [[448, 2]], -256, "GR0", 2)
-    v("set", (T.one[:], 1.0), "", "one", 256)
-    v("set", (T.t32[:], 32.0), "", "t32", 304)
-    v("set", (T.tW[:], 0.0), "", "zW", 256)
+    v("set", (T.one[:], 1.0), "", "one", 304)
+    act(T.t32[:], T.one[:], "one", "t32", 608, scale=32.0)
+    act(T.tW[:], T.one[:, 0:512], "one", "zW", 512, scale=0.0)
     v("set", (T.UV[:, 0:16], BIG), "", "pad0")
     v("set", (T.UV[:, TB:VV + 16], BIG), "", "TBm pad1")
     v("set", (T.ID[:, 0:1], EPS), "", "ID")
-    v("ts", (T.DD[:, 0:C], T.one[:, 0:C], 0.0, None, OP.mult), "one", "DD", 192)
-    v("ts", (T.DD[:, C:], T.one[:, 0:C], 0.0, None, OP.mult), "one", "DD1", 192)
+    for h in range(2):
+        sel(T.DD[:, C * h:C * h + C], T.one[:, 0:C], [[0, C]], OP.is_gt, 0, 0, "one", "DD" + "1" * h, C)
     sel(T.seg[:], T.one[:, 0:C], [[0, NB], [1, 16]], OP.not_equal, 0, 0, "one", "seg", C)
     sel(T.junk[:, 0:128], T.one[:, 0:128], [[-16, 8], [0, 16]], OP.is_ge, 0, 1, "one", "junk0", 128)
     sel(T.BD[:], T.junk[:, 0:128], [[16, 8], [0, 16]], OP.is_ge, 15, -1, "junk0", "BD", 128)
@@ -165,7 +171,7 @@ def rank_program(g, core, T, topo):
         one = T.PP[:, 16 * i + col:16 * i + col + 1]
         v("ts", (one, one, BIG, None, OP.add), "PP%d" % i, "PP%d" % i)
     v("ts", (T.PP[:, 32:48], T.dm[:, 0:16], 0.0, 512.0, OP.is_equal, OP.mult), "dm0", "PP2")
-    v("ts", (T.PP[:, 32:33], T.PP[:, 32:33], T.PP[:, 47:48], -1024.0, OP.subtract, OP.add), "PP2", "PP2")
+    v("ts", (T.PP[:, 32:33], T.PP[:, 32:33], -1024.0, None, OP.add), "PP2", "PP2")
     v("ts", (T.PP[:, 64:96], T.dm[:], 0.0, 512.0, OP.is_equal, OP.mult), "dm0 dm1", "PP4")
     v("ts", (T.tm[:], T.dm[:], -1.0, -1024.0, OP.is_equal, OP.mult), "dm0 dm1", "tm0 tm1")
     v("tt", (T.PP[:, 64:96], T.PP[:, 64:96], T.tm[:], OP.add), "PP4 tm0 tm1", "PP4")
@@ -175,20 +181,20 @@ def rank_program(g, core, T, topo):
         act(T[name][:], T.PP[:, 16 * i:16 * i + 16].indirect(T.rep[:, 0:n // 16]), key + " rep", name + (" cx1" if name == "cx" else ""), gs(n), scale=sc)
     v("copy", (T.c4[:], T.c3[:]), "c3", "c4", 192)
     v("ts", (T.c4[:, 0::16], T.c3[:, 0::16], -512.0, 512.0, OP.is_equal, OP.mult), "c3", "c4")
-    v("ts", (k0, T.PP[:, 95:96], -1.0, KX - 512.0 + 30.0, OP.mult, OP.add), "PP4", "k0")
-    v("ts", (k1, T.PP[:, 95:96], -1.0, KX - 512.0 - 2.0, OP.mult, OP.add), "PP4", "k1")
-    v("ts", (kL, lane, -2.0, k0, OP.mult, OP.add), "lane k0", "kL")
-    v("ts", (kR, lane, 2.0, k1, OP.mult, OP.add), "lane k1", "kR")
+    act(kP, T.PP[:, 47:48], "PP2", "kP", f=AF.Identity, scale=-1.0, bias=KX)
+    act(kH, T.PP[:, 47:48], "PP2", "kH", f=AF.Identity, scale=-0.5, bias=KX / 2)
+    act(kC, T.PP[:, 47:48], "PP2", "kC", f=AF.Identity, scale=2.0, bias=1559.0 - 2 * KX)
+    act(k0, T.PP[:, 95:96], "PP4 kP", "k0", f=AF.Identity, scale=-1.0, bias=kP)
+    v("ts", (kL, T.dm[:, 15:16], 2.0, k0, OP.mult, OP.add), "dm0 k0", "kL0")
+    v("ts", (kR, T.dm[:, 1:2], -2.0, k0, OP.mult, OP.add), "dm0 k0", "kR0")
+    v("ts", (T.cF[:, 4:6], T.cF[:, 4:6], -512.0, None, OP.add), "kL0 kR0", "kL kR")
     v("scan", (T.ERd[:], T.ER[:], T.c5[:, 0:80], -5000.0, OP.max, OP.add), keys("ER", 6) + " c5", "ERd", 80)
     v("ts", (T.lE[:, 0:3], T.ERd[:, 15:48:16], 2048.0, None, OP.add), "ERd", "lE")
     v("ts", (T.lE[:, 4:6], T.ERd[:, 63::16], 2048.0, e16, OP.add, OP.add), "ERd e16", "lT")
     v("ts", (T.aW[:, 24:48], T.aW[:, 0:24], lane, 0.5, OP.add, OP.add), "aW0 lane", "aW1")
     v("tt", (T.c5[:, 15::16], T.c5[:, 15::16], T.aW[:, 24:48], OP.add), "c5 aW1", "c5")
-    v("ts", (lane2, lane, 2.0, None, OP.mult), "lane", "lane2")
-    v("ts", (T.sm[:, 0:25], T.HI[:, 0:25], lane2, 0.0, OP.subtract, OP.is_equal), "HI0 lane2", "sm0 sm1")
-    v("ts", (T.sm[:, 48:73], T.HI[:, 0:25], lane2, 1.0, OP.subtract, OP.is_equal), "HI0 lane2", "sm2 sm3")
-    v("ts", (T.sm[:, 96:121], T.sm[:, 48:73], 512.0, None, OP.mult), "sm2 sm3", "sm4 sm5")
-    v("tt", (T.OH[:, 15::16], T.sm[:, 0:25], T.sm[:, 96:121], OP.add), "sm0 sm1 sm4 sm5 OH", "OH")
+    v("ts", (T.sm[:, 0:26], T.sm[:, 0:26], lane, None, OP.is_equal), "sm0 sm1 lane", "sm0 sm1")
+    v("tt", (T.OH[:, 15::16], T.sm[:, 24::-1], T.sm[:, 72:47:-1], OP.mult), "sm0 sm1 sm2 sm3 OH", "OH")
     Jc = lambda i: T.J[:, 20 * i:20 * i + 20]
     Ji = T.cI[:, 40:60]
     v("ts", (Jc(1), Jc(0), lane, None, OP.add), "J0 lane", "J1")
@@ -205,8 +211,8 @@ def rank_program(g, core, T, topo):
     v("ts", (T.lBM[:, 0:20], Jc(5), -1.0, 25.0, OP.mult, OP.add), "J5", "lBM0")
     v("copy", (T.lBM[:, 20:40], Jc(5)), "J5", "lBM1")
     for s in range(4):
-        act(T.tW[:, 5 * s::16], T.BD[:, s::4], "BD zW", "tW%d" % s, 64, scale=2.0)
-        sel(T.tE[:, 512 * s:512 * s + 512], T.one[:], [[-1, 512]], OP.is_equal, s, 4, "one", "tE%d" % s, 512)
+        act(T.tW[:, 5 * s::16], T.BD[:, s::4], "BD zW", "tW%d" % s, scale=2.0)
+        sel(T.tE[:, 512 * s:512 * s + 512], T.one[:, 0:512], [[-1, 512]], OP.is_equal, s, 4, "one", "tE%d" % s, 512)
     v("q", (T.kqW[:], T.ksW[:], T.tW[:]), keys("tW", 4), "kW", qc(128))
     v("q", (T.kqE[:], T.ksE[:], T.tE[:]), keys("tE", 4), "kE", qc(512))
 
@@ -216,47 +222,48 @@ def rank_program(g, core, T, topo):
         off = T.upk[:, 8 * i:8 * i + 8]
         v("copy", (T.qp[:, 128 * i:128 * i + 128].bitcast(dt.uint32), T.qu[:].bitcast(dt.uint32).indirect(off)), "qu upk", "qp%d" % i, gv(128))
         act(T.sp[:, 128 * i:128 * i + 128], T.su[:].indirect(off), "qu upk", "sp%d" % i, gs(128))
-    v("q", (T.qx0[:, 128:], T.sx0[:, 128:], T.X[:, 512:]), "Xa0", "qx0a", qc(256))
-    v("q", (T.qx0[:, 0:128], T.sx0[:, 0:128], T.X[:, 0:512]), "Xb", "qx0b", qc(128))
+    for (a, b), c in zip(PARTS, "abc"):
+        v("q", (T.qx0[:, a:b], T.sx0[:, a:b], T.X[:, 4 * a:4 * b]), "X%s0" % c, "qx0" + c, qc(128))
 
+    first = site[0]
     for t in range(R):
+        site[0] = first
         qx, sx, lq, ls = [T[n + str(t)] for n in ("qx", "sx", "lq", "ls")]
-        kx = "qx%da qx%db" % (t, t)
+        kx = "qx%da qx%db qx%dc" % (t, t, t)
         send(lq[:].bitcast(dt.uint8), qx[:].bitcast(dt.uint8), "aq%d" % t, kx, "sent0")
         send(ls[:], sx[:], "aq%d" % t, kx, "sent1")
         landed("aq%d" % t, 2 * n_in, "sent0 sent1", "qL%d" % t, 4000.0)
-        for p, a, b, bs, bd in (("a", 128, C, 1, 3), ("b", 0, 128, 4, 5)):
+        mm(1, C, T.qp[:, 128:], T.sp[:, 128:], qx[:], sx[:], True, True, "qp1 sp1 " + kx)
+        act(T.A[:, 2 * C:], bank(1), "#1", "A2", C, f=AF.Sign)
+        for (a, b), p, bs in zip(PARTS, "abc", (0, 6, 2)):
             n = b - a
-            for bk, i in ((bs, 0), (bd, 1)):
-                mm(bk, n, T.qp[:, 128 * i:128 * i + 128], T.sp[:, 128 * i:128 * i + 128], qx[:, a:b], sx[:, a:b], True, True,
-                   "qp%d sp%d qx%d%s" % (i, i, t, p))
+            mm(bs, n, T.qp[:, 0:128], T.sp[:, 0:128], qx[:, a:b], sx[:, a:b], True, True, "qp0 sp0 qx%d%s" % (t, p))
             ks = "#%d" % bs
             va, ua = VV + 16 + C - b, UU + 16 + a
-            act(T.A[:, 2 * C + a:2 * C + b], bank(bd, n), "#%d" % bd, "A2" + p, n, f=AF.Sign)
             v("scan", (T.UV[:, va:va + n], rev(T.c1, a, b), rbank(bs, n), 0.0, OP.add, OP.max), "c1 " + ks, "V" + p, n)
             v("scan", (T.UV[:, ua:ua + n], T.c2[:, a:b], bank(bs, n), 0.0, OP.add, OP.max), "c2 " + ks, "U" + p, n)
             v("tt", (T.A[:, C + a:C + b], bank(bs, n), rev(T.UV, va, va + n), OP.is_ge), ks + " V" + p, "A0" + p, n)
             v("tt", (T.A[:, a + 1:b], bank(bs, n, 1), T.UV[:, ua:ua + n - 1], OP.is_gt), ks + " U" + p, "A1" + p, n)
             act(T.S[:, a:b], bank(bs, n), ks, "S" + p, n)
-        kU, kV = "Ua Ub pad0", "Va Vb pad1"
-        v("tt", (T.UV[:, TB + 1:TB + 25], T.UV[:, VV + 399:VV + 15:-16], T.UV[:, UU + 31:UU + 400:16], OP.max), "Va Vb Ua Ub", "TBm")
+        kU, kV = "Ua Ub Uc pad0", "Va Vb Vc pad1"
+        v("tt", (T.UV[:, TB + 1:TB + 25], T.UV[:, VV + 399:VV + 15:-16], T.UV[:, UU + 31:UU + 400:16], OP.max), "Va Vb Vc Ua Ub Uc", "TBm")
         for h in range(2):
             act(T.BMx[:, 304 * h:304 * h + 304], wB.indirect(T.lBM[:, 20 * h:20 * h + 19]), "TBm lBM%d" % h, "BMx%d" % h, gs(304))
-        v("set", (T.A[:, 0:C:16], 0.0), "", "A1a A1b")
-        v("scan", (T.CNT[:, 0:C], T.seg[:], T.A[:, C:2 * C], 0.0, OP.mult, OP.add), "seg A0a A0b", "CL", 192)
-        v("scan", (T.CNT[:, C:], T.seg[:], T.A[:, 0:C], 0.0, OP.mult, OP.add), "seg A1a A1b", "CR", 192)
-        v("tt", (T.m[:], T.CNT[:, 15::16], T.cc[:], OP.is_equal), "CL CR cc", "m", 96)
+        act(T.A[:, 0:C:16], T.one[:, 0:NB], "one", "A1a A1b A1c", scale=0.0)
+        v("scan", (T.CNT[:, 0:C], T.seg[:], T.A[:, C:2 * C], 0.0, OP.mult, OP.add), "seg A0a A0b A0c", "CL", 192)
+        v("scan", (T.CNT[:, C:], T.seg[:], T.A[:, 0:C], 0.0, OP.mult, OP.add), "seg A1a A1b A1c", "CR", 192)
+        v("tt", (T.m[:], T.CNT[:, 15::16], T.cc[:], OP.is_equal), "CL CR cc", "m")
         v("copy", (T.ML[:], T.m[:]), "m", "ML")
-        v("tt", (T.mb[:], T.m[:], T.base[:], OP.mult), "m base0 base1", "mb", 96)
-        v("tt", (T.corr[:], T.base[:], T.mb[:], OP.subtract), "mb base0 base1", "corr", 96)
+        v("tt", (T.mb[:], T.m[:], T.base[:], OP.mult), "m base0 base1", "mb")
+        v("tt", (T.corr[:], T.base[:], T.mb[:], OP.subtract), "mb base0 base1", "corr")
         v("tt", (sm(0), T.CNT[:, C + 15::16], T.CNT[:, 15:C:16], OP.subtract), "CL CR", "sm0")
         for h in (1, 0):
             act(T.FR[:, C * h:C * h + C], T.FT[:].indirect(T.ML[:, 24 * h:24 * h + 24]), "FT ML", "FR%d" % h, gs(C))
-        v("q", (T.qa[:], T.sa[:], T.A[:]), "A0a A0b A1a A1b A2a A2b", "qa", qc(288))
-        mm(0, 192, T.kqW[:], T.ksW[:], T.qa[:, 0:192], T.sa[:, 0:192], True, False, "kW qa")
-        mm(2, 128, T.kqW[:], T.ksW[:], T.qa[:, 160:288], T.sa[:, 160:288], True, True, "kW qa")
-        v("scan", (T.fr[:], bank(2, 128, 32), T.c6[:, 0:96], -5000.0, OP.max, OP.add), "#2 c6", "fr", 96)
-        v("ts", (sm(1), T.fr[:, 3::4], -500.0, -5000.0, OP.is_le, OP.mult), "fr", "sm1")
+        v("q", (T.qa[:], T.sa[:], T.A[:]), "A0a A0b A0c A1a A1b A1c A2", "qa", qc(288))
+        mm(4, 192, T.kqW[:], T.ksW[:], T.qa[:, 0:192], T.sa[:, 0:192], True, False, "kW qa")
+        mm(5, 128, T.kqW[:], T.ksW[:], T.qa[:, 160:288], T.sa[:, 160:288], True, True, "kW qa")
+        v("scan", (T.fr[:], bank(5, 128, 32), T.c6[:, 0:96], -5000.0, OP.max, OP.add), "#5 c6", "fr", 96)
+        act(sm(1), T.fr[:, 3::4], "fr", "sm1", f=AF.Relu, scale=-100.0, bias=-49000.0)
         v("tt", (T.cov[:, 0:304], wU.indirect(T.lTH[:, 0:19]), T.BMx[:, 0:304], OP.is_ge), kU + " lTH BMx0", "cov0", gv(304))
         v("tt", (T.cov[:, 304:608], wV.indirect(T.lTH[:, 0:19]), T.BMx[:, 304:608], OP.is_gt), kV + " lTH BMx1", "cov1", gv(304))
         v("scan", (T.run[:], T.t32[:], T.cov[:], 0.0, OP.add, OP.mult), "t32 cov0 cov1", "run", 304)
@@ -264,17 +271,17 @@ def rank_program(g, core, T, topo):
         v("ts", (T.ix[:], T.E[:], -0.5, -1.0, OP.mult, OP.add), "E", "ix")
         v("ts", (T.cx[:, 3:96:4], T.E[:, 0:24], 0.0, kL, OP.min, OP.add), "E kL", "cx")
         v("ts", (T.cx[:, 99::4], T.E[:, 24:48], 0.0, kR, OP.min, OP.add), "E kR", "cx1")
-        v("tt", (T.B[:, 0:C], wU.indirect(T.ix[:, 0:24]), T.S[:], OP.is_lt), kU + " ix Sa Sb", "B0", gv(C))
-        v("tt", (T.B[:, C:], wV.indirect(T.ix[:, 24:48]), T.S[:], OP.is_le), kV + " ix Sa Sb", "B1", gv(C))
+        v("tt", (T.B[:, 0:C], wU.indirect(T.ix[:, 0:24]), T.S[:], OP.is_lt), kU + " ix Sa Sb Sc", "B0", gv(C))
+        v("tt", (T.B[:, C:], wV.indirect(T.ix[:, 24:48]), T.S[:], OP.is_le), kV + " ix Sa Sb Sc", "B1", gv(C))
         v("q", (T.qb[:], T.sb[:], T.B[:]), "B0 B1", "qb", qc(192))
-        mm(0, 192, T.kqW[:], T.ksW[:], T.qb[:], T.sb[:], False, True, "kW qb")
-        v("scan", (T.xx[:], bank(0, 192), T.cx[:], 5000.0, OP.min, OP.add), "#0 cx cx1", "xx", 192)
-        v("ts", (T.lp[:], T.xx[:, 3::4], -0.5, KX / 2, OP.mult, OP.add), "xx", "lp")
-        v("tt", (T.P2[:], T.xx[:, 3::4], T.corr[:], OP.subtract), "xx corr", "P2", 96)
+        mm(4, 192, T.kqW[:], T.ksW[:], T.qb[:], T.sb[:], False, True, "kW qb")
+        v("scan", (T.xx[:], bank(4, 192), T.cx[:], 5000.0, OP.min, OP.add), "#4 cx cx1", "xx", 192)
+        v("ts", (T.lp[:], T.xx[:, 3::4], -0.5, kH, OP.mult, OP.add), "xx kH", "lp")
+        v("tt", (T.P2[:], T.xx[:, 3::4], T.corr[:], OP.subtract), "xx corr", "P2")
         for i, a in ((0, 24), (1, 0)):
             act(T.junk[:, C * i:C * i + C], T.OH[:].indirect(T.ix[:, a:a + 24]), "OH ix", "junk%d acc%d" % (i, i), gs(C) + 24,
                 accum_out=T.acc[:, i:i + 1])
-            v("ts", (T.rp[:, 32 * i:32 * i + 32], T.one[:, 0:32], T.acc[:, i:i + 1], None, OP.mult), "one acc%d" % i, "rp%d" % i)
+            act(T.rp[:, 32 * i:32 * i + 32], T.one[:, 0:32], "one acc%d" % i, "rp%d" % i, f=AF.Identity, scale=T.acc[:, i:i + 1])
         v("tr", (T.rt[:], T.rp[:]), "rp0 rp1", "rt")
         v("copy", (T.WI[:], T.rt[:].indirect(T.lE[:, 4:6])), "rt lT", "WI", gv(32))
         v("ts", (T.HI[:, 0::2], T.WI[:], 511, None, OP.bitwise_and), "WI", "HI0")
@@ -283,27 +290,24 @@ def rank_program(g, core, T, topo):
         v("scan", (T.GR[:, 2:C + 2], T.DD[:, C:], rev(T.FR), 192.0, OP.add, OP.subtract), "DD FR0", "GR", 192)
         v("scan", (T.GL[:, 2:C + 2], T.DD[:, 0:C], T.FR[:, C:], 192.0, OP.add, OP.subtract), "DD FR1", "GL", 192)
         act(T.Gg[:, C:], T.GR[:, 0:C + 2].indirect(T.lp[:, 24:48]), "GR GR0 lp", "GgR", gs(C))
-        if GGV:
-            v("copy", (T.Gg[:, 0:C], T.GL[:, 0:C + 2].indirect(T.lp[:, 0:24])), "GL GL0 lp", "GgL", gv(C))
-        else:
-            act(T.Gg[:, 0:C], T.GL[:, 0:C + 2].indirect(T.lp[:, 0:24]), "GL GL0 lp", "GgL", gs(C))
+        v("copy", (T.Gg[:, 0:C], T.GL[:, 0:C + 2].indirect(T.lp[:, 0:24])), "GL GL0 lp", "GgL", gv(C))
         v("scan", (rev(T.mR), rev(T.Gg, C, 2 * C), rev(T.c3), -2000.0, OP.max, OP.add), "GgR c3", "mR", 192)
         pL, pR = T.P2[:, 0:24], T.P2[:, 24:48]
-        v("tt", (sm(2), sm(0), pL, OP.subtract), "sm0 P2", "sm2")
+        v("tt", (T.c4[:, 15::16], sm(0), pL, OP.subtract), "sm0 P2", "c4")
         v("tt", (sm(3), pL, pR, OP.add), "P2", "sm3")
         v("tt", (sm(4), pR, pL, OP.subtract), "P2", "sm4")
-        v("tt", (sm(5), sm(4), sm(1), OP.add), "sm4 sm1", "sm5")
+        v("tt", (sm(5), sm(4), sm(1), OP.subtract), "sm4 sm1", "sm5")
         v("ts", (T.zi[:], sm(5), 0.5, 384.0, OP.mult, OP.add), "sm5", "zi")
         act(T.z[:], T.ID[:].indirect(T.zi[:]), "ID zi", "z", gs(C))
-        v("tt", (T.c4[:, 15::16], sm(2), T.mR[:, 0::16], OP.subtract), "sm2 mR", "c4")
         v("scan", (T.mL[:], T.Gg[:, 0:C], T.c4[:], -2000.0, OP.max, OP.add), "GgL c4", "mL", 192)
-        v("ts", (T.oc16[:, 0:24], T.mL[:, 15::16], 1100.0, None, OP.add), "mL", "op16")
-        v("tt", (sm(6), sm(3), T.mL[:, 15::16], OP.add), "sm3 mL", "sm6")
-        v("ts", (T.oc16[:, 24:48], sm(6), 1871.0 - 2 * KX, None, OP.add), "sm6", "cl16")
-        DB, OB = (0, 2, 6, 7), (1, 3, 4, 5)
-        for b in range(4):
-            mm(DB[b], C, T.kqE[:, 128 * b:128 * b + 128], T.ksE[:, 128 * b:128 * b + 128], lq[:], ls[:], True, True, "kE qL%d" % t)
-            act(T.Dd[:, b::4], bank(DB[b]), "#%d op16" % DB[b], "Dd%d" % b, C)
+        v("tt", (sm(6), sm(3), T.mR[:, 0::16], OP.subtract), "sm3 mR", "sm6")
+        v("tt", (sm(2), T.mL[:, 15::16], T.mR[:, 0::16], OP.subtract), "mL mR", "sm2")
+        v("tt", (sm(8), T.mL[:, 15::16], sm(6), OP.add), "mL sm6", "sm8")
+        v("ts", (T.oc16[:, 0:24], sm(2), 788.0, None, OP.add), "sm2", "op16")
+        v("ts", (T.oc16[:, 24:48], sm(8), kC, None, OP.add), "sm8 kC", "cl16")
+        for b, bk in enumerate((0, 1, 6, 7)):
+            mm(bk, C, T.kqE[:, 128 * b:128 * b + 128], T.ksE[:, 128 * b:128 * b + 128], lq[:], ls[:], True, True, "kE lp qL%d" % t)
+            act(T.Dd[:, b::4], bank(bk), "#%d op16" % bk, "Dd%d" % b, C)
         v("copy", (T.EW[:].indirect(T.oc16[:, 0:24]), T.z[:]), "op16 z", "EW", sv(C))
         v("copy", (T.EW[:].indirect(T.oc16[:, 24:48]), T.z[:]), "cl16 z", "EW", sv(C))
         v("ts", (T.PH[:, 0:C], T.EW[:, 0:C], 1 / EPS, -1.0, OP.mult, OP.max), "EW", "PH0", C)
@@ -312,48 +316,62 @@ def rank_program(g, core, T, topo):
         act(T.Yg[:, 192:], T.Y[:].indirect(T.oc16[:, 12:24]), "Y op16", "Yg1", gs(192))
         v("copy", (T.Yg[:, 0:192], T.Y[:].indirect(T.oc16[:, 0:12])), "Y op16", "Yg0", gv(192))
         v("scan", (T.dg[:], T.Yg[:], T.c5[:], -5000.0, OP.max, OP.add), "Yg0 Yg1 c5", "dg", C)
-        act(sm(7), T.dg[:, 15::16], "dg", "sm7", 64, f=AF.Abs, bias=2048.0)
+        act(sm(7), T.dg[:, 15::16], "dg", "sm7", f=AF.Abs, bias=2048.0)
         v("ts", (T.at[:], sm(7), -0.5, None, OP.add), "sm7", "at")
         v("copy", (T.O[:].indirect(T.at[:, 0:24]), T.arow[:]), "at arow", "O", sv(C))
         ob, ll = T.ob[:, 24 * t:24 * t + 24], T.ll[:, 24 * t:24 * t + 24]
         v("scan", (T.o4[:, H:], T.O[:, H:], T.c6[:, H:], -2000.0, OP.max, OP.add), "O c6", "o4b")
         v("ts", (ob, T.o4[:, H + 3::4], 4.0, l4c, OP.mult, OP.add), "o4b l4c", "ob%d" % t)
         send(ll, ob, "al%d" % t, "ob%d" % t, "sent2")
-        landed("al%d" % t, n_in, "sent2", "ll%d" % t, 2800.0)
+        landed("al%d" % t, n_in, "sent2", "ll%d" % t, LL)
         v("scan", (T.o4[:, 0:H], T.O[:, 0:H], T.c6[:, 0:H], -2000.0, OP.max, OP.add), "O c6", "o4a", H // 2)
         v("ts", (T.oo[:], T.o4[:, 3:H:4], 4.0, l4c, OP.mult, OP.add), "o4a l4c", "oo")
         if t == R - 1:
             act(T.O32[:], T.O[:], "O", "O32", C, f=AF.Identity, bias=192.0)
             dma("y", "dol", T.ol[:], T.O32[0:128:16, :], "O32", "")
-        act(T.Z[:, 960:], T.X[:].indirect(T.oo[:, 36:72]), XA + " Xb oo", "Z2", gs(576))
-        v("copy", (T.Z[:, 384:960], T.X[:].indirect(T.oo[:, 0:36])), XA + " Xb oo", "Z1", gv(576))
-        act(T.Z[:, 0:384], T.Dd[:].indirect(ll), keys("Dd", 4) + " ll%d" % t, "Z0", gs(C))
-        v("q", (T.qz[:, K:], T.sz[:, K:], T.Z[:, 4 * K:]), "Z1 Z2", "qz", qc(H))
         wv = lambda b: (T.wq[:, 128 * b:128 * b + 128], T.wsp[:, 128 * b:128 * b + 128])
-        v("ts", (T.Z64[:, 384:1152], T.Z[:, 384:1152], 64.0, None, OP.mult), "Z1 Z2", "Z64a", 384)
-        act(T.Z64[:, 1152:], T.Z[:, 1152:], "Z2", "Z64c", 384, scale=64.0)
-        for b in range(4):
-            mm(OB[b], H, *wv(b), T.qz[:, K:], T.sz[:, K:], True, True, "wq wsp qz")
-            v("tt", (T.X64[:, 4 * K + b::4], bank(OB[b], H), T.Z64[:, 4 * K + b::4], OP.add), "#%d Z64a Z64c" % OB[b], "X64a%d" % b, H)
-            act(T.X[:, 4 * K + b::4], T.X64[:, 4 * K + b::4], "X64a%d" % b, "Xa%d" % b, H, scale=0.015625)
-        v("q", (T.qzb[:], T.szb[:], T.Z[:, 0:512]), "Z0 Z1", "qzb", qc(128))
-        v("ts", (T.Z64[:, 0:4 * K], T.Z[:, 0:4 * K], 64.0, None, OP.mult), "Z0", "Z64b", 2 * K)
-        for b in range(4):
-            mm(DB[b], 128, *wv(b), T.qzb[:], T.szb[:], True, True, "wq wsp qzb")
-            v("tt", (T.X64[:, b:4 * K:4], bank(DB[b], K), T.Z64[:, b:4 * K:4], OP.add), "#%d Z64b" % DB[b], "X64b%d" % b, K)
         qn, sn = T["qx%d" % (t + 1)], T["sx%d" % (t + 1)]
-        v("q", (qn[:, 128:], sn[:, 128:], T.X[:, 512:]), XA, "qx%da" % (t + 1), qc(256))
-        v("ts", (T.X[:, 0:4 * K], T.X64[:, 0:4 * K], 0.015625, None, OP.mult), keys("X64b", 4), "Xb", 2 * K)
-        v("q", (qn[:, 0:128], sn[:, 0:128], T.X[:, 0:512]), XA + " Xb", "qx%db" % (t + 1), qc(128))
+        for c, a, e, cut in (("a", K, 256, CUT[0]), ("b", 256, C, CUT[1])):
+            m0, m1, m2 = (a - K) // 4, (cut - K) // 4, (e - K) // 4
+            v("copy", (T.Z[:, 4 * a:4 * cut], T.X[:].indirect(T.oo[:, m0:m1])), XA + " oo", "Z%s0" % c, gv(4 * (cut - a)))
+            act(T.Z[:, 4 * cut:4 * e], T.X[:].indirect(T.oo[:, m1:m2]), XA + " oo", "Z%s1" % c, gs(4 * (e - cut)))
+            v("q", (T.qz[:, a:e], T.sz[:, a:e], T.Z[:, 4 * a:4 * e]), "Z%s0 Z%s1" % (c, c), "qz" + c, qc(e - a))
+        h = 12 if t == R - 1 else 0
+        act(T.Z[:, 16 * h:4 * K], T.Dd[:].indirect(T.ll[:, 24 * t + h:24 * t + 24]), keys("Dd", 4) + " ll%d" % t, "Zc1" if h else "Zc0 Zc1", gs(C - 16 * h))
+        if h:
+            v("copy", (T.Z[:, 0:16 * h], T.Dd[:].indirect(T.ll[:, 24 * t:24 * t + h])), keys("Dd", 4) + " ll%d" % t, "Zc0", gv(16 * h))
+        v("q", (T.qzb[:], T.szb[:], T.Z[:, 0:512]), "Zc0 Zc1 Za0 Za1", "qzc", qc(128))
+        for c, a, e, b0 in (("a", K, 256, 0), ("b", 256, C, 4), ("c", 0, K, 2)):
+            n, kz = e - a, "Z%s0 Z%s1" % (c, c)
+            zq, zs = (T.qzb[:], T.szb[:]) if c == "c" else (T.qz[:, a:e], T.sz[:, a:e])
+            if c in Z64S:
+                act(T.Z64[:, 4 * a:4 * e], T.Z[:, 4 * a:4 * e], kz, "Z64" + c, 4 * n, scale=64.0)
+            else:
+                v("ts", (T.Z64[:, 4 * a:4 * e], T.Z[:, 4 * a:4 * e], 64.0, None, OP.mult), kz, "Z64" + c, 2 * n)
+            for b in range(4):
+                mm(b0 + b, max(n, 128), *wv(b), zq, zs, True, True, "wq wsp qz" + c)
+                v("tt", (T.X64[:, 4 * a + b:4 * e:4], bank(b0 + b, n), T.Z64[:, 4 * a + b:4 * e:4], OP.add), "#%d Z64%s" % (b0 + b, c), "X64%s%d" % (c, b), n)
+            if c in XV:
+                v("ts", (T.X[:, 4 * a:4 * e], T.X64[:, 4 * a:4 * e], 0.015625, None, OP.mult), keys("X64" + c, 4), keys("X" + c, 4), 2 * n)
+            else:
+                for b in range(4):
+                    act(T.X[:, 4 * a + b:4 * e:4], T.X64[:, 4 * a + b:4 * e:4], "X64%s%d" % (c, b), "X%s%d" % (c, b), n, scale=0.015625)
+        for (a, b), c in zip(PARTS, "abc"):
+            v("q", (qn[:, a:b], sn[:, a:b], T.X[:, 4 * a:4 * b]), keys("X" + c, 4) + (" " + keys("Xa", 4) if c == "c" else ""), "qx%d%s" % (t + 1, c), qc(128))
 
-    for p, a, b, bk in (("a", 128, C, 1), ("b", 0, 128, 4)):
+    site[0] += 8
+    for (a, b), p, bk in zip(PARTS, "abc", (0, 6, 2)):
         kx = "qx%d%s" % (R, p)
         mm(bk, b - a, T.qv[:], T.sv[:], T.qx3[:, a:b], T.sx3[:, a:b], True, True, "qv " + kx)
         dma("y", "doc", T.oc[:, 4 * a:4 * b], T.qx3[:, a:b].bitcast(dt.uint8), kx, "")
-        v("copy", (T.ys[:, a:b], bank(bk, b - a)), "#%d" % bk, "ys" + p, b - a)
-        dma("s", "dy", T.y[:, a:b], T.ys[:, a:b], "ys" + p, "")
+        if p == "c":
+            v("copy", (T.ys[:, a:b], bank(bk, b - a)), "#%d" % bk, "ys" + p, b - a)
+        else:
+            act(T.ys[:, a:b], bank(bk, b - a), "#%d" % bk, "ys" + p, b - a)
+    dma("s", "dy", T.y[:, 128:], T.ys[:, 128:], "ysa ysb", "")
+    dma("s", "dy", T.y[:, 0:128], T.ys[:, 0:128], "ysc", "")
     for k in range(4):
-        dma("ys"[k // 3], "dos", T.osc[4 * k:4 * k + 4, :], T.sx3[32 * k:32 * k + 4, :], "qx%da qx%db" % (R, R), "")
+        dma("ys"[k // 3], "dos", T.osc[4 * k:4 * k + 4, :], T.sx3[32 * k:32 * k + 4, :], "qx%da qx%db qx%dc" % (R, R, R), "")
 
     n = len(ops)
     ahead, users = [0.0] * n, [[] for _ in ops]
@@ -370,9 +388,9 @@ def rank_program(g, core, T, topo):
             at = {i: max(tm, free[ops[i]["q"]]) for i, tm in ready.items()}
             i0 = min(at, key=lambda i: (at[i], -ahead[i]))
             mine = [i for i in at if ops[i]["q"] == ops[i0]["q"]]
-            best = max([i for i in mine if at[i] <= at[i0] + 200.0], key=lambda i: ahead[i] + bias[i])
+            best = max([i for i in mine if at[i] <= at[i0] + 200.0], key=lambda i: ahead[i] + bias[ops[i]["site"]])
             fill = [i for i in mine if at[i] < at[best] and at[i] + ops[i]["busy"] <= at[best] + 60.0]
-            i = max(fill, key=lambda i: ahead[i] + bias[i]) if fill else best
+            i = max(fill, key=lambda i: ahead[i] + bias[ops[i]["site"]]) if fill else best
             del ready[i]
             order.append(i)
             free[ops[i]["q"]] = end[i] = at[i] + ops[i]["busy"]
@@ -380,21 +398,35 @@ def rank_program(g, core, T, topo):
                 left[j] -= 1
                 if not left[j]:
                     ready[j] = max(end[d] + (ops[d]["lag"] if w else 0.0) for d, w in ops[j]["deps"].items())
-        return max(end[i] + ops[i]["lag"] for i in range(n)), order
+        return order
+
+    def span(order):
+        total = 0.0
+        for a, b in LAGS:
+            free, end = {q: 0.0 for q in "vstgyx"}, [0.0] * n
+            for i in order:
+                o = ops[i]
+                at = max([free[o["q"]]] + [end[d] + (lag[d] * (a if lag[d] == LAG else b) if w else 0.0) for d, w in o["deps"].items()])
+                free[o["q"]] = end[i] = at + o["busy"]
+            total += max(end[i] + lag[i] * b for i in range(n))
+        return total
 
     if n not in ORDER:
-        seed, bias = 12345, [0.0] * n
-        span, order = lay_out(bias)
+        lag = [o["lag"] for o in ops]
+        seed, bias = SEED, [0.0] * site[0]
+        order = lay_out(bias)
+        best = span(order)
         for _ in range(TRIES):
             other = list(bias)
-            for _k in range(8):
+            for _k in range(MUT):
                 seed = (seed * 1103515245 + 12345) % 2147483648
-                i = (seed >> 8) % n
+                i = (seed >> 8) % len(bias)
                 seed = (seed * 1103515245 + 12345) % 2147483648
                 other[i] = ((seed >> 8) % 3001) - 1500.0
-            a, b = lay_out(other)
-            if a <= span:
-                span, order, bias = a, b, other
+            b = lay_out(other)
+            a = span(b)
+            if a <= best:
+                best, order, bias = a, b, other
         ORDER[n] = order
     total, known = {}, {q: {} for q in QS}
 
@@ -416,6 +448,3 @@ def rank_program(g, core, T, topo):
         total[o["sem"]] = o["count"] = total.get(o["sem"], 0) + o["inc"]
     for sem, val in total.items():
         wait("g", sem, val)
-
-
-GGV = False

from concourse.mybir import dt, AluOpType as OP, ActivationFunctionType as AF

C, K, R, N = 384, 96, 3, 4
NB, H = C // 16, C - K
F32, BF, F16, I32, U16, Q4, U8 = "float32", "bfloat16", "float16", "int32", "uint16", "float8_e4m3fn_x4", "uint8"
BIG, KX, EPS = 1e28, 1813.0, 2.0 ** -12
UU, TB, VV = 0, 400, 432

SCRATCH = {"ps": ("psum", [128, 4096], F32)}
for _d, _l in (
        (BF, "X:1536 X64:1536 Z:1536 Z64:1536 Dd:1536 ut:512 vt:512 tW:512 tE:2048 A:1152 B:768 one:608 t32:608 BD:128 seg:384 "
             "CNT:768 cov:608 run:608 junk:768 FT:16 FR:768 GL:400 GR:400 Gg:768 OH:400 c1:384 c2:384 c3:384 c6:384 O:384 arow:384 "
             "PH:768 base:48 cc:48"),
        (F16, "c4:384 mL:384 mR:384 DD:768 o4:384 m:48 mb:48 corr:48 P2:48 xx:192"),
        (Q4, "qu:128 qv:128 qp:256 wq:512 qz:384 qzb:128 kqW:128 kqE:512 qa:288 qb:192 qx0:384 qx1:384 qx2:384 qx3:384 lq0:384 lq1:384 lq2:384"),
        (U8, "su:128 sv:128 sp:256 wsp:512 sz:384 szb:128 ksW:128 ksE:512 sa:288 sb:192 sx0:384 sx1:384 sx2:384 sx3:384 ls0:384 ls1:384 ls2:384"),
        (I32, "cI:64 WI:32 HI:64"),
        (U16, "rep:24 upk:16 lBM:40 lTH:20 lE:6 ML:48 ix:48 lp:48 zi:24 oc16:48 at:24 oo:72 ob:72 ll:72"),
        (F32, "cF:16 dm:32 tm:32 PP:96 c5:384 cx:192 aW:48 J:160 ER:80 ERd:80 S:384 UV:832 BMx:608 "
              "E:48 acc:2 rp:64 rt:64 fr:96 sm:240 ID:768 z:384 EW:768 Y:768 Yg:384 dg:384 O32:384 ys:384")):
    for _e in _l.split():
        _n, _w = _e.split(":")
        SCRATCH[_n] = ("sbuf", [128, int(_w)], _d)

SEMAPHORES = ["v", "s", "t", "g", "dx0", "dx1", "dx2", "du", "dv", "dwc", "dws", "dy", "dol", "doc", "dos", "loc"] + \
             ["aq%d" % t for t in range(R)] + ["al%d" % t for t in range(R)]

GA, SC, LAG, DLAG, LL = 1.56, 3.8, 200.0, 2400.0, 2800.0
LAGS = ((0.7, 0.75), (1.15, 1.1))
ORDER, TRIES, SEED, MUT = {}, 4000, 12345, 4
CUT, Z64S, XV = (160, 304), "b", "bc"


def rank_program(g, core, T, topo):
    rank = T.rank_of(core)
    if rank is None:
        return
    nxt, prv = T.cores[(rank + 1) % N], T.cores[(rank - 1) % N]
    rid, pid = topo.addr(nxt)[0:2]
    mask = topo.mask(core, nxt)
    n_out, n_in = len(topo.engines(core, nxt)), len(topo.engines(prv, core))
    QS = {"v": g.vector, "s": g.scalar, "t": g.tensor, "g": g, "y": g.sync}
    ops, wrote, read, site = [], {}, {}, [0]

    def add(q, emit, r, w, busy, lag, sem, inc, acc=False):
        r, w = r.split(), w.split()
        deps = {}
        own = lambda i: ops[i]["q"] == q and ops[i]["sem"] == q == sem
        for k in r + w:
            if k in wrote:
                deps[wrote[k]] = deps.get(wrote[k], False) or not (acc and k in w)
        for k in w + [k for k in r if k[0] == "#"]:
            for i in read.get(k, []):
                if k in w or ops[i]["q"] != q:
                    deps[i] = deps.get(i, False) or not own(i)
        ops.append({"q": q, "emit": emit, "deps": deps, "busy": busy, "lag": lag, "sem": sem, "inc": inc, "site": site[0]})
        site[0] += 1
        for k in r:
            read.setdefault(k, []).append(len(ops) - 1)
        for k in w:
            wrote[k] = len(ops) - 1
            read[k] = []

    def op(q, name, args, r, w, c, acc=False, **kw):
        e = QS[q]
        call = {"copy": lambda: e.tensor_copy(*args), "tt": lambda: e.tensor_tensor(*args), "ts": lambda: e.tensor_scalar(*args),
                "scan": lambda: e.tensor_tensor_scan(*args), "set": lambda: e.memset(*args), "q": lambda: e.quantize_mx(*args),
                "tr": lambda: e.transpose(*args), "act": lambda: e.activation(*args, **kw), "mm": lambda: e.matmul_mx(*args),
                "iota": lambda: e.iota(*args, **kw), "sel": lambda: e.affine_select(*args)}[name]
        add(q, lambda: call().then_inc(T.sem[q], 1), r, w, max(c, 64) * 0.9, LAG, q, 1, acc)

    def dma(q, sem, out, in_, r, w):
        add(q, lambda: QS[q].dma_start(out, in_).then_inc(T.sem[sem], 16), r, w, 100.0, DLAG, sem, 16)

    def send(out, in_, sem, r, w):
        add("g", lambda: g.remote_dma(out, in_, T.sem[sem], T.sem.loc, pid, rid, mask), r, w, 300.0, 0.0, "loc", n_out)

    def landed(sem, n, r, w, lag):
        add("x", None, r, w, 0.0, lag, sem, n)

    def v(name, args, r, w, c=64):
        op("v", name, args, r, w, c)

    def act(out, in_, r, w, c=64, f=AF.Copy, **kw):
        op("s", "act", (out, in_, f), r, w, c, **kw)

    def iota(out, pat, base, w, c=32, whole=False):
        if whole:
            op("g", "iota", (out, pat, base, 0), "", w, 157 + 2 * c)
        else:
            op("g", "iota", (out, pat, base, 0), "", w, 157 + 2 * c, allow_small_or_imprecise_dtypes=True)

    def sel(out, in_, pat, cmp, base, cm, r, w, c):
        op("g", "sel", (out, in_, pat, cmp, 0.0, base, cm), r, w, 205 + 2 * c)

    def bank(b, n=C, a=0):
        return T.ps[:, 512 * b + a:512 * b + n]

    def rbank(b, n=C):
        return T.ps[:, 512 * b + n - 1:512 * b - 1:-1] if b else T.ps[:, n - 1::-1]

    def rev(t, a=0, b=C):
        return t[:, b - 1:a - 1:-1] if a else t[:, b - 1::-1]

    def mm(b, n, lq, ls, rq, rs, start, stop, r):
        op("t", "mm", (bank(b, n), lq, ls, rq, rs, start, stop), r, "#%d" % b, 0.7 * (n + 16), acc=not start)

    gv = lambda n: 60 + GA * n
    gs = lambda n: 78 + GA * n
    sv = lambda n: 60 + SC * n
    qc = lambda n: 15 + 1.06 * n
    lane, l4c, lq4, e16, kL, kR, k0, kP, kH, kC = [T.cF[:, i:i + 1] for i in range(10)]
    sm = lambda i: T.sm[:, 24 * i:24 * i + 24]
    keys = lambda s, n: " ".join(s + str(i) for i in range(n))
    XA = " ".join(keys("X" + c, 4) for c in "abc")
    PARTS = ((128, 256), (256, C), (0, 128))
    wU, wB, wV = T.UV[:, UU:UU + 400], T.UV[:, TB:TB + 32], T.UV[:, VV:VV + 400]

    dma("y", "dx0", T.X[:, 512:1024], T.x[:, 512:1024], "", keys("Xa", 4))
    dma("s", "du", T.ut[:], T.u[:], "", "ut")
    dma("y", "dx1", T.X[:, 1024:], T.x[:, 1024:], "", keys("Xb", 4))
    dma("s", "dx2", T.X[:, 0:512], T.x[:, 0:512], "", keys("Xc", 4))
    dma("y", "dwc", T.wq[:].bitcast(dt.uint8), T.wc[:], "Xc0", "wq")
    dma("y", "dws", T.wsp[:], T.ws[:], "Xc0", "wsp")
    dma("y", "dv", T.vt[:], T.v[:], "Xc0", "vt")

    op("g", "iota", (T.cI[:, 0:1], [[0, 1]], 0, 1), "", "cI0", 157)
    iota(T.cI[:, 16:32], [[1, 2], [16, 8]], 0, "cIu", 16, whole=True)
    iota(T.tm[:, 0:16], [[1, 16]], 0, "tm0", 16)
    iota(T.tm[:, 16:32], [[0, 4], [1, 4]], 0, "tm1", 16)
    iota(T.aW[:, 0:24], [[16, NB]], 0, "aW0", 24)
    iota(T.J[:, 0:20], [[16, 20]], 0, "J0", 20)
    iota(T.FT[:], [[1, 16]], 0, "FT", 16)
    iota(T.cc[:], [[-1, 2], [0, NB]], 1, "cc", 48)
    iota(T.base[:, 0:24], [[32, NB]], 32, "base0", 24)
    iota(T.base[:, 24:48], [[-32, NB]], 32 * NB, "base1", 24)
    for i, (a, b, pat, b0) in enumerate(((0, 12, [[25, 12]], 328), (12, 24, [[-24, 12]], 591), (24, 36, [[24, 12]], 23),
                                         (36, 48, [[-25, 12]], 299), (48, 72, [[32, 2], [1, 12]], 0), (72, 80, [[0, 8]], 0))):
        iota(T.ER[:, a:b], pat, b0, "ER%d" % i, b - a)
    iota(T.sm[:, 0:26], [[1, 13], [0, 2]], 0, "sm0 sm1", 26)
    iota(T.sm[:, 48:74], [[0, 13], [511, 2]], 1, "sm2 sm3", 26)
    iota(T.OH[:], [[0, 400]], 0, "OH", 400)
    iota(T.ID[:], [[-1, 768]], 0, "ID", 768)
    iota(T.arow[:], [[1, C]], -192, "arow", C)
    iota(T.GL[:, 0:2], [[448, 2]], -256, "GL0", 2)
    iota(T.GR[:, 0:2], [[448, 2]], -256, "GR0", 2)
    v("set", (T.one[:], 1.0), "", "one", 304)
    act(T.t32[:], T.one[:], "one", "t32", 608, scale=32.0)
    act(T.tW[:], T.one[:, 0:512], "one", "zW", 512, scale=0.0)
    v("set", (T.UV[:, 0:16], BIG), "", "pad0")
    v("set", (T.UV[:, TB:VV + 16], BIG), "", "TBm pad1")
    v("set", (T.ID[:, 0:1], EPS), "", "ID")
    for h in range(2):
        sel(T.DD[:, C * h:C * h + C], T.one[:, 0:C], [[0, C]], OP.is_gt, 0, 0, "one", "DD" + "1" * h, C)
    sel(T.seg[:], T.one[:, 0:C], [[0, NB], [1, 16]], OP.not_equal, 0, 0, "one", "seg", C)
    sel(T.junk[:, 0:128], T.one[:, 0:128], [[-16, 8], [0, 16]], OP.is_ge, 0, 1, "one", "junk0", 128)
    sel(T.BD[:], T.junk[:, 0:128], [[16, 8], [0, 16]], OP.is_ge, 15, -1, "junk0", "BD", 128)
    for col, key, n in ((lane, "lane", 15), (e16, "e16", 16)):
        v("ts", (T.cI[:, n - 14:n - 13], T.cI[:, 0:1], n, None, OP.bitwise_and), "cI0", "i" + key)
        v("copy", (col, T.cI[:, n - 14:n - 13]), "i" + key, key)
    v("ts", (T.cI[:, 3:4], T.cI[:, 1:2], 2, None, OP.arith_shift_right), "ilane", "cI3")
    v("ts", (T.cI[:, 4:5], T.cI[:, 1:2], 3, None, OP.bitwise_and), "ilane", "cI4")
    v("copy", (lq4, T.cI[:, 3:4]), "cI3", "lq4")
    v("ts", (l4c, T.cI[:, 4:5], 4.0 * (512 + 192), None, OP.add), "cI4", "l4c")
    v("copy", (T.upk[:], T.cI[:, 16:32]), "cIu", "upk")
    v("ts", (T.rep[:], T.aW[:, 0:24], 0.0, lane, OP.mult, OP.add), "aW0 lane", "rep")
    v("ts", (T.dm[:, 0:16], T.tm[:, 0:16], lane, None, OP.subtract), "tm0 lane", "dm0")
    v("ts", (T.dm[:, 16:32], T.tm[:, 16:32], lq4, None, OP.subtract), "tm1 lq4", "dm1")
    for i, col in ((0, 15), (1, 0)):
        v("ts", (T.PP[:, 16 * i:16 * i + 16], T.dm[:, 0:16], 0.0, -10 * BIG, OP.is_equal, OP.mult), "dm0", "PP%d" % i)
        one = T.PP[:, 16 * i + col:16 * i + col + 1]
        v("ts", (one, one, BIG, None, OP.add), "PP%d" % i, "PP%d" % i)
    v("ts", (T.PP[:, 32:48], T.dm[:, 0:16], 0.0, 512.0, OP.is_equal, OP.mult), "dm0", "PP2")
    v("ts", (T.PP[:, 32:33], T.PP[:, 32:33], -1024.0, None, OP.add), "PP2", "PP2")
    v("ts", (T.PP[:, 64:96], T.dm[:], 0.0, 512.0, OP.is_equal, OP.mult), "dm0 dm1", "PP4")
    v("ts", (T.tm[:], T.dm[:], -1.0, -1024.0, OP.is_equal, OP.mult), "dm0 dm1", "tm0 tm1")
    v("tt", (T.PP[:, 64:96], T.PP[:, 64:96], T.tm[:], OP.add), "PP4 tm0 tm1", "PP4")
    v("ts", (T.PP[:, 79:96:4], T.PP[:, 79:96:4], -1024.0, None, OP.add), "PP4", "PP4")
    for name, i, key, n, sc in (("c1", 0, "PP0", C, 1.0), ("c2", 1, "PP1", C, 1.0), ("c3", 2, "PP2", C, 1.0), ("c5", 4, "PP4", C, 4.0),
                                ("c6", 5, "PP4", C, 1.0), ("cx", 5, "PP4", 192, -1.0)):
        act(T[name][:], T.PP[:, 16 * i:16 * i + 16].indirect(T.rep[:, 0:n // 16]), key + " rep", name + (" cx1" if name == "cx" else ""), gs(n), scale=sc)
    v("copy", (T.c4[:], T.c3[:]), "c3", "c4", 192)
    v("ts", (T.c4[:, 0::16], T.c3[:, 0::16], -512.0, 512.0, OP.is_equal, OP.mult), "c3", "c4")
    act(kP, T.PP[:, 47:48], "PP2", "kP", f=AF.Identity, scale=-1.0, bias=KX)
    act(kH, T.PP[:, 47:48], "PP2", "kH", f=AF.Identity, scale=-0.5, bias=KX / 2)
    act(kC, T.PP[:, 47:48], "PP2", "kC", f=AF.Identity, scale=2.0, bias=1559.0 - 2 * KX)
    act(k0, T.PP[:, 95:96], "PP4 kP", "k0", f=AF.Identity, scale=-1.0, bias=kP)
    v("ts", (kL, T.dm[:, 15:16], 2.0, k0, OP.mult, OP.add), "dm0 k0", "kL0")
    v("ts", (kR, T.dm[:, 1:2], -2.0, k0, OP.mult, OP.add), "dm0 k0", "kR0")
    v("ts", (T.cF[:, 4:6], T.cF[:, 4:6], -512.0, None, OP.add), "kL0 kR0", "kL kR")
    v("scan", (T.ERd[:], T.ER[:], T.c5[:, 0:80], -5000.0, OP.max, OP.add), keys("ER", 6) + " c5", "ERd", 80)
    v("ts", (T.lE[:, 0:3], T.ERd[:, 15:48:16], 2048.0, None, OP.add), "ERd", "lE")
    v("ts", (T.lE[:, 4:6], T.ERd[:, 63::16], 2048.0, e16, OP.add, OP.add), "ERd e16", "lT")
    v("ts", (T.aW[:, 24:48], T.aW[:, 0:24], lane, 0.5, OP.add, OP.add), "aW0 lane", "aW1")
    v("tt", (T.c5[:, 15::16], T.c5[:, 15::16], T.aW[:, 24:48], OP.add), "c5 aW1", "c5")
    v("ts", (T.sm[:, 0:26], T.sm[:, 0:26], lane, None, OP.is_equal), "sm0 sm1 lane", "sm0 sm1")
    v("tt", (T.OH[:, 15::16], T.sm[:, 24::-1], T.sm[:, 72:47:-1], OP.mult), "sm0 sm1 sm2 sm3 OH", "OH")
    Jc = lambda i: T.J[:, 20 * i:20 * i + 20]
    Ji = T.cI[:, 40:60]
    v("ts", (Jc(1), Jc(0), lane, None, OP.add), "J0 lane", "J1")
    v("ts", (Ji, Jc(1), -12.0, 0.04, OP.add, OP.mult), "J1", "Ji")
    v("ts", (Jc(2), Ji, -25.0, None, OP.mult), "Ji", "J2")
    v("ts", (Jc(3), Ji, -1.0, 24.0, OP.mult, OP.add), "Ji", "J3")
    v("ts", (Jc(4), Ji, 1.0, None, OP.add), "Ji", "J4")
    v("tt", (Jc(5), Jc(1), Jc(2), OP.add), "J1 J2", "J5")
    v("tt", (Jc(6), Jc(5), Jc(3), OP.is_ge), "J5 J3", "J6")
    v("tt", (Jc(7), Jc(6), Jc(3), OP.mult), "J6 J3", "J7")
    v("tt", (Jc(5), Jc(5), Jc(7), OP.subtract), "J5 J7", "J5")
    v("tt", (Jc(4), Jc(4), Jc(7), OP.max), "J4 J7", "J4")
    v("ts", (T.lTH[:], Jc(4), 16.0, 15.0, OP.mult, OP.add), "J4", "lTH")
    v("ts", (T.lBM[:, 0:20], Jc(5), -1.0, 25.0, OP.mult, OP.add), "J5", "lBM0")
    v("copy", (T.lBM[:, 20:40], Jc(5)), "J5", "lBM1")
    for s in range(4):
        act(T.tW[:, 5 * s::16], T.BD[:, s::4], "BD zW", "tW%d" % s, scale=2.0)
        sel(T.tE[:, 512 * s:512 * s + 512], T.one[:, 0:512], [[-1, 512]], OP.is_equal, s, 4, "one", "tE%d" % s, 512)
    v("q", (T.kqW[:], T.ksW[:], T.tW[:]), keys("tW", 4), "kW", qc(128))
    v("q", (T.kqE[:], T.ksE[:], T.tE[:]), keys("tE", 4), "kE", qc(512))

    v("q", (T.qu[:], T.su[:], T.ut[:]), "ut", "qu", qc(128))
    v("q", (T.qv[:], T.sv[:], T.vt[:]), "vt", "qv", qc(128))
    for i in range(2):
        off = T.upk[:, 8 * i:8 * i + 8]
        v("copy", (T.qp[:, 128 * i:128 * i + 128].bitcast(dt.uint32), T.qu[:].bitcast(dt.uint32).indirect(off)), "qu upk", "qp%d" % i, gv(128))
        act(T.sp[:, 128 * i:128 * i + 128], T.su[:].indirect(off), "qu upk", "sp%d" % i, gs(128))
    for (a, b), c in zip(PARTS, "abc"):
        v("q", (T.qx0[:, a:b], T.sx0[:, a:b], T.X[:, 4 * a:4 * b]), "X%s0" % c, "qx0" + c, qc(128))

    first = site[0]
    for t in range(R):
        site[0] = first
        qx, sx, lq, ls = [T[n + str(t)] for n in ("qx", "sx", "lq", "ls")]
        kx = "qx%da qx%db qx%dc" % (t, t, t)
        send(lq[:].bitcast(dt.uint8), qx[:].bitcast(dt.uint8), "aq%d" % t, kx, "sent0")
        send(ls[:], sx[:], "aq%d" % t, kx, "sent1")
        landed("aq%d" % t, 2 * n_in, "sent0 sent1", "qL%d" % t, 4000.0)
        mm(1, C, T.qp[:, 128:], T.sp[:, 128:], qx[:], sx[:], True, True, "qp1 sp1 " + kx)
        act(T.A[:, 2 * C:], bank(1), "#1", "A2", C, f=AF.Sign)
        for (a, b), p, bs in zip(PARTS, "abc", (0, 6, 2)):
            n = b - a
            mm(bs, n, T.qp[:, 0:128], T.sp[:, 0:128], qx[:, a:b], sx[:, a:b], True, True, "qp0 sp0 qx%d%s" % (t, p))
            ks = "#%d" % bs
            va, ua = VV + 16 + C - b, UU + 16 + a
            v("scan", (T.UV[:, va:va + n], rev(T.c1, a, b), rbank(bs, n), 0.0, OP.add, OP.max), "c1 " + ks, "V" + p, n)
            v("scan", (T.UV[:, ua:ua + n], T.c2[:, a:b], bank(bs, n), 0.0, OP.add, OP.max), "c2 " + ks, "U" + p, n)
            v("tt", (T.A[:, C + a:C + b], bank(bs, n), rev(T.UV, va, va + n), OP.is_ge), ks + " V" + p, "A0" + p, n)
            v("tt", (T.A[:, a + 1:b], bank(bs, n, 1), T.UV[:, ua:ua + n - 1], OP.is_gt), ks + " U" + p, "A1" + p, n)
            act(T.S[:, a:b], bank(bs, n), ks, "S" + p, n)
        kU, kV = "Ua Ub Uc pad0", "Va Vb Vc pad1"
        v("tt", (T.UV[:, TB + 1:TB + 25], T.UV[:, VV + 399:VV + 15:-16], T.UV[:, UU + 31:UU + 400:16], OP.max), "Va Vb Vc Ua Ub Uc", "TBm")
        for h in range(2):
            act(T.BMx[:, 304 * h:304 * h + 304], wB.indirect(T.lBM[:, 20 * h:20 * h + 19]), "TBm lBM%d" % h, "BMx%d" % h, gs(304))
        act(T.A[:, 0:C:16], T.one[:, 0:NB], "one", "A1a A1b A1c", scale=0.0)
        v("scan", (T.CNT[:, 0:C], T.seg[:], T.A[:, C:2 * C], 0.0, OP.mult, OP.add), "seg A0a A0b A0c", "CL", 192)
        v("scan", (T.CNT[:, C:], T.seg[:], T.A[:, 0:C], 0.0, OP.mult, OP.add), "seg A1a A1b A1c", "CR", 192)
        v("tt", (T.m[:], T.CNT[:, 15::16], T.cc[:], OP.is_equal), "CL CR cc", "m")
        v("copy", (T.ML[:], T.m[:]), "m", "ML")
        v("tt", (T.mb[:], T.m[:], T.base[:], OP.mult), "m base0 base1", "mb")
        v("tt", (T.corr[:], T.base[:], T.mb[:], OP.subtract), "mb base0 base1", "corr")
        v("tt", (sm(0), T.CNT[:, C + 15::16], T.CNT[:, 15:C:16], OP.subtract), "CL CR", "sm0")
        for h in (1, 0):
            act(T.FR[:, C * h:C * h + C], T.FT[:].indirect(T.ML[:, 24 * h:24 * h + 24]), "FT ML", "FR%d" % h, gs(C))
        v("q", (T.qa[:], T.sa[:], T.A[:]), "A0a A0b A0c A1a A1b A1c A2", "qa", qc(288))
        mm(4, 192, T.kqW[:], T.ksW[:], T.qa[:, 0:192], T.sa[:, 0:192], True, False, "kW qa")
        mm(5, 128, T.kqW[:], T.ksW[:], T.qa[:, 160:288], T.sa[:, 160:288], True, True, "kW qa")
        v("scan", (T.fr[:], bank(5, 128, 32), T.c6[:, 0:96], -5000.0, OP.max, OP.add), "#5 c6", "fr", 96)
        act(sm(1), T.fr[:, 3::4], "fr", "sm1", f=AF.Relu, scale=-100.0, bias=-49000.0)
        v("tt", (T.cov[:, 0:304], wU.indirect(T.lTH[:, 0:19]), T.BMx[:, 0:304], OP.is_ge), kU + " lTH BMx0", "cov0", gv(304))
        v("tt", (T.cov[:, 304:608], wV.indirect(T.lTH[:, 0:19]), T.BMx[:, 304:608], OP.is_gt), kV + " lTH BMx1", "cov1", gv(304))
        v("scan", (T.run[:], T.t32[:], T.cov[:], 0.0, OP.add, OP.mult), "t32 cov0 cov1", "run", 304)
        v("tt", (T.E[:], T.run[:].indirect(T.lE[:, 0:3]), T.mb[:], OP.subtract), "run lE mb", "E", gv(48))
        v("ts", (T.ix[:], T.E[:], -0.5, -1.0, OP.mult, OP.add), "E", "ix")
        v("ts", (T.cx[:, 3:96:4], T.E[:, 0:24], 0.0, kL, OP.min, OP.add), "E kL", "cx")
        v("ts", (T.cx[:, 99::4], T.E[:, 24:48], 0.0, kR, OP.min, OP.add), "E kR", "cx1")
        v("tt", (T.B[:, 0:C], wU.indirect(T.ix[:, 0:24]), T.S[:], OP.is_lt), kU + " ix Sa Sb Sc", "B0", gv(C))
        v("tt", (T.B[:, C:], wV.indirect(T.ix[:, 24:48]), T.S[:], OP.is_le), kV + " ix Sa Sb Sc", "B1", gv(C))
        v("q", (T.qb[:], T.sb[:], T.B[:]), "B0 B1", "qb", qc(192))
        mm(4, 192, T.kqW[:], T.ksW[:], T.qb[:], T.sb[:], False, True, "kW qb")
        v("scan", (T.xx[:], bank(4, 192), T.cx[:], 5000.0, OP.min, OP.add), "#4 cx cx1", "xx", 192)
        v("ts", (T.lp[:], T.xx[:, 3::4], -0.5, kH, OP.mult, OP.add), "xx kH", "lp")
        v("tt", (T.P2[:], T.xx[:, 3::4], T.corr[:], OP.subtract), "xx corr", "P2")
        for i, a in ((0, 24), (1, 0)):
            act(T.junk[:, C * i:C * i + C], T.OH[:].indirect(T.ix[:, a:a + 24]), "OH ix", "junk%d acc%d" % (i, i), gs(C) + 24,
                accum_out=T.acc[:, i:i + 1])
            act(T.rp[:, 32 * i:32 * i + 32], T.one[:, 0:32], "one acc%d" % i, "rp%d" % i, f=AF.Identity, scale=T.acc[:, i:i + 1])
        v("tr", (T.rt[:], T.rp[:]), "rp0 rp1", "rt")
        v("copy", (T.WI[:], T.rt[:].indirect(T.lE[:, 4:6])), "rt lT", "WI", gv(32))
        v("ts", (T.HI[:, 0::2], T.WI[:], 511, None, OP.bitwise_and), "WI", "HI0")
        v("ts", (T.HI[:, 1::2], T.WI[:], 9, None, OP.arith_shift_right), "WI", "HI1")
        v("copy", (T.DD[:, 0::16], T.HI[:, 0:48]), "HI0 HI1 DD1", "DD")
        v("scan", (T.GR[:, 2:C + 2], T.DD[:, C:], rev(T.FR), 192.0, OP.add, OP.subtract), "DD FR0", "GR", 192)
        v("scan", (T.GL[:, 2:C + 2], T.DD[:, 0:C], T.FR[:, C:], 192.0, OP.add, OP.subtract), "DD FR1", "GL", 192)
        act(T.Gg[:, C:], T.GR[:, 0:C + 2].indirect(T.lp[:, 24:48]), "GR GR0 lp", "GgR", gs(C))
        v("copy", (T.Gg[:, 0:C], T.GL[:, 0:C + 2].indirect(T.lp[:, 0:24])), "GL GL0 lp", "GgL", gv(C))
        v("scan", (rev(T.mR), rev(T.Gg, C, 2 * C), rev(T.c3), -2000.0, OP.max, OP.add), "GgR c3", "mR", 192)
        pL, pR = T.P2[:, 0:24], T.P2[:, 24:48]
        v("tt", (T.c4[:, 15::16], sm(0), pL, OP.subtract), "sm0 P2", "c4")
        v("tt", (sm(3), pL, pR, OP.add), "P2", "sm3")
        v("tt", (sm(4), pR, pL, OP.subtract), "P2", "sm4")
        v("tt", (sm(5), sm(4), sm(1), OP.subtract), "sm4 sm1", "sm5")
        v("ts", (T.zi[:], sm(5), 0.5, 384.0, OP.mult, OP.add), "sm5", "zi")
        act(T.z[:], T.ID[:].indirect(T.zi[:]), "ID zi", "z", gs(C))
        v("scan", (T.mL[:], T.Gg[:, 0:C], T.c4[:], -2000.0, OP.max, OP.add), "GgL c4", "mL", 192)
        v("tt", (sm(6), sm(3), T.mR[:, 0::16], OP.subtract), "sm3 mR", "sm6")
        v("tt", (sm(2), T.mL[:, 15::16], T.mR[:, 0::16], OP.subtract), "mL mR", "sm2")
        v("tt", (sm(8), T.mL[:, 15::16], sm(6), OP.add), "mL sm6", "sm8")
        v("ts", (T.oc16[:, 0:24], sm(2), 788.0, None, OP.add), "sm2", "op16")
        v("ts", (T.oc16[:, 24:48], sm(8), kC, None, OP.add), "sm8 kC", "cl16")
        for b, bk in enumerate((0, 1, 6, 7)):
            mm(bk, C, T.kqE[:, 128 * b:128 * b + 128], T.ksE[:, 128 * b:128 * b + 128], lq[:], ls[:], True, True, "kE lp qL%d" % t)
            act(T.Dd[:, b::4], bank(bk), "#%d op16" % bk, "Dd%d" % b, C)
        v("copy", (T.EW[:].indirect(T.oc16[:, 0:24]), T.z[:]), "op16 z", "EW", sv(C))
        v("copy", (T.EW[:].indirect(T.oc16[:, 24:48]), T.z[:]), "cl16 z", "EW", sv(C))
        v("ts", (T.PH[:, 0:C], T.EW[:, 0:C], 1 / EPS, -1.0, OP.mult, OP.max), "EW", "PH0", C)
        act(T.PH[:, C:], T.EW[:, C:], "EW", "PH1", C, f=AF.Sign)
        v("scan", (T.Y[:], T.PH[:], T.EW[:], 0.0, OP.mult, OP.add), "PH0 PH1 EW", "Y", 2 * C)
        act(T.Yg[:, 192:], T.Y[:].indirect(T.oc16[:, 12:24]), "Y op16", "Yg1", gs(192))
        v("copy", (T.Yg[:, 0:192], T.Y[:].indirect(T.oc16[:, 0:12])), "Y op16", "Yg0", gv(192))
        v("scan", (T.dg[:], T.Yg[:], T.c5[:], -5000.0, OP.max, OP.add), "Yg0 Yg1 c5", "dg", C)
        act(sm(7), T.dg[:, 15::16], "dg", "sm7", f=AF.Abs, bias=2048.0)
        v("ts", (T.at[:], sm(7), -0.5, None, OP.add), "sm7", "at")
        v("copy", (T.O[:].indirect(T.at[:, 0:24]), T.arow[:]), "at arow", "O", sv(C))
        ob, ll = T.ob[:, 24 * t:24 * t + 24], T.ll[:, 24 * t:24 * t + 24]
        v("scan", (T.o4[:, H:], T.O[:, H:], T.c6[:, H:], -2000.0, OP.max, OP.add), "O c6", "o4b")
        v("ts", (ob, T.o4[:, H + 3::4], 4.0, l4c, OP.mult, OP.add), "o4b l4c", "ob%d" % t)
        send(ll, ob, "al%d" % t, "ob%d" % t, "sent2")
        landed("al%d" % t, n_in, "sent2", "ll%d" % t, LL)
        v("scan", (T.o4[:, 0:H], T.O[:, 0:H], T.c6[:, 0:H], -2000.0, OP.max, OP.add), "O c6", "o4a", H // 2)
        v("ts", (T.oo[:], T.o4[:, 3:H:4], 4.0, l4c, OP.mult, OP.add), "o4a l4c", "oo")
        if t == R - 1:
            act(T.O32[:], T.O[:], "O", "O32", C, f=AF.Identity, bias=192.0)
            dma("y", "dol", T.ol[:], T.O32[0:128:16, :], "O32", "")
        wv = lambda b: (T.wq[:, 128 * b:128 * b + 128], T.wsp[:, 128 * b:128 * b + 128])
        qn, sn = T["qx%d" % (t + 1)], T["sx%d" % (t + 1)]
        for c, a, e, cut in (("a", K, 256, CUT[0]), ("b", 256, C, CUT[1])):
            m0, m1, m2 = (a - K) // 4, (cut - K) // 4, (e - K) // 4
            v("copy", (T.Z[:, 4 * a:4 * cut], T.X[:].indirect(T.oo[:, m0:m1])), XA + " oo", "Z%s0" % c, gv(4 * (cut - a)))
            act(T.Z[:, 4 * cut:4 * e], T.X[:].indirect(T.oo[:, m1:m2]), XA + " oo", "Z%s1" % c, gs(4 * (e - cut)))
            v("q", (T.qz[:, a:e], T.sz[:, a:e], T.Z[:, 4 * a:4 * e]), "Z%s0 Z%s1" % (c, c), "qz" + c, qc(e - a))
        h = 12 if t == R - 1 else 0
        act(T.Z[:, 16 * h:4 * K], T.Dd[:].indirect(T.ll[:, 24 * t + h:24 * t + 24]), keys("Dd", 4) + " ll%d" % t, "Zc1" if h else "Zc0 Zc1", gs(C - 16 * h))
        if h:
            v("copy", (T.Z[:, 0:16 * h], T.Dd[:].indirect(T.ll[:, 24 * t:24 * t + h])), keys("Dd", 4) + " ll%d" % t, "Zc0", gv(16 * h))
        v("q", (T.qzb[:], T.szb[:], T.Z[:, 0:512]), "Zc0 Zc1 Za0 Za1", "qzc", qc(128))
        for c, a, e, b0 in (("a", K, 256, 0), ("b", 256, C, 4), ("c", 0, K, 2)):
            n, kz = e - a, "Z%s0 Z%s1" % (c, c)
            zq, zs = (T.qzb[:], T.szb[:]) if c == "c" else (T.qz[:, a:e], T.sz[:, a:e])
            if c in Z64S:
                act(T.Z64[:, 4 * a:4 * e], T.Z[:, 4 * a:4 * e], kz, "Z64" + c, 4 * n, scale=64.0)
            else:
                v("ts", (T.Z64[:, 4 * a:4 * e], T.Z[:, 4 * a:4 * e], 64.0, None, OP.mult), kz, "Z64" + c, 2 * n)
            for b in range(4):
                mm(b0 + b, max(n, 128), *wv(b), zq, zs, True, True, "wq wsp qz" + c)
                v("tt", (T.X64[:, 4 * a + b:4 * e:4], bank(b0 + b, n), T.Z64[:, 4 * a + b:4 * e:4], OP.add), "#%d Z64%s" % (b0 + b, c), "X64%s%d" % (c, b), n)
            if c in XV:
                v("ts", (T.X[:, 4 * a:4 * e], T.X64[:, 4 * a:4 * e], 0.015625, None, OP.mult), keys("X64" + c, 4), keys("X" + c, 4), 2 * n)
            else:
                for b in range(4):
                    act(T.X[:, 4 * a + b:4 * e:4], T.X64[:, 4 * a + b:4 * e:4], "X64%s%d" % (c, b), "X%s%d" % (c, b), n, scale=0.015625)
        for (a, b), c in zip(PARTS, "abc"):
            v("q", (qn[:, a:b], sn[:, a:b], T.X[:, 4 * a:4 * b]), keys("X" + c, 4) + (" " + keys("Xa", 4) if c == "c" else ""), "qx%d%s" % (t + 1, c), qc(128))

    site[0] += 8
    for (a, b), p, bk in zip(PARTS, "abc", (0, 6, 2)):
        kx = "qx%d%s" % (R, p)
        mm(bk, b - a, T.qv[:], T.sv[:], T.qx3[:, a:b], T.sx3[:, a:b], True, True, "qv " + kx)
        dma("y", "doc", T.oc[:, 4 * a:4 * b], T.qx3[:, a:b].bitcast(dt.uint8), kx, "")
        if p == "c":
            v("copy", (T.ys[:, a:b], bank(bk, b - a)), "#%d" % bk, "ys" + p, b - a)
        else:
            act(T.ys[:, a:b], bank(bk, b - a), "#%d" % bk, "ys" + p, b - a)
    dma("s", "dy", T.y[:, 128:], T.ys[:, 128:], "ysa ysb", "")
    dma("s", "dy", T.y[:, 0:128], T.ys[:, 0:128], "ysc", "")
    for k in range(4):
        dma("ys"[k // 3], "dos", T.osc[4 * k:4 * k + 4, :], T.sx3[32 * k:32 * k + 4, :], "qx%da qx%db qx%dc" % (R, R, R), "")

    n = len(ops)
    ahead, users = [0.0] * n, [[] for _ in ops]
    for i, o in enumerate(ops):
        for d in o["deps"]:
            users[d].append(i)
    for i in range(n - 1, -1, -1):
        ahead[i] = ops[i]["busy"] + ops[i]["lag"] + max([ahead[j] for j in users[i]] + [0.0])

    def lay_out(bias):
        left = [len(o["deps"]) for o in ops]
        ready, free, order, end = {i: 0.0 for i in range(n) if not left[i]}, {q: 0.0 for q in "vstgyx"}, [], [0.0] * n
        while ready:
            at = {i: max(tm, free[ops[i]["q"]]) for i, tm in ready.items()}
            i0 = min(at, key=lambda i: (at[i], -ahead[i]))
            mine = [i for i in at if ops[i]["q"] == ops[i0]["q"]]
            best = max([i for i in mine if at[i] <= at[i0] + 200.0], key=lambda i: ahead[i] + bias[ops[i]["site"]])
            fill = [i for i in mine if at[i] < at[best] and at[i] + ops[i]["busy"] <= at[best] + 60.0]
            i = max(fill, key=lambda i: ahead[i] + bias[ops[i]["site"]]) if fill else best
            del ready[i]
            order.append(i)
            free[ops[i]["q"]] = end[i] = at[i] + ops[i]["busy"]
            for j in users[i]:
                left[j] -= 1
                if not left[j]:
                    ready[j] = max(end[d] + (ops[d]["lag"] if w else 0.0) for d, w in ops[j]["deps"].items())
        return order

    def span(order):
        total = 0.0
        for a, b in LAGS:
            free, end = {q: 0.0 for q in "vstgyx"}, [0.0] * n
            for i in order:
                o = ops[i]
                at = max([free[o["q"]]] + [end[d] + (lag[d] * (a if lag[d] == LAG else b) if w else 0.0) for d, w in o["deps"].items()])
                free[o["q"]] = end[i] = at + o["busy"]
            total += max(end[i] + lag[i] * b for i in range(n))
        return total

    if n not in ORDER:
        lag = [o["lag"] for o in ops]
        seed, bias = SEED, [0.0] * site[0]
        order = lay_out(bias)
        best = span(order)
        for _ in range(TRIES):
            other = list(bias)
            for _k in range(MUT):
                seed = (seed * 1103515245 + 12345) % 2147483648
                i = (seed >> 8) % len(bias)
                seed = (seed * 1103515245 + 12345) % 2147483648
                other[i] = ((seed >> 8) % 3001) - 1500.0
            b = lay_out(other)
            a = span(b)
            if a <= best:
                best, order, bias = a, b, other
        ORDER[n] = order
    total, known = {}, {q: {} for q in QS}

    def wait(q, sem, val):
        if known[q].get(sem, 0) < val:
            QS[q].wait_ge(T.sem[sem], val)
            known[q][sem] = val

    for i in ORDER[n]:
        o = ops[i]
        if o["emit"]:
            need = {}
            for d, s in o["deps"].items():
                if s and ops[d]["sem"] != "loc":
                    need[ops[d]["sem"]] = max(need.get(ops[d]["sem"], 0), ops[d]["count"])
            for sem, val in need.items():
                wait(o["q"], sem, val)
            o["emit"]()
        total[o["sem"]] = o["count"] = total.get(o["sem"], 0) + o["inc"]
    for sem, val in total.items():
        wait("g", sem, val)
